import numpy as np, ml_dtypes
CORES = [48,51,52,55]
N = 4
BF = ml_dtypes.bfloat16
def gentries(a):
    return np.ascontiguousarray(a.reshape(8, 16, -1).transpose(0, 2, 1)).reshape(8, -1)
def gtable(e):
    e = np.asarray(e); return np.ascontiguousarray(e.reshape(8, -1, 16).transpose(0, 2, 1)).reshape(128, -1).astype(np.int32)
V, XW, L, RO, CAP, TH, EPS, LIM = 1920, 4096, 128, 5, 256, 80, 24, 14
def of(rng, lev, want):
    out = np.zeros(want.shape, np.int64)
    for q in range(N):
        for g in range(8):
            o = np.argsort(lev[q, g], kind="stable"); st = np.searchsorted(lev[q, g][o], np.arange(7))
            a, b = st[want[q, g]], st[want[q, g] + 1]
            out[q, g] = o[a + ((b - a) * rng.random(want[q, g].shape)).astype(np.int64)]
    return out
def parts(rng):
    lev = rng.integers(0, 5, (N, 8, XW)); lev = np.where(rng.random((N, 8, XW)) < rng.choice(np.array([0.1, 0.2, 0.35]), (N, 8, 1)), 5, lev)
    like = np.minimum(3 * lev[:, :, None, :] + rng.integers(0, 3, (N, 8, 16, 1)) + (rng.random((N, 8, 16, XW)) * rng.integers(1, 5, (N, 8, 1, XW))).astype(np.int64), 15)
    x = np.where(lev[:, :, None, :] == 5, rng.integers(0, 16, (N, 8, 16, XW)), like)
    own = lev[:, :, :V]; keep = rng.random((N, 8, V, 8)) < rng.choice(np.array([0.4, 0.75, 0.95]), (N, 8, V, 1))
    s = of(rng, own, np.where(keep, own[..., None], rng.integers(0, 6, (N, 8, V, 8))))
    p = np.where(rng.random((N, 8, V, 1)) < 0.12, of(rng, lev, np.zeros((N, 8, V, 8), np.int64)), rng.integers(0, XW, (N, 8, V, 8)))
    e = np.ascontiguousarray(np.concatenate([p, s], axis=3).transpose(0, 1, 3, 2))
    v = rng.integers(0, V, (N, 8, L)); v = np.where(rng.random((N, 8, L)) < 0.2, np.take_along_axis(v, rng.integers(0, L, (N, 8, L)), 2), v)
    return e, x, v, rng.integers(0, 256, (N, 8, 16))
def pack(e, x, v, w):
    return {"e0": np.ascontiguousarray(e).reshape(N, 128, V).astype(np.int32), "x0": np.ascontiguousarray(x).reshape(N, 128, XW).astype(np.float32).astype(BF),
            "v0": np.stack([gtable(a) for a in v]), "wt": np.ascontiguousarray(w).reshape(N, 128, 1).astype(np.int32)}
def node(e, v, p, s):
    e[:8, v] = p; e[8:, v] = s
def place(w, c):
    u = int(np.add.reduce(w * c)) & (XW - 1)
    return ((u * u >> 5) + u) & (XW - 1)
def total(rng, s):
    o = np.full(16, s >> 4); o[rng.permutation(16)[:s & 15]] += 1; a = rng.permutation(16)
    for i in range(8):
        m = int(rng.integers(0, min(int(o[a[2 * i]]), 15 - int(o[a[2 * i + 1]])) + 1)); o[a[2 * i]] -= m; o[a[2 * i + 1]] += m
    return o
def away(rng, c, d):
    o = c.copy()
    for r in rng.permutation(16):
        k = int(c[r]); s = min(d, max(k, 15 - k)); o[r] = k + s if 15 - k >= k else k - s; d -= s
    return o
def fan(rng, e, nd, n, pr, far, fit):
    for i in range(7):
        s = np.full(8, fit); s[rng.permutation(8)[:n // 7 + int(i < n % 7)]] = far; node(e, nd[i], pr, s)
def setup_inputs(rng):
    return pack(*parts(rng))
def setup_inputs_corners(rng):
    e, x, v, w = parts(rng); w = np.maximum(w, 1); goal = (CAP, CAP + 1, CAP - 1, 0, 8 * L, 1, CAP, 8)
    for q in range(N):
        for g in range(8):
            eg, xg, wg = e[q, g], x[q, g], w[q, g]
            a1, a0 = total(rng, TH), total(rng, TH - 1); ha = place(wg, a1)
            for i in range(64):
                m1 = total(rng, TH + 40); hm = place(wg, m1)
                if hm != ha: break
            c = rng.permutation(V); c = c[(c != ha) & (c != hm)]
            cb, ca, cz, cm, cp, cf, cx = c[:7]
            xg[:, ha] = away(rng, a1, EPS + 1); xg[:, hm] = away(rng, m1, EPS)
            xg[:, cb] = 15; xg[:, ca] = a1; xg[:, cz] = a0; xg[:, cm] = m1
            xg[:, cp] = total(rng, 120); xg[:, cf] = away(rng, xg[:, cp], EPS); xg[:, cx] = away(rng, xg[:, cp], EPS + 1)
            nd = rng.permutation(V)
            for k in range(9):
                node(eg, nd[k], np.where(rng.permutation(8) < k, ca, rng.choice(np.array([cm, cz]), 8)), rng.integers(0, V, 8))
            node(eg, nd[9], cz, rng.integers(0, V, 8)); node(eg, nd[10], cm, cp)
            fan(rng, eg, nd[11:18], LIM, cm, cx, cf); fan(rng, eg, nd[18:25], LIM + 1, cm, cx, cf)
            at = nd[25:25 + L]; n = goal[(q + g) % 8]
            kind = rng.choice(np.array([0, 9, 10, 11]), L); kind[:n // 8] = 8
            if n % 8: kind[n // 8] = n % 8
            kind = rng.permutation(kind)
            for l in range(L):
                k = int(kind[l])
                s = np.full(8, nd[k]) if k < 10 else np.concatenate([nd[10:11], nd[11:18] if k == 10 else nd[18:25]])
                node(eg, at[l], cb, s)
            v[q, g] = at
    return pack(e, x, v, w)
def setup_inputs_crowd(rng):
    e, x, v, w = parts(rng); w = np.maximum(w, 1); w[2, 4] = 0
    for q in range(N):
        for g in range(8):
            eg, xg, wg = e[q, g], x[q, g], w[q, g]
            h = place(wg, np.full(16, 15)); c = XW // 4 + rng.permutation(V - XW // 4); c = c[c != h]
            cb, cp, cq = c[:3]; dd = c[3:11]; na, nb, nc, turn, hold = c[11:16]; lo = rng.integers(0, 4, 16)
            xg[:, h] = 0; xg[:, cb] = 15; xg[:, cp] = lo; xg[:, dd] = lo[:, None]; xg[:, cq] = rng.integers(12, 16, 16)
            node(eg, na, cb, dd); node(eg, nb, cb, cq); node(eg, nc, cb, c[16:24])
            node(eg, turn, cb, np.array([na] + 7 * [nb])); node(eg, hold, cb, nc)
            node(eg, dd[0], cb, cp); fan(rng, eg, dd[1:], LIM + 7, cb, cq, cp)
            o = np.full(L, hold); any2 = rng.integers(0, V, 2); k = (q + g) % 6
            if q < 2:
                o[:] = turn
                if q == 1 and g == 7: o[L - 1] = hold
            elif k == 1: o[L - 1] = turn
            elif k == 2: o[rng.integers(0, L)] = any2[0]
            elif k == 3: o = rng.choice(np.array([turn, hold, any2[0], any2[1]]), L)
            elif k == 4: o[:] = any2[0]
            elif k == 5: o[:] = any2[0]; o[0] = any2[1]
            v[q, g] = o
    return pack(e, x, v, w)
def tips(rng, n, shape, a, b):
    r = rng.random(shape)
    return np.where(r < a, 0, np.where(r < a + b, n - 1, rng.integers(0, n, shape)))
def setup_inputs_ends(rng):
    pops = np.array([0, 4, 7, 10, 13, 16]); lev = rng.integers(0, 6, (N, 8, XW)); row = np.argsort(rng.random((N, 8, 16)), axis=-1)
    lev[..., 0] = np.where(np.arange(8) % 2 == 0, 4, 1); lev[..., V - 1] = 2; lev[..., XW - 1] = 5
    flip = (rng.random((N, 8, 1, XW)) < 0.5) & (np.arange(16)[:, None] == rng.integers(0, 16, (N, 8, 1, XW))); flip[..., [0, V - 1, XW - 1]] = False
    x = 15 * ((row[..., None] < pops[lev][:, :, None, :]) ^ flip).astype(np.int64)
    e = np.concatenate([tips(rng, XW, (N, 8, 8, V), 0.45, 0.45), tips(rng, V, (N, 8, 8, V), 0.45, 0.35)], axis=2)
    v = tips(rng, V, (N, 8, L), 0.35, 0.45); w = 255 * rng.integers(0, 2, (N, 8, 16)); w[:, 7] = 255
    for q in range(N):
        node(e[q, 7], V - 1, XW - 1, 0); node(e[q, 7], 0, XW - 1, np.array([V - 1, 0] * 4)); v[q, 7] = V - 1
        x[q, 7, :, place(w[q, 7], np.full(16, 15))] = 0
        node(e[q, 6], V - 2, XW - 1, np.array([V - 3] + [V - 4] * 7)); node(e[q, 6], V - 3, XW - 1, 0); node(e[q, 6], V - 4, XW - 1, V - 1)
        v[q, 6, 0] = V - 2; v[q, 6, L - 2:] = V - 2
    return pack(e, x, v, w)
def setup_inputs_quiet(rng):
    e, x, v, w = parts(rng); w = np.maximum(w, 1)
    for q in range(N):
        few = rng.permutation(8 * L).reshape(8, L) < 7 + 8 * int(rng.integers(0, L))
        for g in range(8):
            eg, xg = e[q, g], x[q, g]
            for i in range(64):
                h = place(w[q, g], np.full(16, 15))
                if h >= XW // 4: break
                w[q, g] = rng.integers(1, 256, 16)
            c = XW // 4 + rng.permutation(V - XW // 4); c = c[c != h]
            cb, cz = c[:2]; xg[:, h] = 0; xg[:, cb] = 15; xg[:, cz] = 0
            if q % 2 == 0:
                z, asks, mids = c[2:10], c[10:18], c[18:26]; y1, y2, y3, ask0, mid0, ask4 = c[26:32]
                for k in range(8):
                    node(eg, z[k], cz, rng.choice(z, 8)); node(eg, asks[k], cb, mids[k]); node(eg, mids[k], cb, np.roll(z, k))
                node(eg, ask0, cb, mid0); node(eg, mid0, cb, y1); node(eg, y1, cz, y2); node(eg, y2, cz, y3); node(eg, y3, cz, ask4); node(eg, ask4, cb, mids[0])
                v[q, g] = asks[rng.integers(0, 8, L)]; v[q, g, int(rng.integers(1, CAP // 8))] = ask0
            else:
                cp, cq, na, nb, turn, first, idle = c[2:9]; dd = c[9:17]; lo = rng.integers(0, 4, 16)
                xg[:, cp] = lo; xg[:, dd] = lo[:, None]; xg[:, na] = lo; xg[:, nb] = lo; xg[:, cq] = rng.integers(12, 16, 16)
                node(eg, na, cb, dd); node(eg, nb, cb, cq); node(eg, dd[0], cb, cp); fan(rng, eg, dd[1:], LIM + 7, cb, cq, cp)
                node(eg, turn, cb, np.array([nb] + 7 * [na])); node(eg, first, cb, np.array([turn] + 7 * [nb])); node(eg, idle, cz, turn)
                v[q, g] = np.where(few[g], first, idle)
    return pack(e, x, v, w)
def setup_inputs_spread(rng):
    full = rng.random((N, 8, 1, XW)) < rng.choice(np.array([0.3, 0.6, 1.0]), (N, 8, 1, 1))
    x = np.minimum((rng.random((N, 8, 16, XW)) * np.where(full, 16, rng.integers(1, 17, (N, 8, 1, XW)))).astype(np.int64), 15)
    s = np.minimum((V * rng.random((N, 8, 8, V)) ** rng.choice(np.array([1.0, 2.0]), (N, 8, 1, 1))).astype(np.int64), V - 1)
    e = np.concatenate([rng.integers(0, XW, (N, 8, 8, V)), s], axis=2)
    v = np.minimum((V * rng.random((N, 8, L)) ** rng.choice(np.array([1.0, 3.0]), (N, 8, 1))).astype(np.int64), V - 1)
    w = np.minimum(np.exp2(8 * rng.random((N, 8, 16))).astype(np.int64) - 1, 255)
    return pack(e, x, v, w)
def check_inputs(d):
    bad = []
    for k, lo, hi in (("e0", 0, XW - 1), ("x0", 0, 15), ("v0", 0, V - 1), ("wt", 0, 255)):
        a = np.asarray(d[k]).astype(np.float64)
        if not np.all((a >= lo) & (a <= hi)): bad.append("range of " + k)
    if np.max(np.asarray(d["e0"]).reshape(-1, 16, V)[:, 8:]) >= V: bad.append("range of the subs in e0")
    a = np.asarray(d["x0"]).astype(np.float32)
    if np.any(a != np.floor(a)): bad.append("whole numbers in x0")
    return bad
def reference(e0, x0, v0, wt):
    M = 8 * N
    E = np.ascontiguousarray(e0.reshape(M, 16, V).transpose(0, 2, 1)).astype(np.int64)
    X = np.ascontiguousarray(x0.astype(np.float32).reshape(M, 16, XW).transpose(0, 2, 1)).astype(np.int32)
    v = np.stack([gentries(a) for a in v0]).reshape(M, L).astype(np.int64); w = wt.reshape(M, 1, 1, 16).astype(np.int32)
    k = np.arange(M); k1, k2, k3 = k[:, None], k[:, None, None], k[:, None, None, None]
    A = np.zeros((M, 1), np.int64); lower = np.arange(L)[None, :] < np.arange(L)[:, None]
    for t in range(RO):
        c = E[k1, v]; p, s = c[..., :8], c[..., 8:]
        c = E[k2, s]; pp, ss = c[..., :8], c[..., 8:]
        m = np.minimum(X[k2, p][:, :, :, None, :], X[k3, pp])
        alive = np.add.reduce(m, axis=4) >= TH
        full = np.any(alive, axis=2); first = np.argmax(alive, axis=2)
        sub = np.take_along_axis(ss, first[:, :, None, :], 2)[:, :, 0]
        far = np.add.reduce(np.abs(X[k3, ss] - X[k2, sub][:, :, None]), axis=4) > EPS
        pi = np.max(np.where((alive & ~far)[..., None], m, 0), axis=2)
        stand = np.add.reduce((alive & far).astype(np.int64), axis=(2, 3)) <= LIM + (A & 7)
        u = np.add.reduce(w * pi, axis=3).astype(np.int64) & (XW - 1); h = ((u * u >> 5) + u) & (XW - 1)
        known = np.add.reduce(np.abs(X[k2, h] - pi), axis=3) <= EPS
        new = XW // 4 * (t & 3) + np.arange(8 * L).reshape(L, 8); name = np.where(known, h, new)
        ask = stand[:, :, None] & full & ~known
        one = ask.reshape(M, 8 * L).astype(np.int64); before = (np.add.accumulate(one, axis=1) - one).reshape(M, L, 8)
        k4 = (k // 8 + 1 + t % (N - 1)) % N * 8 + k % 8
        got = X[k4[:, None, None], h]
        val = np.where((ask & (before < CAP))[..., None], (pi + got) >> 1, pi)
        best = np.argmax(np.where(full, np.add.reduce(pi, axis=3), -1), axis=2)
        go = np.where(stand & np.any(full, axis=2), np.take_along_axis(sub, best[..., None], 2)[..., 0], s[:, :, t])
        lead = stand & ~np.any((v[:, :, None] == v[:, None, :]) & stand[:, None, :] & lower, axis=2)
        pair = np.concatenate([np.where(full, name, p), np.where(full, sub, s)], axis=2)
        a, l = np.nonzero(lead); E[a, v[a, l]] = pair[a, l]
        a, l, j = np.nonzero(ask); X[a, new[l, j]] = val[a, l, j]
        A = np.repeat(np.add.reduce((~stand).reshape(N, 8 * L).astype(np.int64), axis=1), 8)[:, None]; v = go
    return {"ye": np.ascontiguousarray(E.transpose(0, 2, 1)).reshape(N, 128, V).astype(np.float32),
            "yx": np.ascontiguousarray(X.transpose(0, 2, 1)).reshape(N, 128, XW).astype(np.float32).astype(BF),
            "yv": np.stack([gtable(a) for a in v.reshape(N, 8, L)]).astype(np.float32)}

@@ -1,0 +1,923 @@
+import numpy as np
+from concourse.mybir import AluOpType, AxisListType, ActivationFunctionType
+
+H = "float16"
+V, XW, RO = 1920, 4096, 5
+XA = 1024
+HALVES = [0, 4, 5]
+OWN_ACT = [0]
+EQ_ACT, EQ_LATE = [1], False
+BY_MIN = [(1, 1), (1, 2), (1, 3), (1, 4)]
+VIA_ACT = (9, 11, 13, 15)
+
+SCRATCH = {}
+SPEC = {}
+
+
+def _decl(where, dtype, spec):
+    pool, at = "pool_" + dtype, 0
+    for name, cols in spec.items():
+        if where == "sbuf" and cols <= 64:
+            SPEC[name] = (where, [128, cols], dtype, pool, at)
+            at += (cols + 15) // 16 * 16
+        else:
+            SPEC[name] = (where, [128, cols], dtype, name, 0)
+            SCRATCH[name] = (where, [128, cols], dtype)
+    if at:
+        SCRATCH[pool] = (where, [128, at], dtype)
+
+
+_decl("psum", "float32", {"ps%d" % k: 512 for k in range(8)})
+_decl("sbuf", "bfloat16", {
+    "X": XW, "XR0": XW, "XR1": XW, "XR2": XW, "XR3": XW, "XR4": XW, "m": 8192, "s": 8192, "a": 7168, "ad": 7168,
+    "W": 3072, "XP": 1024, "b": 1024, "d2": 1024, "ad2": 1024, "rec": 1024, "F1": 1024, "al": 512, "P": 512,
+    "penT": 512, "EQ": 1024, "EQm": 1024, "z0": 512, "z1": 512, "IDb": 128, "NIDb": 128, "BLK": 128, "BD": 18 * 128,
+    "WB": 16, "OBb": 16, "OB256": 16, "OBk": 16, "OBm": 16, "ONES": 128, "BIAS": 256, "BIAS2": 256, "TRI": 128, "st": 16,
+    "ask": 64, "sf": 64, "WS": 32, "wb": 16, "SelS": 64, "WIDE": 1024, "OBh": 16, "Bm4": 32, "RB": 256, "t0": 128, "t1": 128, "I2K": 128, "N2K": 128, "EQa": 1024, "xh": 512, "incl": 64, "IDa": 128, "IDc": 128, "JK": 64})
+_decl("sbuf", H, {"N1h": 128, "N2h": 1024, "Th": 1024, "IWh": 192, "PM": 16 * 128,
+                  "vr": 128, "nvr": 128, "Rb": 256})
+_decl("sbuf", "float32", {
+    "E": 2048, "IOT": V, "N1f": 128, "N1T": 128, "sc": 512, "NS": 128, "nT": 64, "nmh": 72, "fr": 128, "cn": 128, "lc": 8,
+    "full": 64, "lv": 8, "wsf": 8, "OBs": 8, "dl": 128, "df": 128, "En": 128, "tq": 64, "aM": 128,
+    "Rc": 128, "Rh": 256, "Rv": 128, "Rs": 128, "aD": 128, "k3": 64, "k4": 64, "ld": 8, "vmd": 8, "VM": 128,
+    "thr": 8, "yvf": 8, "wf": 8, "ONE": 192, "IW": 192, "FC": 32, "MC": 24, "E16": 24, "CF": 24,
+    "r128": 128, "rc": 128, "rh": 128, "r4": 128, "rg": 128, "rn": 128, "rd": 128, "MH": 128, "MK": 128, "MD": 128,
+    "M4": 128, "CM": 128, "Bm2": 64, "Bm4f": 32, "OBf": 8, "NM": 128, "DM": 128, "RS": 64, "Sel32": 64})
+_decl("sbuf", "int32", {"E0": V, "vi": 8, "wi": 8, "IC": 24, "ui": 64, "u": 64, "u32": 64, "uw": 64, "h": 64,
+                        "gi": 8, "go": 8, "si": 8, "nm": 8, "Ai": 8, "A7": 8, "wsi": 8})
+_decl("sbuf", "uint16", {"VL": 8, "SL": 8, "LP": 128, "OP": 512, "AL": 448, "BL": 64, "HL": 64, "CL": 64, "LS": 80,
+                         "LI": 120})
+
+ENG = ("pe", "dve", "act", "pool", "sp")
+SEMAPHORES = (["c_" + e for e in ENG[:4]] + ["dma%d" % k for k in range(24)] + ["arr%d" % t for t in range(RO)]
+              + ["snt%d" % t for t in range(RO)])
+OP_ = AluOpType
+AF = ActivationFunctionType
+
+
+def A(name, c0=0, c1=None, step=1):
+    return ("ap", name, c0, SPEC[name][1][1] if c1 is None else c1, step)
+
+
+def IND(win, off):
+    return ("ind", win, off)
+
+
+def HB(name, c0=None, c1=None):
+    return ("hbm", name, c0, c1)
+
+
+def _n(x):
+    if x[0] == "ind":
+        return 16 * _n(x[2])
+    return len(range(x[2], x[3], x[4]))
+
+
+def _two(x):
+    return SPEC[x[1]][0] == "sbuf" and SPEC[x[1]][2] in ("bfloat16", "float16", "uint16")
+
+
+def _spans(x):
+    if not isinstance(x, tuple):
+        return []
+    if x[0] == "ind":
+        return _spans(x[1]) + _spans(x[2])
+    if x[0] == "hbm":
+        return []
+    return [(x[1], x[2], x[2] + (_n(x) - 1) * x[4] + 1)]
+
+
+def program(CY=1.04, G=1.5, PE=0.52, BW=330.0):
+    ops = []
+
+    def add(eng, kind, out, ins, par, ns, hold=None):
+        ops.append({"eng": eng, "kind": kind, "out": out, "ins": ins, "par": par, "ns": ns,
+                    "hold": ns if hold is None else hold})
+
+    def vcost(out, ins, rate=None):
+        full = [x for x in ins if isinstance(x, tuple)]
+        if out[0] == "ind":
+            return 60 + 3.5 * CY * _n(out)
+        if full and full[0][0] == "ind":
+            return 60 + G * CY * _n(out)
+        if rate is None:
+            rate = 0.5 if all(_two(x) for x in [out] + [y for y in full if _n(y) > 1]) else 1.0
+        return 40 + CY * max(64, rate * _n(out))
+
+    def cp(out, in_):
+        add("dve", "copy", out, [in_], None, vcost(out, [in_]))
+
+    def ts(out, in0, s1, op0, s2=None, op1=None):
+        add("dve", "ts", out, [in0, s1, s2], (op0, op1), vcost(out, [in0]))
+
+    def tt(out, in0, in1, op):
+        sb = all(x[0] == "ind" or SPEC[x[1]][0] == "sbuf" for x in (in0, in1))
+        add("dve", "tt", out, [in0, in1], op, vcost(out, [in0, in1], 2.0 if sb else 1.0))
+
+    def scan(out, d0, d1, op0, op1):
+        add("dve", "scan", out, [d0, d1], (op0, op1), vcost(out, [d0, d1]))
+
+    def mset(out, c):
+        add("dve", "memset", out, [], c, vcost(out, []))
+
+    def act(out, in_, func, bias=0.0, scale=1.0):
+        ns = (80 + G * CY * _n(out)) if in_[0] == "ind" else 60 + CY * max(64, _n(out))
+        add("act", "act", out, [in_, bias, scale], func, ns)
+
+    def mm(out, lhsT, rhs, start=True, stop=True):
+        f = 4 if SPEC[rhs[1]][2] == "float32" else 1
+        add("pe", "mm", out, [lhsT, rhs], (start, stop), PE * f * max(64, _n(rhs)))
+
+    def iota(out, pattern, base, cm):
+        add("pool", "iota", out, [], (pattern, base, cm), 160 + 2 * CY * _n(out))
+
+    def sel(out, in_, pattern, op, base, cm):
+        add("pool", "sel", out, [in_], (pattern, op, base, cm), 200 + 2 * CY * _n(out))
+
+    ndma = [0]
+
+    def dma(q, out, in_, nbytes):
+        add(q, "dma", out, [in_], "dma%d" % ndma[0], 2000 + nbytes / BW, 60)
+        ndma[0] += 1
+
+    add_, sub_, mul, mx, mn = OP_.add, OP_.subtract, OP_.mult, OP_.max, OP_.min
+    eq, shr, band = OP_.is_equal, OP_.arith_shift_right, OP_.bitwise_and
+    ps = ["ps%d" % k for k in range(8)]
+
+    dma("sp", A("vi"), HB("v0"), 4096)
+    dma("sp", A("E0", 0, 960), HB("e0", 0, 960), 500000)
+    dma("act", A("E0", 960, V), HB("e0", 960, V), 1000000)
+    dma("sp", A("X", 0, 2048), HB("x0", 0, 2048), 2000000)
+    dma("act", A("X", 2048, XW), HB("x0", 2048, XW), 2000000)
+    dma("sp", A("wi", 0, 1), HB("wt"), 512)
+
+    def lin(out, in_, scale, bias=0.0):
+        act(out, in_, AF.Identity, bias, scale)
+    cp(A("VL"), A("vi"))
+
+    iota(A("IC", 0, 1), [[0, 1]], 0, 1)
+    cols = {"p": 0}
+    for name, sh, msk in (("k8", 3, 1), ("q4", 2, 3), ("e16", 4, 1), ("c16", 0, 15), ("b1", 0, 1), ("b2", 0, 3),
+                          ("g", 4, 7), ("h1", 1, 63), ("h2", 2, 31), ("j", 0, 7), ("y1", 1, 1), ("y2", 1, 3),
+                          ("c4", 2, 1)):
+        cols[name] = len(cols)
+        ts(A("IC", cols[name], cols[name] + 1), A("IC", 0, 1), sh, shr, msk, band)
+    cp(A("FC", 0, len(cols)), A("IC", 0, len(cols)))
+
+    def col(name):
+        return A("FC", cols[name], cols[name] + 1)
+
+    def newcol(name):
+        cols[name] = len(cols)
+        return col(name)
+
+    mset(A("ONE"), 1.0)
+    sel(A("IW"), A("ONE"), [[-1, 192]], eq, 32, 1)
+    cp(A("IWh"), A("IW"))
+    iota(A("r128"), [[1, 128]], 0, 0)
+    ts(newcol("shift"), col("k8"), 2048.0, mul, -2048.0, add_)
+    ts(A("MC", 0, 2), A("r128", 0, 2), col("k8"), eq)
+    ts(A("MC", 4, 8), A("r128", 0, 4), col("q4"), eq)
+    ts(A("MC", 8, 10), A("r128", 0, 2), col("e16"), eq)
+    npm = [0]
+
+    def perm(shift, mcol):
+        o = A("PM", 128 * npm[0], 128 * npm[0] + 128)
+        npm[0] += 1
+        ts(o, A("IWh", 32 - shift, 160 - shift), A("MC", mcol, mcol + 1), mul)
+        return o
+    PK = [[perm(8 * (h - kind), kind) for h in range(2)] for kind in range(2)]
+    Q = [[perm(4 * l2 - 8 - 4 * c, 6 + c) for l2 in range(4)] for c in range(2)]
+    R = [[perm(16 * (e - yy), 8 + yy) for yy in range(2)] for e in range(2)]
+    ID32 = A("IW", 32, 160)
+    lin(A("IDb"), ID32, 1.0)
+    lin(A("NIDb"), ID32, -1.0)
+    lin(A("IDa"), ID32, -32.5)
+    lin(A("IDc"), ID32, 1.0 / 8192)
+    sel(A("Sel32"), A("ONE", 0, 64), [[2, 4], [16, 8], [1, 2]], eq, 8, -1)
+    lin(A("SelS"), A("Sel32"), 1.0)
+    iota(A("rg"), [[1, 8], [0, 16]], 0, 0)
+    ts(A("BLK"), A("rg"), col("g"), eq)
+    ts(A("OBf"), A("r128", 0, 8), col("g"), eq)
+    OBb = A("OBb", 0, 8)
+    lin(OBb, A("OBf"), 1.0)
+    lin(A("OB256", 0, 8), A("OBf"), 256.0)
+    lin(A("OBh", 0, 8), A("OBf"), 1.0 / 16)
+    cp(A("wf", 0, 1), A("wi", 0, 1))
+    lin(A("WB", 0, 8), A("OBf"), A("wf", 0, 1))
+    lin(A("OBk", 0, 8), A("OBf"), 16384.0)
+    lin(A("ONES"), A("ONE", 0, 128), 1.0)
+    for hf in range(2):
+        lin(A("BIAS", 128 * hf, 128 * hf + 128), A("ONE", 0, 128), 15.0)
+        lin(A("BIAS2", 128 * hf, 128 * hf + 128), A("ONE", 0, 128), -64.0)
+    sel(A("TRI"), A("ONES"), [[1, 128]], OP_.is_gt, 0, -1)
+    ts(A("E16", 0, 17), A("r128", 0, 17), col("c16"), eq)
+    tt(A("CF", 0, 16), A("E16", 1, 17), A("E16", 0, 16), sub_)
+    ts(A("CF", 7, 16, 8), A("E16", 7, 16, 8), -2.0, mul)
+    cp(A("CF", 16, 18), A("E16", 0, 9, 8))
+    for x in range(18):
+        act(A("BD", 128 * x, 128 * x + 128), A("BLK"), AF.Copy, 0.0, A("CF", x, x + 1))
+    lin(A("OBs"), A("OBf"), 1.0 / 16)
+    for g_ in range(8):
+        lin(A("WIDE", 128 * g_, 128 * g_ + 128), A("ONE", 0, 128), A("OBs", g_, g_ + 1))
+    iota(A("r4"), [[0, 8], [1, 4], [0, 4]], 0, 0)
+    iota(A("rh"), [[0, 8], [1, 2], [0, 8]], 0, 0)
+    iota(A("rc"), [[0, 8], [1, 16]], 0, 0)
+    iota(A("rn"), [[0, 16], [1, 8]], 0, 8)
+    iota(A("rd"), [[0, 16], [508, 2], [0, 4]], 1024, -4)
+    lin(A("N2K"), ID32, -2048.0)
+    lin(A("I2K"), ID32, 2048.0)
+    lin(A("WB", 8, 16), A("WB", 0, 8), -128.0)
+    lin(A("wb", 0, 1), A("wf", 0, 1), 1.0)
+    mm(A(ps[6], 0, 1), A("BLK"), A("wb", 0, 1))
+    cp(A("wsi", 0, 1), A(ps[6], 0, 1))
+    ts(A("wsi", 1, 2), A("wsi", 0, 1), 4032, band)
+    ts(A("wsi", 2, 3), A("wsi", 0, 1), 63, band)
+    cp(A("wsf", 0, 2), A("wsi", 1, 3))
+    for j0 in range(2):
+        for part in range(2):
+            ts(A("WS", 16 * j0 + 8 * part, 16 * j0 + 8 * part + 8), A("OBf"), A("E16", 8 * j0, 8 * j0 + 1), mul,
+               A("wsf", part, part + 1), mul)
+    lin(newcol("ndump"), col("p"), -1.0, -float(V))
+    iota(A("IOT"), [[1, V]], 0, 0)
+    lin(A("t0"), A("BLK"), 256.0)
+    ilo, ihi = min(i for _, i in BY_MIN), max(i for _, i in BY_MIN)
+    for j0 in range(2):
+        sel(A("t1"), A("t0"), [[0, 8], [1, 16]], OP_.is_ge, -(8 * j0 + 7 - ihi), 0)
+        sel(A("RB", 128 * j0, 128 * j0 + 128), A("t1"), [[0, 8], [-1, 16]], OP_.is_ge, 8 * j0 + 7 - ilo, 0)
+    ts(A("M4"), A("r4"), col("b2"), eq)
+    ts(A("Bm4f"), A("r128", 0, 32), col("h2"), eq)
+    lin(A("Bm4"), A("Bm4f"), 1.0)
+    ts(A("MH"), A("rh"), col("b1"), eq)
+    lin(A("MK"), A("MH"), 1024.0)
+    lin(A("nmh", 64, 72), A("ONE", 0, 8), 0.0)
+    LCN = A("LS", 60, 68)
+    lin(newcol("nk8"), col("k8"), -8.0, 8.0)
+    lin(newcol("lcn"), col("k8"), 64.0, col("j"))
+    ts(A("lc"), A("r128", 0, 8), col("nk8"), mul, col("lcn"), add_)
+    ts(LCN, A("lc"), 64.0, mn)
+    lin(A("OBm", 0, 8), A("OBf"), -512.0)
+    ts(A("CM"), A("rc"), col("c16"), eq)
+    ts(A("Bm2"), A("r128", 0, 64), col("h1"), eq)
+    tt(A("NM"), A("MH"), A("rn"), mul)
+    tt(A("MD"), A("MH"), A("rd"), mul)
+    lin(newcol("dump"), col("p"), 1.0, float(V))
+    lin(A("DM"), A("CM"), col("dump"))
+    lin(newcol("p8"), col("p"), 16384.0)
+    lin(A("JK"), A("rn", 0, 64), -2048.0, col("p8"))
+    act(A("RS"), A("rn", 0, 64), AF.Identity, col("p8"), -2048.0)
+    act(A("RS"), A("RS"), AF.Sign, 0.0, -1.0)
+    lin(newcol("t1"), col("b1"), 8.0, 7.0)
+    lin(newcol("lb"), col("y1"), 128.0, col("t1"))
+    lin(newcol("t2"), col("y2"), 128.0, col("t1"))
+    lin(newcol("lsub"), col("k8"), 16.0, col("t2"))
+    lin(newcol("lns"), col("k8"), 64.0, col("j"))
+    lin(newcol("t3"), col("k8"), 4.0, col("b2"))
+    lin(newcol("lhg"), col("c4"), 32.0, col("t3"))
+    LB, LSUB, LDUP, LREP, LR8, LNS, LH4, LHG = (
+        A("LS", 0, 8), A("LS", 8, 12), A("LS", 16, 24), A("LS", 24, 32), A("LS", 32, 36), A("LS", 40, 48),
+        A("LS", 48, 56), A("LS", 56, 60))
+    ts(LH4, A("r128", 0, 8), 4.0, mul, col("b2"), add_)
+    ts(LHG, A("r128", 0, 4), 8.0, mul, col("lhg"), add_)
+    ts(LB, A("r128", 0, 8), 16.0, mul, col("lb"), add_)
+    ts(LSUB, A("r128", 0, 4), 32.0, mul, col("lsub"), add_)
+    ts(LDUP, A("r128", 0, 8), 8.0, mul, col("j"), add_)
+    cp(LREP, A("r128", 0, 8))
+    ts(LR8, A("r128", 0, 4), 2.0, mul, col("k8"), add_)
+    ts(LNS, A("r128", 0, 8), 8.0, mul, col("lns"), add_)
+    mset(A("thr", 0, 1), 14.0)
+    ts(A("LI"), A("r128", 0, V // 16), 16.0, mul, col("c16"), add_)
+    for k in range(3):
+        act(A("E", 640 * k, 640 * k + 640), IND(A("E0"), A("LI", 40 * k, 40 * k + 40)), AF.Copy)
+
+    EW, XWIN = A("E", 0, V), A("X")
+    nscan = [0, 0]
+    for t in range(RO):
+        blk = 1024 * (t % 4)
+        XR = "XR%d" % t
+        EW = A("E", 0, V) if t else A("E0")
+        add("pool", "send", None, [XWIN], t, 9000, 1500)
+        add(None, "arrive", A(XR), [], t, 0)
+        dma("sp", A("W", 0, 1024), A("X", blk, blk + 1024), 262144)
+        if t == RO - 1:
+            dma("sp", HB("yx", 1024, XW), A("X", 1024, XW), 786432)
+        ts(A("N1h"), IND(EW, A("VL")), col("shift"), add_)
+        for kind in range(2):
+            for h in range(2):
+                mm(A(ps[7], 64 * kind, 64 * kind + 64), PK[kind][h], A("N1h", h, 128, 2), h == 0, h == 1)
+        cp(A("LP", 64, 128), A(ps[7], 64, 128))
+        ts(A("LP", 0, 64), A(ps[7], 0, 64), 2048.0, add_)
+        ts(A("N2h"), IND(EW, A("LP", 64, 128)), col("shift"), add_)
+        for hf in range(2):
+            act(A("XP", 512 * hf, 512 * hf + 512), IND(XWIN, A("LP", 32 * hf, 32 * hf + 32)), AF.Copy)
+        add("dve", "tr", A("Th"), [A("N2h")], None, vcost(A("Th"), [A("N2h")]))
+        for c in range(2):
+            for i in range(1, 8):
+                for l2 in range(4):
+                    mm(A(ps[c], 32 * (i - 1), 32 * i), Q[c][l2], A("N2h", 8 * l2 + i, 1024, 32), l2 == 0, l2 == 3)
+            cp(A("AL", 224 * c, 224 * c + 224), A(ps[c], 0, 224))
+            for jj in range(4):
+                for yy in range(2):
+                    for e in range(2):
+                        mm(A(ps[2 + c], 64 * jj + yy, 64 * jj + 64, 2), R[e][yy],
+                           A("Th", 16 * e + 4 * c + jj, 1024, 32), e == 0, e == 1)
+                if c == 0 and jj == 0:
+                    ts(A("OP", 0, 64), A(ps[2], 0, 64), 2048.0, add_)
+            ts(A("OP", 256 * c + (0 if c else 64), 256 * c + 256), A(ps[2 + c], 0 if c else 64, 256), 2048.0, add_)
+        act(A("N1f"), IND(EW, A("VL")), AF.Copy)
+        mm(A(ps[7], 128, 256), A("N1f"), ID32)
+        act(A("N1T"), A(ps[7], 128, 256), AF.Copy)
+        cp(A("vr"), IND(A("IOT"), A("VL")))
+        ts(A("nvr"), A("vr"), -1.0, mul)
+        mm(A(ps[7], 256, 264), A("vr"), A("OBh", 0, 8))
+        lin(A("vmd"), A(ps[7], 256, 264), 1.0, col("ndump"))
+
+        def same_node(bank):
+            for hf in range(2):
+                mm(A(ps[bank + hf]), A("nvr"), A("WIDE", 512 * hf, 512 * hf + 512), True, False)
+                for g4 in range(4):
+                    g_ = 4 * hf + g4
+                    mm(A(ps[bank + hf], 128 * g4, 128 * g4 + 128), A("WIDE", 128 * g_, 128 * g_ + 128), A("vr"),
+                       False, g4 == 3)
+                o0, o1 = 512 * hf, 512 * hf + 512
+                if hf in EQ_ACT:
+                    act(A("EQa", o0, o1), A(ps[bank + hf]), AF.Abs)
+                    ts(A("EQ", o0, o1), A("EQa", o0, o1), 0.0, eq)
+                else:
+                    ts(A("EQ", o0, o1), A(ps[bank + hf]), 0.0, eq)
+                sel(A("EQm", o0, o1), A("EQ", o0, o1), [[0, 4], [1, 128]], OP_.is_gt, 0, -1)
+        if not EQ_LATE:
+            same_node(2)
+        lin(A("nT"), A("rn", 0, 64), 1.0, float(blk))
+        for c in range(2):
+            for k in range(4):
+                act(A("a", 3584 * c + 896 * k, 3584 * c + 896 * k + 896),
+                    IND(XWIN, A("AL", 224 * c + 56 * k, 224 * c + 56 * k + 56)), AF.Copy)
+            for jj in range(4):
+                j = 4 * c + jj
+                for l0, l1 in ([(0, 32), (32, 64)] if j in HALVES else [(0, 64)]):
+                    tt(A("m", 1024 * j + 16 * l0, 1024 * j + 16 * l1), IND(XWIN, A("OP", 64 * j + l0, 64 * j + l1)),
+                       A("XP", 16 * l0, 16 * l1), mn)
+                o = 128 * (jj >> 1) + 8 * (jj & 1)
+                for i in range(8):
+                    mm(A(ps[5 + c], o + 7 - i, 128 * (jj >> 1) + 128, 16), A("m", 1024 * j + i, 1024 * j + 1024, 8), OBb)
+            w0, w1 = 256 * c, 256 * c + 256
+            mm(A(ps[4], w0, w1), A("ONES"), A("BIAS2"), True, False)
+            for i in range(8):
+                mm(A(ps[4], w0 + 7 - i, w1, 8), A("N2h", i, 1024, 8), A("SelS", 32 * c, 32 * c + 32), False, False)
+            ts(A("al", w0, w1), A(ps[5 + c], 0, 256), 80.0, OP_.is_ge, -8192.0, mul)
+            mm(A(ps[4], w0, w1), A("NIDb"), A("al", w0, w1), False, True)
+            scan(A("sc", w0, w1), A("al", w0, w1), A(ps[4], w0, w1), add_, mx)
+            tt(A("Rb", 128 * c, 128 * c + 128), IND(A("sc", w0, w1), LB), A("M4"), mul)
+            mm(A(ps[7], 320 + 32 * c, 352 + 32 * c), A("Rb", 128 * c, 128 * c + 128), A("Bm4"))
+            cp(A("BL", 32 * c, 32 * c + 32), A(ps[7], 320 + 32 * c, 352 + 32 * c))
+            act(A("b", 512 * c, 512 * c + 512), IND(XWIN, A("BL", 32 * c, 32 * c + 32)), AF.Copy)
+        act(A("NS", 64, 128), IND(A("sc"), LSUB), AF.Copy)
+
+        def names(c):
+            sb = ps[4]
+            PI = A("W", 1024 + 512 * c, 1536 + 512 * c)
+            q0, q1, o0, o1 = 32 * c, 32 * c + 32, 512 * c, 512 * c + 512
+            for pb, l0, l1 in [(ps[4] if c == 0 else ps[0], 0, 128)]:
+                for jj in range(4):
+                    j = 4 * c + jj
+                    o = A(pb, jj, 4 * (l1 - l0), 4)
+                    mm(o, A("IDb"), A("s", 1024 * j + 8 * l0 + 7, 1024 * j + 8 * l1, 8), True, False)
+                    x = 16 + (j & 1)
+                    mm(o, A("BD", 128 * x, 128 * x + 128), A("penT", 128 * (j >> 1) + l0, 128 * (j >> 1) + l1), False, True)
+                o = A("W", 1024 + o0 + 4 * l0, 1024 + o0 + 4 * l1)
+                act(o, A(pb, 0, 4 * (l1 - l0)), AF.Relu, -128.0)
+            for jj in range(4):
+                j, o = 4 * c + jj, A(ps[5], jj, 32, 4)
+                if c == 0:
+                    mm(o, A("W", 1024 + o0 + jj, 1024 + o1, 4), A("WB", 0, 8))
+                else:
+                    pT = A("penT", 128 * (j >> 1), 128 * (j >> 1) + 128)
+                    mm(o, A("ONES"), A("WB", 8, 16), True, False)
+                    mm(o, pT, A("WS", 16 * (j & 1), 16 * (j & 1) + 8), False, False)
+                    mm(o, pT, A("WS", 16 * (j & 1) + 8, 16 * (j & 1) + 16), False, False)
+                    mm(o, A("s", 1024 * j + 7, 1024 * j + 1024, 8), A("WB", 0, 8), False, True)
+            cp(A("ui", q0, q1), A(ps[5], 0, 32))
+            ts(A("u", q0, q1), A("ui", q0, q1), 4095, band)
+            ts(A("u32", q0, q1), A("u", q0, q1), 32.0, add_)
+            tt(A("uw", q0, q1), A("u", q0, q1), A("u32", q0, q1), mul)
+            ts(A("h", q0, q1), A("uw", q0, q1), 5, shr, 4095, band)
+            tt(A("Rh", 128 * c, 128 * c + 128), IND(A("h", q0, q1), LH4), A("M4"), mul)
+            mm(A(ps[5], 32, 64), A("Rh", 128 * c, 128 * c + 128), A("Bm4f"))
+            cp(A("HL", q0, q1), A(ps[5], 32, 64))
+            if c in OWN_ACT:
+                act(A("xh"), IND(XWIN, A("HL", q0, q1)), AF.Copy)
+                mm(A(sb), A("NIDb"), PI, True, False)
+                mm(A(sb), A("IDb"), A("xh"), False, True)
+                act(A("ad2", o0, o1), A(sb), AF.Abs)
+            else:
+                for k in range(2):
+                    o = o0 + 256 * k
+                    tt(A("d2", o, o + 256), IND(XWIN, A("HL", q0 + 16 * k, q0 + 16 * k + 16)),
+                       A("W", 1024 + o, 1280 + o), sub_)
+                    act(A("ad2", o, o + 256), A("d2", o, o + 256), AF.Abs)
+            act(A("rec", o0, o1), IND(A(XR), A("HL", q0, q1)), AF.Copy)
+            mm(A(sb), A("IDb"), PI, True, False)
+            mm(A(sb), A("IDb"), A("rec", o0, o1), False, True)
+            act(A("F1", o0, o1), A(sb), AF.Identity, 127.75, 0.5)
+            act(A("W", 2048 + o0, 2048 + o1), A("F1", o0, o1), AF.Identity, -128.0)
+
+        for c in range(2):
+            w0, w1 = 256 * c, 256 * c + 256
+            mm(A(ps[5 + c], 256, 512), A("ONES"), A("BIAS"), True, False)
+            mm(A(ps[5 + c], 256, 512), A("IDb"), A("al", w0, w1), False, False)
+            mine = [i for i in range(1, 8) if (c, i) in BY_MIN]
+            rest = [i for i in range(1, 8) if (c, i) not in BY_MIN]
+            turn = []
+            while mine or rest:
+                turn += [x.pop(0) for x in (rest, mine) if x]
+            held = ps[4] if c else ps[2]
+            for i in turn:
+                if (c, i) in BY_MIN:
+                    o = 3584 * c + 512 * (i - 1)
+                    for jj in range(4):
+                        oo = 256 + 128 * (jj >> 1)
+                        mm(A(ps[5 + c], oo + 8 * (jj & 1) + 7 - i, oo + 128, 16), A("a", o + jj, o + 512, 4),
+                           A("OB256", 0, 8), False, False)
+            if any((c, i) in BY_MIN for i in turn):
+                mm(A(held), A("IDb"), A("b", 512 * c, 512 * c + 512))
+                for jj in range(4):
+                    oo = 256 + 128 * (jj >> 1)
+                    mm(A(ps[5 + c], oo, oo + 128), A("b", 512 * c + jj, 512 * c + 512, 4),
+                       A("RB", 128 * (jj & 1), 128 * (jj & 1) + 128), False, False)
+            nabs = 0
+            for i in turn:
+                o = 3584 * c + 512 * (i - 1)
+                terms = [("ad", o, "OB256")]
+                if (c, i) in BY_MIN:
+                    tt(A("ad", o, o + 512), A("a", o, o + 512), A(held), mn)
+                    terms = [("ad", o, "OBm")]
+                else:
+                    bank = ps[nabs % 2]
+                    nabs += 1
+                    mm(A(bank), A("IDb"), A("a", o, o + 512), True, False)
+                    mm(A(bank), A("NIDb"), A("b", 512 * c, 512 * c + 512), False, True)
+                    act(A("ad", o, o + 512), A(bank), AF.Abs)
+                for name, o2, rhs in terms:
+                    for jj in range(4):
+                        oo = 256 + 128 * (jj >> 1)
+                        mm(A(ps[5 + c], oo + 8 * (jj & 1) + 7 - i, oo + 128, 16), A(name, o2 + jj, o2 + 512, 4),
+                           A(rhs, 0, 8), False, i == turn[-1] and jj == 3 and name == "ad")
+            act(A("P", w0, w1), A(ps[5 + c], 256, 512), AF.Sign)
+            for yy in range(2):
+                o = w0 + 128 * yy
+                mm(A(ps[5 + c], 128 * yy, 128 * yy + 128), A("al", o, o + 128), A("IDc"), True, False)
+                mm(A(ps[5 + c], 128 * yy, 128 * yy + 128), A("P", o, o + 128), A("IDa"), False, True)
+            act(A("penT", w0, w1), A(ps[5 + c], 0, 256), AF.Identity, 96.5)
+            if c == 1:
+                names(0)
+                if EQ_LATE:
+                    same_node(0)
+            for jj in range(4):
+                j = 4 * c + jj
+                for hf in range(2):
+                    bank = ps[2 + nscan[0] % 2]
+                    pT = A("penT", 128 * (j >> 1) + 64 * hf, 128 * (j >> 1) + 64 * hf + 64)
+                    for i in range(8):
+                        x = 8 * (j & 1) + 7 - i
+                        mm(A(bank, i, 512, 8), A("BD", 128 * x, 128 * x + 128), pT)
+                    o = 1024 * j + 512 * hf
+                    src = A(bank)
+                    if (2 * j + hf) in VIA_ACT:
+                        src = A("z%d" % (nscan[1] % 2))
+                        nscan[1] += 1
+                        act(src, A(bank), AF.Copy)
+                    scan(A("s", o, o + 512), src, A("m", o, o + 512), add_, mx)
+                    nscan[0] += 1
+        ST = A("st", 0, 8)
+        for y in range(4):
+            mm(A(ps[7], 384, 392), A("penT", 128 * y, 128 * y + 128), OBb, y == 0, y == 3)
+        ts(A("si"), A(ps[7], 384, 392), -1.0, mul, 16384.0, add_)
+        ts(A("nm"), A("si"), 63, band)
+        ts(ST, A("nm"), A("thr", 0, 1), OP_.is_le)
+        mm(A(ps[7], 392, 400), A("NIDb"), ST, True, False)
+        for g_ in range(8):
+            mm(A(ps[7], 392 + g_, 393 + g_), A("EQm", 128 * g_, 128 * g_ + 128), A("st", g_, g_ + 1), False, g_ == 7)
+        act(A("ld"), A(ps[7], 392, 400), AF.Relu, 0.0, -1.0)
+        tt(A("lv"), A("ld"), A("vmd"), mul)
+        tt(A("Rs"), IND(A("lv"), LREP), A("CM"), mul)
+        mm(A(ps[7], 400, 408), A("DM"), A("OBf"), True, False)
+        mm(A(ps[7], 400, 408), A("Rs"), A("OBf"), False, True)
+        cp(A("SL"), A(ps[7], 400, 408))
+        if t < RO - 1:
+            for g_ in range(8):
+                mm(A(ps[7], 408, 409), A("ONES"), A("st", g_, g_ + 1), g_ == 0, g_ == 7)
+            ts(A("Ai", 0, 1), A(ps[7], 408, 409), -1.0, mul, 1024.0, add_)
+            ts(A("A7", 0, 1), A("Ai", 0, 1), 7, band)
+            ts(A("thr", 0, 1), A("A7", 0, 1), 14.0, add_)
+        names(1)
+        mm(A(ps[2], 0, 64), A("NM"), A("Bm2"), True, False)
+        for j in range(8):
+            o = 1024 + 512 * (j >> 2)
+            mm(A(ps[6], j, 64, 8), A("W", o + (j & 3), o + 512, 4), OBb)
+        act(A("full"), A(ps[6], 0, 64), AF.Sign)
+        mm(A(ps[6], 64, 128), A("IDb"), A("JK"), True, False)
+        mm(A(ps[6], 64, 128), ID32, A("NS", 64, 128), False, False)
+        for j in range(8):
+            o = 1024 + 512 * (j >> 2)
+            mm(A(ps[6], 64 + j, 128, 8), A("W", o + (j & 3), o + 512, 4), A("OBk", 0, 8), False, j == 7)
+        tt(A("sf"), IND(ST, LR8), A("full"), mul)
+        tt(A("k3"), A("sf"), A(ps[6], 64, 128), mul)
+        scan(A("k4"), A("RS"), A("k3"), mul, mx)
+        tt(A("gi"), A("k4", 7, 64, 8), A("N1T", 8 + t, 128, 16), mx)
+        ts(A("go"), A("gi"), 2047, band)
+        tt(A("Rv"), IND(A("go"), LREP), A("CM"), mul)
+        mm(A(ps[6], 128, 136), A("Rv"), A("OBf"))
+        if t < RO - 1:
+            cp(A("VL"), A(ps[6], 128, 136))
+        else:
+            cp(A("yvf"), A(ps[6], 128, 136))
+            dma("sp", HB("yv"), A("yvf"), 4096)
+        act(A("NS", 0, 64), IND(A("h"), LHG), AF.Copy)
+        tt(A("nmh", 0, 64), A("nT"), A("NS", 0, 64), sub_)
+        tt(A("dl"), IND(A("NS"), LNS), A("N1T"), sub_)
+        tt(A("fr"), IND(A("full"), LDUP), A("dl"), mul)
+        mm(A(ps[7], 0, 128), A("fr"), ID32, True, False)
+        act(A("cn"), IND(A("nmh", 0, 65), LCN), AF.Copy)
+        mm(A(ps[5], 64, 128), A("I2K"), A("sf"), True, False)
+        for j in range(8):
+            o = 512 * (j >> 2)
+            mm(A(ps[5], 64 + j, 128, 8), A("ad2", o + (j & 3), o + 512, 4), OBb, False, j == 7)
+        ts(A("ask"), A(ps[5], 64, 128), 2048.0 + 24.0, OP_.is_gt)
+        tt(A("df"), IND(A("ask"), LDUP), A("cn"), mul)
+        mm(A(ps[7], 0, 128), A("df"), ID32, False, True)
+        tt(A("En"), A("N1f"), A(ps[7], 0, 128), add_)
+        cp(IND(A("E"), A("SL")), A("En"))
+        scan(A("incl"), A("RS"), A("ask"), mul, add_)
+        mm(A(ps[3], 0, 64), A("N2K"), A("ask"), True, False)
+        mm(A(ps[3], 0, 64), A("IDb"), A("incl"), False, False)
+        for j in range(8):
+            mm(A(ps[3], j, 64, 8), A("TRI"), A("incl", 7, 64, 8), False, j == 7)
+        tt(A("aD"), IND(A("ask"), LDUP), A("MD"), mul)
+        mm(A(ps[2], 0, 64), A("aD"), A("Bm2"), False, False)
+        ts(A("tq"), A(ps[3], 0, 64), 256.0 - 2048.0, OP_.is_le)
+        tt(A("Rc"), IND(A("tq"), LDUP), A("MK"), mul)
+        mm(A(ps[2], 0, 64), A("Rc"), A("Bm2"), False, True)
+        cp(A("CL"), A(ps[2], 0, 64))
+        xa = XA if t < RO - 1 else 512
+        act(A("X", blk, blk + xa), IND(A("W"), A("CL", 0, xa // 16)), AF.Copy)
+        if xa < 1024:
+            cp(A("X", blk + xa, blk + 1024), IND(A("W"), A("CL", xa // 16, 64)))
+    dma("sp", HB("ye", 0, 960), A("E", 0, 960), 1000000)
+    dma("sp", HB("ye", 960, V), A("E", 960, V), 1000000)
+    dma("sp", HB("yx", 0, 1024), A("X", 0, 1024), 262144)
+    seen = {}
+    for o in ops:
+        out = o["out"]
+        key = o["eng"] + ":" + (out[1] if out[0] != "ind" else out[1][1] + "!") if out and o["eng"] else "-"
+        if o["kind"] == "send":
+            seen.clear()
+        seen[key] = seen.get(key, 0) + 1
+        o["key"] = "%s#%d" % (key, seen[key])
+    return ops
+
+
+def dependencies(ops):
+    seen = {}
+    for k, o in enumerate(ops):
+        hard, soft = set(), set()
+        reads = [s for x in o["ins"] for s in _spans(x)]
+        writes = []
+        if o["out"] is not None:
+            if o["out"][0] == "ind":
+                writes, reads = _spans(o["out"][1]), reads + _spans(o["out"][2])
+            else:
+                writes = _spans(o["out"])
+        asyn = o["kind"] in ("dma", "send", "arrive")
+        for isw, group in ((False, reads), (True, writes)):
+            for name, lo, hi in group:
+                psum = SPEC[name][0] == "psum"
+                keep = []
+                for rec in seen.get(name, []):
+                    k2, w2, lo2, hi2 = rec
+                    if k2 == k:
+                        keep.append(rec)
+                        continue
+                    o2 = ops[k2]
+                    same = o2["eng"] == o["eng"] and not asyn and o2["kind"] not in ("dma", "send", "arrive")
+                    over = lo < hi2 and lo2 < hi
+                    if psum and not same:
+                        hard.add(k2)
+                        continue
+                    if psum:
+                        soft.add(k2)
+                        continue
+                    if over and (isw or w2):
+                        hard.add(k2)
+                        if isw and lo <= lo2 and hi2 <= hi and (not same or o["out"][0] == "ind" or o["out"][0] == "ap" and o["out"][4] == 1):
+                            continue
+                    keep.append(rec)
+                keep.append((k, isw, lo, hi))
+                seen[name] = keep
+        o["hard"], o["soft"] = hard, soft - hard
+    send = {o["par"]: k for k, o in enumerate(ops) if o["kind"] == "send"}
+    for o in ops:
+        o["time"] = set([send[o["par"]]]) if o["kind"] == "arrive" else set()
+
+
+def schedule(ops):
+    n = len(ops)
+    LX, LS_ = 120.0, 70.0
+    after = [[] for _ in range(n)]
+    for k, o in enumerate(ops):
+        for d in o["hard"] | o["soft"] | o["time"]:
+            after[d].append(k)
+    rank = [0.0] * n
+    for k in range(n - 1, -1, -1):
+        rank[k] = ops[k]["ns"] + max([rank[x] + (LX if k in ops[x]["hard"] else 0.0) for x in after[k]] + [0.0])
+    left = [len(o["hard"] | o["soft"] | o["time"]) for o in ops]
+    ready_at = [0.0] * n
+    free = {e: 0.0 for e in ENG}
+    pool = {e: [] for e in ENG}
+    order = {e: [] for e in ENG}
+    start = [0.0] * n
+
+    def finish(k):
+        todo = [k]
+        while todo:
+            q = todo.pop()
+            for x in after[q]:
+                if q in ops[x]["soft"]:
+                    at = start[q] + ops[q]["hold"]
+                else:
+                    at = start[q] + ops[q]["ns"] + (LS_ if ops[q]["eng"] == ops[x]["eng"] else LX)
+                ready_at[x] = max(ready_at[x], at)
+                left[x] -= 1
+                if left[x] == 0:
+                    if ops[x]["eng"] is None:
+                        start[x] = ready_at[x]
+                        todo.append(x)
+                    else:
+                        pool[ops[x]["eng"]].append(x)
+    for k in range(n):
+        if left[k] == 0:
+            pool[ops[k]["eng"]].append(k)
+    while any(pool.values()):
+        best = None
+        for e in ENG:
+            if pool[e]:
+                at = max(free[e], min(ready_at[x] for x in pool[e]))
+                if best is None or at < best[0]:
+                    best = (at, e)
+        at, e = best
+        cand = [x for x in pool[e] if ready_at[x] <= at + 60.0]
+        k = max(cand, key=lambda x: (ops[x]["ns"] < 1000 and ops[x]["key"][4:6] not in ("EQ", "s#"), rank[x], -x))
+        pool[e].remove(k)
+        start[k] = max(at, ready_at[k])
+        free[e] = start[k] + ops[k]["hold"]
+        order[e].append(k)
+        finish(k)
+    return order, start
+
+
+HINT = {}
+for _e, _text in (
+        ("dve", "OP#1 .6 m#1 .9 AL#1 1.7 OP#2 1.75 m#2 1.9 m#3 2.8 AL#2 3.4 OP#3 3.5 m#4 4.5 m#5 6.2 al#1 8.5 m#6 8.9 sc#1 9.0 "
+                "Rb#1 9.3 m#7 9.9 BL#1 9.8 m#8 11 m#9 12 m#10 13 m#11 14.6 al#2 16.4 sc#2 17 Rb#2 17.3 BL#2 17.7 s#1 18 "
+                "s#2 18.6 s#3 19.2 ad#1 19.7 ad#2 20.3 ad#3 20.9 ad#4 21.2 s#4 21.5 s#5 22 s#6 22.6 s#7 23.2 s#8 23.8"),
+        ("act", "a#1 1.7 a#2 3.2 a#3 4.7 a#4 6.2 a#5 7.7 a#6 9.2 b#1 10.7 ad#1 11.6 ad#2 12.2 ad#3 12.8 ad#4 13.4 ad#5 14 "
+                "ad#6 14.6 ad#7 15.2 P#1 15.9 a#7 16.2 penT#1 16.1 b#2 17.8 a#8 18.7 ad#8 20.2 ad#9 20.8 ad#10 21.4 "
+                "ad#11 22 P#2 22.7 penT#2 23.2")):
+    _w = _text.split()
+    for _i in range(0, len(_w), 2):
+        HINT[_e + ":" + _w[_i]] = float(_w[_i + 1])
+
+
+def improve(ops, start, steps, seed=1):
+    n = len(ops)
+    hold, ns, eng = [o["hold"] for o in ops], [o["ns"] for o in ops], [o["eng"] for o in ops]
+    pred = [[(d, hold[d]) for d in o["soft"]]
+            + [(d, ns[d] + (70.0 if eng[d] == o["eng"] else 120.0)) for d in o["hard"] | o["time"]] for o in ops]
+    back = [[] for _ in ops]
+    for k in range(n):
+        for d, lag in pred[k]:
+            back[d].append((k, hold[k] + lag - hold[d]))
+
+    def place(key, pre, rel, fwd):
+        key = list(key)
+        for k in (range(n) if fwd else range(n - 1, -1, -1)):
+            for d, _ in pre[k]:
+                if key[d] >= key[k]:
+                    key[k] = key[d] + 1e-3
+        st = [0.0] * n
+        busy = {e: ([], []) for e in ENG}
+        for k in sorted(range(n), key=lambda q: key[q]):
+            at = rel[k]
+            for d, lag in pre[k]:
+                if st[d] + lag > at:
+                    at = st[d] + lag
+            if eng[k] is not None:
+                lo, hi = busy[eng[k]]
+                a, b = 0, len(hi)
+                while a < b:
+                    mid = (a + b) // 2
+                    if hi[mid] <= at:
+                        a = mid + 1
+                    else:
+                        b = mid
+                while a < len(lo) and lo[a] < at + hold[k]:
+                    at = hi[a]
+                    a += 1
+                lo.insert(a, at)
+                hi.insert(a, at + hold[k])
+            st[k] = at
+        return st
+    zero, tail = [0.0] * n, [ns[k] - hold[k] for k in range(n)]
+
+    def justify(st):
+        r = place([-(st[k] + hold[k]) for k in range(n)], back, tail, False)
+        return place([-(r[k] + hold[k]) for k in range(n)], pred, zero, True)
+
+    def span(st):
+        return max(st[k] + ns[k] for k in range(n))
+    groups = {}
+    for k, o in enumerate(ops):
+        if eng[k] in ("dve", "act"):
+            groups.setdefault(o["key"], []).append(k)
+    names = sorted(x for x in groups if len(groups[x]) > 1)
+    second = [k for k, o in enumerate(ops) if o["kind"] == "send"][1]
+    early = [k for k in range(second) if eng[k] in ("dve", "act", "pool")]
+    rng = np.random.default_rng(seed)
+    cur = justify(start)
+    for _ in range(3):
+        key, base = list(cur), 0.0
+        for k, o in enumerate(ops):
+            if o["key"] == "dve:Th#1":
+                base = cur[k]
+            if o["key"] in HINT:
+                key[k] = base + 1000.0 * HINT[o["key"]]
+        first = min(k for k, o in enumerate(ops) if o["kind"] == "send")
+        for k in range(first):
+            key[k] = 1e9
+            name = ops[k]["key"].split("#")[0]
+            if name in ("dve:BLK", "dve:E16", "dve:CF", "dve:OBf") or (eng[k] == "pool" and name != "pool:IOT"):
+                key[k] = 1000.0 + k
+        for k in range(n - 1, -1, -1):
+            for d, lag in pred[k]:
+                if key[d] > key[k] - lag and (key[k] < cur[k] or d < first or k < first + 140):
+                    key[d] = key[k] - lag
+        cur = place(key, pred, zero, True)
+    best, cost = cur, span(cur)
+    low = cost
+    for it in range(steps):
+        key = list(cur)
+        for _ in range(int(rng.integers(1, 3))):
+            shift = float(rng.choice([-1.0, 1.0]) * np.exp(rng.uniform(5.0, 9.0)))
+            if rng.random() < 0.35:
+                key[early[int(rng.integers(len(early)))]] += shift
+                continue
+            for k in groups[names[int(rng.integers(len(names)))]]:
+                key[k] += shift
+        for k in range(n - 1, -1, -1):
+            for d, lag in pred[k]:
+                if key[d] > key[k] - lag and key[k] < cur[k]:
+                    key[d] = key[k] - lag
+        st = place(key, pred, zero, True)
+        if it % 4 == 0:
+            st = justify(st)
+        c = span(st)
+        if c <= cost + 400.0 * (1.0 - it / steps):
+            cur, cost = st, c
+            if c < low:
+                best, low = st, c
+    order = {e: sorted((k for k in range(n) if eng[k] == e), key=lambda q: (best[q], q)) for e in ENG}
+    return order, best
+
+
+def plan(steps=2500, seed=1):
+    ops = program()
+    dependencies(ops)
+    order, start = schedule(ops)
+    order, start = improve(ops, start, steps, seed)
+    pos = {}
+    for e in ENG:
+        for i, k in enumerate(order[e]):
+            pos[k] = i
+    seq = sorted((k for e in ENG for k in order[e]), key=lambda k: (start[k], pos[k]))
+    know = {e: {} for e in ENG}
+    done = {}
+    for k in seq:
+        o = ops[k]
+        kn = know[o["eng"]]
+        waits = []
+        for d in sorted(o["hard"], key=lambda d: -start[d]):
+            od = ops[d]
+            if od["kind"] in ("dma", "send", "arrive"):
+                if ("x", d) not in kn:
+                    waits.append(d)
+                    kn[("x", d)] = 1
+                    for key, val in done.get(d, {}).items():
+                        kn[key] = max(kn.get(key, -1), val)
+            elif kn.get(od["eng"], -1) < pos[d]:
+                waits.append(d)
+                kn[od["eng"]] = pos[d]
+                for key, val in done[d].items():
+                    kn[key] = max(kn.get(key, -1), val)
+        o["waits"] = waits
+        done[k] = dict(kn)
+    needed = set(d for o in ops if o["eng"] is not None for d in o["waits"])
+    count = {}
+    for e in ENG:
+        c = 0
+        for k in order[e]:
+            if k in needed and ops[k]["kind"] not in ("dma", "send"):
+                c += 1
+                count[k] = c
+    return ops, order, count, needed, start
+
+
+_PLAN = []
+
+
+def rank_program(g, core, T, topo):
+    rank = T.rank_of(core)
+    if rank is None:
+        return
+    if not _PLAN:
+        _PLAN.append(plan())
+    ops, order, count, needed, _ = _PLAN[0]
+    queue = {"pe": g.tensor, "dve": g.vector, "act": g.scalar, "pool": g, "sp": g.sync}
+    n = len(T.cores)
+
+    def ap(x):
+        if not isinstance(x, tuple):
+            return x
+        if x[0] == "ind":
+            return ap(x[1]).indirect(ap(x[2]))
+        if x[0] == "hbm":
+            return T[x[1]][:] if x[2] is None else T[x[1]][:, x[2]:x[3]]
+        buf, at = SPEC[x[1]][3:]
+        if x[4] == 1:
+            return T[buf][:, at + x[2]:at + x[3]]
+        return T[buf][:, at + x[2]:at + x[3]:x[4]]
+
+    def sem_of(d):
+        o = ops[d]
+        if o["kind"] == "dma":
+            return T.sem[o["par"]], 16
+        if o["kind"] == "send":
+            dst = T.cores[(rank - 1 - o["par"] % (n - 1)) % n]
+            return T.sem["snt%d" % o["par"]], len(topo.engines(core, dst))
+        if o["kind"] == "arrive":
+            src = T.cores[(rank + 1 + o["par"] % (n - 1)) % n]
+            return T.sem["arr%d" % o["par"]], len(topo.engines(src, core))
+        return T.sem["c_" + o["eng"]], count[d]
+
+    for e in ENG:
+        q = queue[e]
+        for k in order[e]:
+            o = ops[k]
+            for d in o["waits"]:
+                s, val = sem_of(d)
+                q.wait_ge(s, val)
+            kind, par = o["kind"], o["par"]
+            out = ap(o["out"]) if o["out"] is not None else None
+            ins = [ap(x) for x in o["ins"]]
+            if kind == "send":
+                dst = T.cores[(rank - 1 - par % (n - 1)) % n]
+                rid, pid, _ = topo.addr(dst)
+                g.remote_dma(T["XR%d" % par][:], ins[0], T.sem["arr%d" % par], T.sem["snt%d" % par], pid, rid,
+                             topo.mask(core, dst))
+                continue
+            if kind == "dma":
+                q.dma_start(out, ins[0]).then_inc(T.sem[par], 16)
+                continue
+            if kind == "mm":
+                r = q.matmul(out, ins[0], ins[1], par[0], par[1])
+            elif kind == "copy":
+                r = q.tensor_copy(out, ins[0])
+            elif kind == "ts":
+                if par[1] is None:
+                    r = q.tensor_scalar(out, ins[0], ins[1], None, par[0])
+                else:
+                    r = q.tensor_scalar(out, ins[0], ins[1], ins[2], par[0], par[1])
+            elif kind == "tt":
+                r = q.tensor_tensor(out, ins[0], ins[1], par)
+            elif kind == "scan":
+                r = q.tensor_tensor_scan(out, ins[0], ins[1], 0.0, par[0], par[1])
+            elif kind == "memset":
+                r = q.memset(out, par)
+            elif kind == "tr":
+                r = q.transpose(out, ins[0])
+            elif kind == "red":
+                r = q.tensor_reduce(out, ins[0], AxisListType.X, OP_.add)
+            elif kind == "act":
+                r = q.activation(out, ins[0], par, ins[1], ins[2])
+            elif kind == "iota":
+                if SPEC[o["out"][1]][2] == "int32":
+                    r = g.iota(out, par[0], par[1], par[2])
+                else:
+                    r = g.iota(out, par[0], par[1], par[2], allow_small_or_imprecise_dtypes=True)
+            else:
+                r = g.affine_select(out, ins[0], par[0], par[1], 0.0, par[2], par[3])
+            if k in count:
+                r.then_inc(T.sem["c_" + e], 1)
+    for k, o in enumerate(ops):
+        if o["kind"] in ("dma", "send", "arrive") and k not in needed:
+            s, val = sem_of(k)
+            g.sync.wait_ge(s, val)

@@ -3,10 +3,12 @@ from concourse.mybir import AluOpType, AxisListType, ActivationFunctionType
 
 H = "float16"
 V, XW, RO = 1920, 4096, 5
+LAG = (220.0, 130.0)
 XA = 1024
 HALVES = [0, 4, 5]
 OWN_ACT = [0]
 EQ_ACT, EQ_LATE = [1], False
+FUSED = []
 BY_MIN = [(1, 1), (1, 2), (1, 3), (1, 4)]
 VIA_ACT = (9, 11, 13, 15)
 
@@ -33,12 +35,12 @@ _decl("sbuf", "bfloat16", {
     "W": 3072, "XP": 1024, "b": 1024, "d2": 1024, "ad2": 1024, "rec": 1024, "F1": 1024, "al": 512, "P": 512,
     "penT": 512, "EQ": 1024, "EQm": 1024, "z0": 512, "z1": 512, "IDb": 128, "NIDb": 128, "BLK": 128, "BD": 18 * 128,
     "WB": 16, "OBb": 16, "OB256": 16, "OBk": 16, "OBm": 16, "ONES": 128, "BIAS": 256, "BIAS2": 256, "TRI": 128, "st": 16,
-    "ask": 64, "sf": 64, "WS": 32, "wb": 16, "SelS": 64, "WIDE": 1024, "OBh": 16, "Bm4": 32, "RB": 256, "t0": 128, "t1": 128, "I2K": 128, "N2K": 128, "EQa": 1024, "xh": 512, "incl": 64, "IDa": 128, "IDc": 128, "JK": 64})
+    "ask": 64, "sf": 64, "WS": 32, "wb": 16, "yn": 16, "N64": 128, "I4M": 128, "B4M": 64, "NWIDE": 1024, "SelS": 64, "WIDE": 1024, "OBh": 16, "Bm4": 32, "RB": 256, "t0": 128, "t1": 128, "I2K": 128, "N2K": 128, "EQa": 1024, "xh": 512, "incl": 64, "IDa": 128, "IDc": 128, "JK": 64})
 _decl("sbuf", H, {"N1h": 128, "N2h": 1024, "Th": 1024, "IWh": 192, "PM": 16 * 128,
                   "vr": 128, "nvr": 128, "Rb": 256})
 _decl("sbuf", "float32", {
     "E": 2048, "IOT": V, "N1f": 128, "N1T": 128, "sc": 512, "NS": 128, "nT": 64, "nmh": 72, "fr": 128, "cn": 128, "lc": 8,
-    "full": 64, "lv": 8, "wsf": 8, "OBs": 8, "dl": 128, "df": 128, "En": 128, "tq": 64, "aM": 128,
+    "full": 64, "sg": 8, "Af": 8, "NOBf": 8, "OBn": 8, "wsf": 8, "OBs": 8, "dl": 128, "df": 128, "En": 128, "tq": 64, "aM": 128,
     "Rc": 128, "Rh": 256, "Rv": 128, "Rs": 128, "aD": 128, "k3": 64, "k4": 64, "ld": 8, "vmd": 8, "VM": 128,
     "thr": 8, "yvf": 8, "wf": 8, "ONE": 192, "IW": 192, "FC": 32, "MC": 24, "E16": 24, "CF": 24,
     "r128": 128, "rc": 128, "rh": 128, "r4": 128, "rg": 128, "rn": 128, "rd": 128, "MH": 128, "MK": 128, "MD": 128,
@@ -87,7 +89,7 @@ def _spans(x):
     return [(x[1], x[2], x[2] + (_n(x) - 1) * x[4] + 1)]
 
 
-def program(CY=1.04, G=1.5, PE=0.52, BW=330.0):
+def program(CY=0.95, G=1.56, PE=0.48, BW=330.0):
     ops = []
 
     def add(eng, kind, out, ins, par, ns, hold=None):
@@ -238,7 +240,6 @@ def program(CY=1.04, G=1.5, PE=0.52, BW=330.0):
         for part in range(2):
             ts(A("WS", 16 * j0 + 8 * part, 16 * j0 + 8 * part + 8), A("OBf"), A("E16", 8 * j0, 8 * j0 + 1), mul,
                A("wsf", part, part + 1), mul)
-    lin(newcol("ndump"), col("p"), -1.0, -float(V))
     iota(A("IOT"), [[1, V]], 0, 0)
     lin(A("t0"), A("BLK"), 256.0)
     ilo, ihi = min(i for _, i in BY_MIN), max(i for _, i in BY_MIN)
@@ -285,7 +286,15 @@ def program(CY=1.04, G=1.5, PE=0.52, BW=330.0):
     cp(LREP, A("r128", 0, 8))
     ts(LR8, A("r128", 0, 4), 2.0, mul, col("k8"), add_)
     ts(LNS, A("r128", 0, 8), 8.0, mul, col("lns"), add_)
-    mset(A("thr", 0, 1), 14.0)
+    lin(A("thr", 0, 1), A("ONE", 0, 1), 4096.0 + 14.5)
+    lin(A("N64"), ID32, -64.0)
+    lin(A("I4M"), ID32, 4194304.0)
+    lin(A("B4M"), A("ONE", 0, 64), -32768.0)
+    lin(A("NOBf"), A("OBf"), -1.0)
+    lin(newcol("d2k"), col("p"), 1.0, float(V - 2048))
+    lin(A("OBn"), A("OBf"), -1.0 / 16)
+    for g_ in range(8):
+        lin(A("NWIDE", 128 * g_, 128 * g_ + 128), A("ONE", 0, 128), A("OBn", g_, g_ + 1))
     ts(A("LI"), A("r128", 0, V // 16), 16.0, mul, col("c16"), add_)
     for k in range(3):
         act(A("E", 640 * k, 640 * k + 640), IND(A("E0"), A("LI", 40 * k, 40 * k + 40)), AF.Copy)
@@ -328,13 +337,10 @@ def program(CY=1.04, G=1.5, PE=0.52, BW=330.0):
         mm(A(ps[7], 128, 256), A("N1f"), ID32)
         act(A("N1T"), A(ps[7], 128, 256), AF.Copy)
         cp(A("vr"), IND(A("IOT"), A("VL")))
-        ts(A("nvr"), A("vr"), -1.0, mul)
-        mm(A(ps[7], 256, 264), A("vr"), A("OBh", 0, 8))
-        lin(A("vmd"), A(ps[7], 256, 264), 1.0, col("ndump"))
 
         def same_node(bank):
             for hf in range(2):
-                mm(A(ps[bank + hf]), A("nvr"), A("WIDE", 512 * hf, 512 * hf + 512), True, False)
+                mm(A(ps[bank + hf]), A("vr"), A("NWIDE", 512 * hf, 512 * hf + 512), True, False)
                 for g4 in range(4):
                     g_ = 4 * hf + g4
                     mm(A(ps[bank + hf], 128 * g4, 128 * g4 + 128), A("WIDE", 128 * g_, 128 * g_ + 128), A("vr"),
@@ -342,17 +348,19 @@ def program(CY=1.04, G=1.5, PE=0.52, BW=330.0):
                 o0, o1 = 512 * hf, 512 * hf + 512
                 if hf in EQ_ACT:
                     act(A("EQa", o0, o1), A(ps[bank + hf]), AF.Abs)
-                    ts(A("EQ", o0, o1), A("EQa", o0, o1), 0.0, eq)
+                    ts(A("EQ", o0, o1), A("EQa", o0, o1), 0.0, eq, 2048.0, mul)
                 else:
-                    ts(A("EQ", o0, o1), A(ps[bank + hf]), 0.0, eq)
+                    ts(A("EQ", o0, o1), A(ps[bank + hf]), 0.0, eq, 2048.0, mul)
                 sel(A("EQm", o0, o1), A("EQ", o0, o1), [[0, 4], [1, 128]], OP_.is_gt, 0, -1)
         if not EQ_LATE:
             same_node(2)
         lin(A("nT"), A("rn", 0, 64), 1.0, float(blk))
         for c in range(2):
-            for k in range(4):
-                act(A("a", 3584 * c + 896 * k, 3584 * c + 896 * k + 896),
-                    IND(XWIN, A("AL", 224 * c + 56 * k, 224 * c + 56 * k + 56)), AF.Copy)
+            top = 224 - 32 * sum(1 for x in FUSED if x[0] == c)
+            step = 2 * ((top + 7) // 8)
+            for k in range(0, top, step):
+                k1 = min(top, k + step)
+                act(A("a", 3584 * c + 16 * k, 3584 * c + 16 * k1), IND(XWIN, A("AL", 224 * c + k, 224 * c + k1)), AF.Copy)
             for jj in range(4):
                 j = 4 * c + jj
                 for l0, l1 in ([(0, 32), (32, 64)] if j in HALVES else [(0, 64)]):
@@ -452,8 +460,12 @@ def program(CY=1.04, G=1.5, PE=0.52, BW=330.0):
                 if (c, i) in BY_MIN:
                     tt(A("ad", o, o + 512), A("a", o, o + 512), A(held), mn)
                     terms = [("ad", o, "OBm")]
+                elif (c, i) in FUSED:
+                    k = 224 * c + 32 * (i - 1)
+                    tt(A("a", o, o + 512), IND(XWIN, A("AL", k, k + 32)), A("b", 512 * c, 512 * c + 512), sub_)
+                    act(A("ad", o, o + 512), A("a", o, o + 512), AF.Abs)
                 else:
-                    bank = ps[nabs % 2]
+                    bank = ps[nabs % (2 if c else 4)]
                     nabs += 1
                     mm(A(bank), A("IDb"), A("a", o, o + 512), True, False)
                     mm(A(bank), A("NIDb"), A("b", 512 * c, 512 * c + 512), False, True)
@@ -476,7 +488,7 @@ def program(CY=1.04, G=1.5, PE=0.52, BW=330.0):
             for jj in range(4):
                 j = 4 * c + jj
                 for hf in range(2):
-                    bank = ps[2 + nscan[0] % 2]
+                    bank = ps[(2, 3, 1)[nscan[0] % 3]] if c else ps[2 + nscan[0] % 2]
                     pT = A("penT", 128 * (j >> 1) + 64 * hf, 128 * (j >> 1) + 64 * hf + 64)
                     for i in range(8):
                         x = 8 * (j & 1) + 7 - i
@@ -492,24 +504,28 @@ def program(CY=1.04, G=1.5, PE=0.52, BW=330.0):
         ST = A("st", 0, 8)
         for y in range(4):
             mm(A(ps[7], 384, 392), A("penT", 128 * y, 128 * y + 128), OBb, y == 0, y == 3)
-        ts(A("si"), A(ps[7], 384, 392), -1.0, mul, 16384.0, add_)
-        ts(A("nm"), A("si"), 63, band)
-        ts(ST, A("nm"), A("thr", 0, 1), OP_.is_le)
-        mm(A(ps[7], 392, 400), A("NIDb"), ST, True, False)
+        lin(A("yn", 0, 8), A(ps[7], 384, 392), 1.0 / 64, 64.4375)
+        for y in range(4):
+            mm(A(ps[7], 416, 424), A("penT", 128 * y, 128 * y + 128), OBb, y == 0, False)
+        mm(A(ps[7], 416, 424), A("N64"), A("yn", 0, 8), False, True)
+        act(A("sg"), A(ps[7], 416, 424), AF.Sign, A("thr", 0, 1))
+        act(ST, A("sg"), AF.Relu)
+        mm(A(ps[7], 392, 400), A("vr"), A("OBh", 0, 8), True, False)
+        mm(A(ps[7], 392, 400), A("N2K"), ST, False, False)
         for g_ in range(8):
             mm(A(ps[7], 392 + g_, 393 + g_), A("EQm", 128 * g_, 128 * g_ + 128), A("st", g_, g_ + 1), False, g_ == 7)
-        act(A("ld"), A(ps[7], 392, 400), AF.Relu, 0.0, -1.0)
-        tt(A("lv"), A("ld"), A("vmd"), mul)
-        tt(A("Rs"), IND(A("lv"), LREP), A("CM"), mul)
+        act(A("ld"), A(ps[7], 392, 400), AF.Relu, col("d2k"), -1.0)
+        tt(A("Rs"), IND(A("ld"), LREP), A("CM"), mul)
         mm(A(ps[7], 400, 408), A("DM"), A("OBf"), True, False)
-        mm(A(ps[7], 400, 408), A("Rs"), A("OBf"), False, True)
+        mm(A(ps[7], 400, 408), A("Rs"), A("NOBf"), False, True)
         cp(A("SL"), A(ps[7], 400, 408))
         if t < RO - 1:
             for g_ in range(8):
                 mm(A(ps[7], 408, 409), A("ONES"), A("st", g_, g_ + 1), g_ == 0, g_ == 7)
-            ts(A("Ai", 0, 1), A(ps[7], 408, 409), -1.0, mul, 1024.0, add_)
-            ts(A("A7", 0, 1), A("Ai", 0, 1), 7, band)
-            ts(A("thr", 0, 1), A("A7", 0, 1), 14.0, add_)
+            lin(A("yn", 8, 9), A(ps[7], 408, 409), -0.125, 255.5625)
+            lin(A("Af", 0, 1), A(ps[7], 408, 409), -1.0, 4096.0 + 14.5 + 1024.0)
+            act(A("Af", 1, 2), A("yn", 8, 9), AF.Relu, -128.0)
+            lin(A("thr", 0, 1), A("Af", 1, 2), -8.0, A("Af", 0, 1))
         names(1)
         mm(A(ps[2], 0, 64), A("NM"), A("Bm2"), True, False)
         for j in range(8):
@@ -518,12 +534,13 @@ def program(CY=1.04, G=1.5, PE=0.52, BW=330.0):
         act(A("full"), A(ps[6], 0, 64), AF.Sign)
         mm(A(ps[6], 64, 128), A("IDb"), A("JK"), True, False)
         mm(A(ps[6], 64, 128), ID32, A("NS", 64, 128), False, False)
+        mm(A(ps[6], 64, 128), A("ONES"), A("B4M"), False, False)
         for j in range(8):
             o = 1024 + 512 * (j >> 2)
-            mm(A(ps[6], 64 + j, 128, 8), A("W", o + (j & 3), o + 512, 4), A("OBk", 0, 8), False, j == 7)
+            mm(A(ps[6], 64 + j, 128, 8), A("W", o + (j & 3), o + 512, 4), A("OBk", 0, 8), False, False)
         tt(A("sf"), IND(ST, LR8), A("full"), mul)
-        tt(A("k3"), A("sf"), A(ps[6], 64, 128), mul)
-        scan(A("k4"), A("RS"), A("k3"), mul, mx)
+        mm(A(ps[6], 64, 128), A("I4M"), A("sf"), False, True)
+        scan(A("k4"), A("RS"), A(ps[6], 64, 128), mul, mx)
         tt(A("gi"), A("k4", 7, 64, 8), A("N1T", 8 + t, 128, 16), mx)
         ts(A("go"), A("gi"), 2047, band)
         tt(A("Rv"), IND(A("go"), LREP), A("CM"), mul)
@@ -622,7 +639,7 @@ def dependencies(ops):
 
 def schedule(ops):
     n = len(ops)
-    LX, LS_ = 120.0, 70.0
+    LX, LS_ = LAG
     after = [[] for _ in range(n)]
     for k, o in enumerate(ops):
         for d in o["hard"] | o["soft"] | o["time"]:
@@ -679,7 +696,7 @@ HINT = {}
 for _e, _text in (
         ("dve", "OP#1 .6 m#1 .9 AL#1 1.7 OP#2 1.75 m#2 1.9 m#3 2.8 AL#2 3.4 OP#3 3.5 m#4 4.5 m#5 6.2 al#1 8.5 m#6 8.9 sc#1 9.0 "
                 "Rb#1 9.3 m#7 9.9 BL#1 9.8 m#8 11 m#9 12 m#10 13 m#11 14.6 al#2 16.4 sc#2 17 Rb#2 17.3 BL#2 17.7 s#1 18 "
-                "s#2 18.6 s#3 19.2 ad#1 19.7 ad#2 20.3 ad#3 20.9 ad#4 21.2 s#4 21.5 s#5 22 s#6 22.6 s#7 23.2 s#8 23.8"),
+                "s#2 18.6 s#3 19.2 a#1 19.3 a#2 19.5 ad#1 19.7 ad#2 20.3 ad#3 20.9 ad#4 21.2 s#4 21.5 s#5 22 s#6 22.6 s#7 23.2 s#8 23.8"),
         ("act", "a#1 1.7 a#2 3.2 a#3 4.7 a#4 6.2 a#5 7.7 a#6 9.2 b#1 10.7 ad#1 11.6 ad#2 12.2 ad#3 12.8 ad#4 13.4 ad#5 14 "
                 "ad#6 14.6 ad#7 15.2 P#1 15.9 a#7 16.2 penT#1 16.1 b#2 17.8 a#8 18.7 ad#8 20.2 ad#9 20.8 ad#10 21.4 "
                 "ad#11 22 P#2 22.7 penT#2 23.2")):
@@ -692,7 +709,7 @@ def improve(ops, start, steps, seed=1):
     n = len(ops)
     hold, ns, eng = [o["hold"] for o in ops], [o["ns"] for o in ops], [o["eng"] for o in ops]
     pred = [[(d, hold[d]) for d in o["soft"]]
-            + [(d, ns[d] + (70.0 if eng[d] == o["eng"] else 120.0)) for d in o["hard"] | o["time"]] for o in ops]
+            + [(d, ns[d] + (LAG[1] if eng[d] == o["eng"] else LAG[0])) for d in o["hard"] | o["time"]] for o in ops]
     back = [[] for _ in ops]
     for k in range(n):
         for d, lag in pred[k]:
@@ -789,7 +806,7 @@ def improve(ops, start, steps, seed=1):
     return order, best
 
 
-def plan(steps=2500, seed=1):
+def plan(steps=3500, seed=3):
     ops = program()
     dependencies(ops)
     order, start = schedule(ops)

@@ -1,16 +1,29 @@
 import numpy as np
-from concourse.mybir import AluOpType, AxisListType, ActivationFunctionType
+from concourse.mybir import AluOpType, ActivationFunctionType
 
 H = "float16"
 V, XW, RO = 1920, 4096, 5
 LAG = (220.0, 130.0)
-XA = 1024
-HALVES = [0, 4, 5]
-OWN_ACT = [0]
-EQ_ACT, EQ_LATE = [1], False
-FUSED = []
-BY_MIN = [(1, 1), (1, 2), (1, 3), (1, 4)]
-VIA_ACT = (9, 11, 13, 15)
+STEPS, SEED = (16000, 2500), 1
+OPT = {
+    "halves": [0, 2, 4, 6],
+    "pairs": [(1, 2), (3, 4), (5, 6), (7,)],
+    "relu": [],
+    "direct": False, "four": False, "fused": 0, "fused_abs": 0, "b_dve": (), "by_min": [], "rec_dve": (),
+    "via_act": (),
+    "own": ("act", "act", "abs", "relu"),
+    "hash_cut": 2, "early": False, "n1": "dve",
+    "n2": ("dve", "act"),
+    "eq_act": [],
+    "eq_bank": (5, 6), "eq_late": [], "mean": 0.5,
+    "a_cut": ([("act", 64)] * 3 + [("act", 32)],) * 2,
+    "act": ("vr", "sf", "P", "penT"),
+    "xa": 1024,
+}
+
+OPT.update(four=True, fused=2, fused_abs=0, halves=[0, 2, 4], via_act=(9, 11, 13, 15), own=("abs", "abs"),
+           a_cut=([("act", 64)] * 3 + [("act", 32)], [("act", 64)] * 2 + [("act", 32)]), eq_late=[1], eq_bank=(5, 7),
+           banks4=(0, 1, 5), banks2=(0, 1, 2, 3), split_p=True)
 
 SCRATCH = {}
 SPEC = {}
@@ -19,7 +32,10 @@ SPEC = {}
 def _decl(where, dtype, spec):
     pool, at = "pool_" + dtype, 0
     for name, cols in spec.items():
-        if where == "sbuf" and cols <= 64:
+        if isinstance(cols, tuple):
+            SPEC[name] = (where, [128] + list(cols), dtype, name, 0)
+            SCRATCH[name] = (where, [128] + list(cols), dtype)
+        elif where == "sbuf" and cols <= 144:
             SPEC[name] = (where, [128, cols], dtype, pool, at)
             at += (cols + 15) // 16 * 16
         else:
@@ -31,34 +47,39 @@ def _decl(where, dtype, spec):
 
 _decl("psum", "float32", {"ps%d" % k: 512 for k in range(8)})
 _decl("sbuf", "bfloat16", {
-    "X": XW, "XR0": XW, "XR1": XW, "XR2": XW, "XR3": XW, "XR4": XW, "m": 8192, "s": 8192, "a": 7168, "ad": 7168,
-    "W": 3072, "XP": 1024, "b": 1024, "d2": 1024, "ad2": 1024, "rec": 1024, "F1": 1024, "al": 512, "P": 512,
-    "penT": 512, "EQ": 1024, "EQm": 1024, "z0": 512, "z1": 512, "IDb": 128, "NIDb": 128, "BLK": 128, "BD": 18 * 128,
-    "WB": 16, "OBb": 16, "OB256": 16, "OBk": 16, "OBm": 16, "ONES": 128, "BIAS": 256, "BIAS2": 256, "TRI": 128, "st": 16,
-    "ask": 64, "sf": 64, "WS": 32, "wb": 16, "yn": 16, "N64": 128, "I4M": 128, "B4M": 64, "NWIDE": 1024, "SelS": 64, "WIDE": 1024, "OBh": 16, "Bm4": 32, "RB": 256, "t0": 128, "t1": 128, "I2K": 128, "N2K": 128, "EQa": 1024, "xh": 512, "incl": 64, "IDa": 128, "IDc": 128, "JK": 64})
-_decl("sbuf", H, {"N1h": 128, "N2h": 1024, "Th": 1024, "IWh": 192, "PM": 16 * 128,
-                  "vr": 128, "nvr": 128, "Rb": 256})
+    "X": XW, "X0": XW, "XR0": XW, "XR1": XW, "XR2": XW, "XR3": XW, "XR4": XW, "m": 8192, "s": 8192, "a": 7168,
+    "ad": 7168, "W": 3072, "XP": 1024, "b": 1024, "d2": 1024, "ad2": 1024, "rec": 1024, "al": 512, "P": 512,
+    "penT": 512, "EQ": 1024, "EQm": 1024, "EQa": 1024, "z0": 512, "z1": 512, "xh": 1024, "BD": 18 * 128,
+    "WIDE": 1024, "NWIDE": 1024, "rgw": 1024, "BIAS": 128,
+    "IDb": 128, "NIDb": 128, "IDa": 128, "I8K": 128, "I2K": 128, "N2K": 128, "N64": 128, "I4M": 128, "BLK": 128,
+    "ONES": 128, "OBb": 8, "OB256": 8, "OB512": 8, "OBn": 8, "OBk": 8, "OBh": 8, "OBm": 8, "WB": 8, "WW": 143, "wb": 1, "SH": 8 * 144,
+    "SelS": 64, "NSel": 64, "yn": 64, "st": (8, 16), "sf": 128, "nask": 128, "incl": 129, "tq": 64, "RS": 64,
+    "OBW": 143, "OBW2": 143, "NOBW": 143, "FW": 134, "M1W": 136, "M2W": 136, "M3W": 136, "tri": 136})
+_decl("sbuf", H, {"N1h": 128, "N2h": 1024, "Th": 1024, "IWh": 192, "PM": 16 * 128, "vr": 128, "Zs": (4, 72, 2),
+                  "Zh": (4, 72, 2), "NMh": 512, "Rv": 128, "Rs": 128, "DL": 8, "nL": 64, "PL": 64, "u1": 64, "yq": 1,
+                  "hq": 64, "WP": 142, "WS": 16, "N1s": 128, "sum": 1024})
 _decl("sbuf", "float32", {
-    "E": 2048, "IOT": V, "N1f": 128, "N1T": 128, "sc": 512, "NS": 128, "nT": 64, "nmh": 72, "fr": 128, "cn": 128, "lc": 8,
-    "full": 64, "sg": 8, "Af": 8, "NOBf": 8, "OBn": 8, "wsf": 8, "OBs": 8, "dl": 128, "df": 128, "En": 128, "tq": 64, "aM": 128,
-    "Rc": 128, "Rh": 256, "Rv": 128, "Rs": 128, "aD": 128, "k3": 64, "k4": 64, "ld": 8, "vmd": 8, "VM": 128,
-    "thr": 8, "yvf": 8, "wf": 8, "ONE": 192, "IW": 192, "FC": 32, "MC": 24, "E16": 24, "CF": 24,
-    "r128": 128, "rc": 128, "rh": 128, "r4": 128, "rg": 128, "rn": 128, "rd": 128, "MH": 128, "MK": 128, "MD": 128,
-    "M4": 128, "CM": 128, "Bm2": 64, "Bm4f": 32, "OBf": 8, "NM": 128, "DM": 128, "RS": 64, "Sel32": 64})
-_decl("sbuf", "int32", {"E0": V, "vi": 8, "wi": 8, "IC": 24, "ui": 64, "u": 64, "u32": 64, "uw": 64, "h": 64,
-                        "gi": 8, "go": 8, "si": 8, "nm": 8, "Ai": 8, "A7": 8, "wsi": 8})
-_decl("sbuf", "uint16", {"VL": 8, "SL": 8, "LP": 128, "OP": 512, "AL": 448, "BL": 64, "HL": 64, "CL": 64, "LS": 80,
-                         "LI": 120})
+    "E": 2048, "IOT": V, "sc": 512, "NN": 512, "e2": 128, "t2": 128, "k4": 64, "ld": 8, "thr": 1, "acc": 1, "af": 1, "yvf": 8,
+    "wf": 1, "wsf": 5, "wl": 64, "N1f": 128, "e1": 128, "ONE": 192, "IW": 192, "NID32": 128, "FC": 40, "MC": 24, "E16": 24, "CF": 24, "r": 144,
+    "rc": 128, "rg": 128, "r8": 136, "rj": 64, "CM": 128, "OBf": 8, "Sel32": 64, "JK": 64, "C1n": 64, "fa": 134,
+    "m5": 136})
+_decl("sbuf", "int32", {"E0": V, "vi": 8, "wi": 1, "IC": 16, "ui": 64, "u": 64, "u32": 64, "uw": 64, "h": 64,
+                        "gi": 8, "go": 8, "wsi": 3})
+_decl("sbuf", "uint16", {"VL": 8, "SL": 8, "LP": 128, "OP": 512, "AL": 448, "BL": 64, "HL": 64, "CL": 64, "LREP": 8})
 
 ENG = ("pe", "dve", "act", "pool", "sp")
-SEMAPHORES = (["c_" + e for e in ENG[:4]] + ["dma%d" % k for k in range(24)] + ["arr%d" % t for t in range(RO)]
-              + ["snt%d" % t for t in range(RO)])
+SEMAPHORES = (["c_" + e for e in ENG[:4]] + ["dma%d" % k for k in range(24)] + ["arr%d" % k for k in range(11)]
+              + ["snt%d" % k for k in range(11)])
 OP_ = AluOpType
 AF = ActivationFunctionType
 
 
 def A(name, c0=0, c1=None, step=1):
     return ("ap", name, c0, SPEC[name][1][1] if c1 is None else c1, step)
+
+
+def ND(name, *index):
+    return ("nd", name, index)
 
 
 def IND(win, off):
@@ -69,32 +90,44 @@ def HB(name, c0=None, c1=None):
     return ("hbm", name, c0, c1)
 
 
+def columns(x):
+    if x[0] == "nd":
+        shape = SPEC[x[1]][1][1:]
+        return np.arange(int(np.prod(shape))).reshape(shape)[x[2]].reshape(-1)
+    return np.arange(x[2], x[3], x[4])
+
+
 def _n(x):
-    if x[0] == "ind":
-        return 16 * _n(x[2])
-    return len(range(x[2], x[3], x[4]))
+    return 16 * _n(x[2]) if x[0] == "ind" else len(columns(x))
 
 
 def _two(x):
-    return SPEC[x[1]][0] == "sbuf" and SPEC[x[1]][2] in ("bfloat16", "float16", "uint16")
+    return SPEC[x[1]][2] in ("bfloat16", "float16", "uint16")
 
 
 def _spans(x):
-    if not isinstance(x, tuple):
+    if not isinstance(x, tuple) or x[0] == "hbm":
         return []
     if x[0] == "ind":
         return _spans(x[1]) + _spans(x[2])
-    if x[0] == "hbm":
-        return []
-    return [(x[1], x[2], x[2] + (_n(x) - 1) * x[4] + 1)]
+    c = columns(x)
+    return [(x[1], int(c[0]), int(c[-1]) + 1)]
 
 
 def program(CY=0.95, G=1.56, PE=0.48, BW=330.0):
     ops = []
+    piece = [0]
 
-    def add(eng, kind, out, ins, par, ns, hold=None):
-        ops.append({"eng": eng, "kind": kind, "out": out, "ins": ins, "par": par, "ns": ns,
-                    "hold": ns if hold is None else hold})
+    def cut():
+        piece[0] += 1
+
+    def add(eng, kind, out, ins, par, ns, hold=None, acc=None):
+        if eng != "pe":
+            cut()
+        ops.append({"eng": eng, "kind": kind, "out": out, "ins": ins, "par": par, "ns": ns, "acc": acc,
+                    "hold": ns if hold is None else hold, "piece": piece[0]})
+        if eng != "pe":
+            cut()
 
     def vcost(out, ins, rate=None):
         full = [x for x in ins if isinstance(x, tuple)]
@@ -122,13 +155,33 @@ def program(CY=0.95, G=1.56, PE=0.48, BW=330.0):
     def mset(out, c):
         add("dve", "memset", out, [], c, vcost(out, []))
 
-    def act(out, in_, func, bias=0.0, scale=1.0):
+    def act(out, in_, func, bias=0.0, scale=1.0, acc=None):
         ns = (80 + G * CY * _n(out)) if in_[0] == "ind" else 60 + CY * max(64, _n(out))
-        add("act", "act", out, [in_, bias, scale], func, ns)
+        add("act", "act", out, [in_, bias, scale], func, ns, acc=acc)
+
+    def lin(out, in_, scale, bias=0.0):
+        act(out, in_, AF.Identity, bias, scale)
+
+    def over(out, in_, bound, above=True):
+        if out[1] in OPT["act"]:
+            sg = 256.0 if above else -256.0
+            act(out, in_, AF.Sigmoid, -sg * bound, sg)
+        else:
+            ts(out, in_, bound, OP_.is_gt if above else OP_.is_lt)
+
+    def shifted(eng, out, in_, by):
+        if eng == "act":
+            lin(out, in_, 1.0, by)
+        else:
+            ts(out, in_, by, add_)
 
     def mm(out, lhsT, rhs, start=True, stop=True):
         f = 4 if SPEC[rhs[1]][2] == "float32" else 1
         add("pe", "mm", out, [lhsT, rhs], (start, stop), PE * f * max(64, _n(rhs)))
+
+    def mms(out, pairs):
+        for k, (lhsT, rhs) in enumerate(pairs):
+            mm(out, lhsT, rhs, k == 0, k == len(pairs) - 1)
 
     def iota(out, pattern, base, cm):
         add("pool", "iota", out, [], (pattern, base, cm), 160 + 2 * CY * _n(out))
@@ -138,8 +191,9 @@ def program(CY=0.95, G=1.56, PE=0.48, BW=330.0):
 
     ndma = [0]
 
-    def dma(q, out, in_, nbytes):
-        add(q, "dma", out, [in_], "dma%d" % ndma[0], 2000 + nbytes / BW, 60)
+    def dma(q, out, in_, nbytes, accum=False):
+        ins = [in_, out] if accum else [in_]
+        add(q, "dma", out, ins, ("dma%d" % ndma[0], accum), 2000 + nbytes / BW, 1500 if q == "pool" else 60)
         ndma[0] += 1
 
     add_, sub_, mul, mx, mn = OP_.add, OP_.subtract, OP_.mult, OP_.max, OP_.min
@@ -149,18 +203,14 @@ def program(CY=0.95, G=1.56, PE=0.48, BW=330.0):
     dma("sp", A("vi"), HB("v0"), 4096)
     dma("sp", A("E0", 0, 960), HB("e0", 0, 960), 500000)
     dma("act", A("E0", 960, V), HB("e0", 960, V), 1000000)
-    dma("sp", A("X", 0, 2048), HB("x0", 0, 2048), 2000000)
-    dma("act", A("X", 2048, XW), HB("x0", 2048, XW), 2000000)
-    dma("sp", A("wi", 0, 1), HB("wt"), 512)
-
-    def lin(out, in_, scale, bias=0.0):
-        act(out, in_, AF.Identity, bias, scale)
+    dma("sp", A("X0", 0, 2048), HB("x0", 0, 2048), 1500000)
+    dma("act", A("X0", 2048, XW), HB("x0", 2048, XW), 2000000)
+    dma("sp", A("wi"), HB("wt"), 512)
     cp(A("VL"), A("vi"))
 
     iota(A("IC", 0, 1), [[0, 1]], 0, 1)
     cols = {"p": 0}
-    for name, sh, msk in (("k8", 3, 1), ("q4", 2, 3), ("e16", 4, 1), ("c16", 0, 15), ("b1", 0, 1), ("b2", 0, 3),
-                          ("g", 4, 7), ("h1", 1, 63), ("h2", 2, 31), ("j", 0, 7), ("y1", 1, 1), ("y2", 1, 3),
+    for name, sh, msk in (("k8", 3, 1), ("q4", 2, 3), ("e16", 4, 1), ("c16", 0, 15), ("b2", 0, 3), ("g", 4, 7),
                           ("c4", 2, 1)):
         cols[name] = len(cols)
         ts(A("IC", cols[name], cols[name] + 1), A("IC", 0, 1), sh, shr, msk, band)
@@ -176,11 +226,12 @@ def program(CY=0.95, G=1.56, PE=0.48, BW=330.0):
     mset(A("ONE"), 1.0)
     sel(A("IW"), A("ONE"), [[-1, 192]], eq, 32, 1)
     cp(A("IWh"), A("IW"))
-    iota(A("r128"), [[1, 128]], 0, 0)
+    iota(A("r"), [[1, 144]], 0, 0)
     ts(newcol("shift"), col("k8"), 2048.0, mul, -2048.0, add_)
-    ts(A("MC", 0, 2), A("r128", 0, 2), col("k8"), eq)
-    ts(A("MC", 4, 8), A("r128", 0, 4), col("q4"), eq)
-    ts(A("MC", 8, 10), A("r128", 0, 2), col("e16"), eq)
+    ts(A("MC", 0, 2), A("r", 0, 2), col("k8"), eq)
+    ts(A("MC", 4, 8), A("r", 0, 4), col("q4"), eq)
+    ts(A("MC", 8, 10), A("r", 0, 2), col("e16"), eq)
+    low8 = A("MC", 0, 1)
     npm = [0]
 
     def perm(shift, mcol):
@@ -189,423 +240,505 @@ def program(CY=0.95, G=1.56, PE=0.48, BW=330.0):
         ts(o, A("IWh", 32 - shift, 160 - shift), A("MC", mcol, mcol + 1), mul)
         return o
     PK = [[perm(8 * (h - kind), kind) for h in range(2)] for kind in range(2)]
-    Q = [[perm(4 * l2 - 8 - 4 * c, 6 + c) for l2 in range(4)] for c in range(2)]
     R = [[perm(16 * (e - yy), 8 + yy) for yy in range(2)] for e in range(2)]
-    ID32 = A("IW", 32, 160)
-    lin(A("IDb"), ID32, 1.0)
-    lin(A("NIDb"), ID32, -1.0)
-    lin(A("IDa"), ID32, -32.5)
-    lin(A("IDc"), ID32, 1.0 / 8192)
+    Q = [[perm(4 * l2 - 8 - 4 * c, 6 + c) for l2 in range(4)] for c in range(2)]
+    ID32, ID, NID = A("IW", 32, 160), A("IDb"), A("NIDb")
+    for name, scale in (("I2K", 2048.0), ("IDb", 1.0), ("NIDb", -1.0), ("IDa", -65.0), ("I8K", 8192.0),
+                        ("N2K", -2048.0), ("N64", -64.0), ("I4M", 4194304.0)):
+        lin(A(name), ID32, scale)
+    lin(A("ONES"), A("ONE", 0, 128), 1.0)
     sel(A("Sel32"), A("ONE", 0, 64), [[2, 4], [16, 8], [1, 2]], eq, 8, -1)
     lin(A("SelS"), A("Sel32"), 1.0)
+    lin(A("NSel"), A("Sel32"), -1.0)
     iota(A("rg"), [[1, 8], [0, 16]], 0, 0)
     ts(A("BLK"), A("rg"), col("g"), eq)
-    ts(A("OBf"), A("r128", 0, 8), col("g"), eq)
-    OBb = A("OBb", 0, 8)
-    lin(OBb, A("OBf"), 1.0)
-    lin(A("OB256", 0, 8), A("OBf"), 256.0)
-    lin(A("OBh", 0, 8), A("OBf"), 1.0 / 16)
-    cp(A("wf", 0, 1), A("wi", 0, 1))
-    lin(A("WB", 0, 8), A("OBf"), A("wf", 0, 1))
-    lin(A("OBk", 0, 8), A("OBf"), 16384.0)
-    lin(A("ONES"), A("ONE", 0, 128), 1.0)
-    for hf in range(2):
-        lin(A("BIAS", 128 * hf, 128 * hf + 128), A("ONE", 0, 128), 15.0)
-        lin(A("BIAS2", 128 * hf, 128 * hf + 128), A("ONE", 0, 128), -64.0)
-    sel(A("TRI"), A("ONES"), [[1, 128]], OP_.is_gt, 0, -1)
-    ts(A("E16", 0, 17), A("r128", 0, 17), col("c16"), eq)
+    ts(A("OBf"), A("r", 0, 8), col("g"), eq)
+    OBb = A("OBb")
+    for name, scale in (("OBb", 1.0), ("OB256", 256.0), ("OB512", 512.0), ("OBn", -256.0), ("OBk", 16384.0),
+                        ("OBh", 1.0 / 16)):
+        lin(A(name), A("OBf"), scale)
+    cp(A("wf"), A("wi"))
+    mset(ND("st", slice(None)), 0.0)
+    lin(newcol("sfb"), col("k8"), 256 * 2048.0, -256 * (2048.0 + 540.5))
+    ts(A("E16", 0, 17), A("r", 0, 17), col("c16"), eq)
     tt(A("CF", 0, 16), A("E16", 1, 17), A("E16", 0, 16), sub_)
     ts(A("CF", 7, 16, 8), A("E16", 7, 16, 8), -2.0, mul)
     cp(A("CF", 16, 18), A("E16", 0, 9, 8))
     for x in range(18):
-        act(A("BD", 128 * x, 128 * x + 128), A("BLK"), AF.Copy, 0.0, A("CF", x, x + 1))
-    lin(A("OBs"), A("OBf"), 1.0 / 16)
-    for g_ in range(8):
-        lin(A("WIDE", 128 * g_, 128 * g_ + 128), A("ONE", 0, 128), A("OBs", g_, g_ + 1))
-    iota(A("r4"), [[0, 8], [1, 4], [0, 4]], 0, 0)
-    iota(A("rh"), [[0, 8], [1, 2], [0, 8]], 0, 0)
-    iota(A("rc"), [[0, 8], [1, 16]], 0, 0)
-    iota(A("rn"), [[0, 16], [1, 8]], 0, 8)
-    iota(A("rd"), [[0, 16], [508, 2], [0, 4]], 1024, -4)
-    lin(A("N2K"), ID32, -2048.0)
-    lin(A("I2K"), ID32, 2048.0)
-    lin(A("WB", 8, 16), A("WB", 0, 8), -128.0)
-    lin(A("wb", 0, 1), A("wf", 0, 1), 1.0)
-    mm(A(ps[6], 0, 1), A("BLK"), A("wb", 0, 1))
-    cp(A("wsi", 0, 1), A(ps[6], 0, 1))
-    ts(A("wsi", 1, 2), A("wsi", 0, 1), 4032, band)
-    ts(A("wsi", 2, 3), A("wsi", 0, 1), 63, band)
-    cp(A("wsf", 0, 2), A("wsi", 1, 3))
-    for j0 in range(2):
-        for part in range(2):
-            ts(A("WS", 16 * j0 + 8 * part, 16 * j0 + 8 * part + 8), A("OBf"), A("E16", 8 * j0, 8 * j0 + 1), mul,
-               A("wsf", part, part + 1), mul)
+        if x % 3:
+            lin(A("BD", 128 * x, 128 * x + 128), A("BLK"), A("CF", x, x + 1))
+        else:
+            ts(A("BD", 128 * x, 128 * x + 128), A("BLK"), A("CF", x, x + 1), mul)
+    iota(A("rgw"), [[1, 8], [0, 128]], 0, 0)
+    ts(A("WIDE"), A("rgw"), col("g"), eq, 1.0 / 16, mul)
+    ts(A("NWIDE"), A("rgw"), col("g"), eq, -1.0 / 16, mul)
     iota(A("IOT"), [[1, V]], 0, 0)
-    lin(A("t0"), A("BLK"), 256.0)
-    ilo, ihi = min(i for _, i in BY_MIN), max(i for _, i in BY_MIN)
-    for j0 in range(2):
-        sel(A("t1"), A("t0"), [[0, 8], [1, 16]], OP_.is_ge, -(8 * j0 + 7 - ihi), 0)
-        sel(A("RB", 128 * j0, 128 * j0 + 128), A("t1"), [[0, 8], [-1, 16]], OP_.is_ge, 8 * j0 + 7 - ilo, 0)
-    ts(A("M4"), A("r4"), col("b2"), eq)
-    ts(A("Bm4f"), A("r128", 0, 32), col("h2"), eq)
-    lin(A("Bm4"), A("Bm4f"), 1.0)
-    ts(A("MH"), A("rh"), col("b1"), eq)
-    lin(A("MK"), A("MH"), 1024.0)
-    lin(A("nmh", 64, 72), A("ONE", 0, 8), 0.0)
-    LCN = A("LS", 60, 68)
-    lin(newcol("nk8"), col("k8"), -8.0, 8.0)
-    lin(newcol("lcn"), col("k8"), 64.0, col("j"))
-    ts(A("lc"), A("r128", 0, 8), col("nk8"), mul, col("lcn"), add_)
-    ts(LCN, A("lc"), 64.0, mn)
-    lin(A("OBm", 0, 8), A("OBf"), -512.0)
+    lin(A("wb"), A("wf"), 1.0)
+    mm(A(ps[6], 0, 1), A("BLK"), A("wb"))
+    ts(A("wsi", 0, 1), A(ps[6], 0, 1), 2048.0, add_)
+    ts(A("wsf", 1, 2), A(ps[6], 0, 1), -256.0, mul, 2097152.0, add_)
+    ts(A("wsf", 4, 5), A(ps[6], 0, 1), -128.0, mul, 2097152.0, add_)
+    ts(A("wsi", 1, 2), A("wsi", 0, 1), 4095, band)
+    tt(A("wsf", 2, 3), A("E16", 0, 1), A("E16", 8, 9), add_)
+    ts(A("wsf", 3, 4), A("wsi", 1, 2), -2048.0, add_, A("wsf", 2, 3), mul)
+    mset(ND("Zs", slice(None)), 0.0)
+    mset(A("incl", 0, 1), 0.0)
+    iota(A("rc"), [[0, 8], [1, 16]], 0, 0)
     ts(A("CM"), A("rc"), col("c16"), eq)
-    ts(A("Bm2"), A("r128", 0, 64), col("h1"), eq)
-    tt(A("NM"), A("MH"), A("rn"), mul)
-    tt(A("MD"), A("MH"), A("rd"), mul)
-    lin(newcol("dump"), col("p"), 1.0, float(V))
-    lin(A("DM"), A("CM"), col("dump"))
-    lin(newcol("p8"), col("p"), 16384.0)
-    lin(A("JK"), A("rn", 0, 64), -2048.0, col("p8"))
-    act(A("RS"), A("rn", 0, 64), AF.Identity, col("p8"), -2048.0)
-    act(A("RS"), A("RS"), AF.Sign, 0.0, -1.0)
-    lin(newcol("t1"), col("b1"), 8.0, 7.0)
-    lin(newcol("lb"), col("y1"), 128.0, col("t1"))
-    lin(newcol("t2"), col("y2"), 128.0, col("t1"))
-    lin(newcol("lsub"), col("k8"), 16.0, col("t2"))
-    lin(newcol("lns"), col("k8"), 64.0, col("j"))
-    lin(newcol("t3"), col("k8"), 4.0, col("b2"))
-    lin(newcol("lhg"), col("c4"), 32.0, col("t3"))
-    LB, LSUB, LDUP, LREP, LR8, LNS, LH4, LHG = (
-        A("LS", 0, 8), A("LS", 8, 12), A("LS", 16, 24), A("LS", 24, 32), A("LS", 32, 36), A("LS", 40, 48),
-        A("LS", 48, 56), A("LS", 56, 60))
-    ts(LH4, A("r128", 0, 8), 4.0, mul, col("b2"), add_)
-    ts(LHG, A("r128", 0, 4), 8.0, mul, col("lhg"), add_)
-    ts(LB, A("r128", 0, 8), 16.0, mul, col("lb"), add_)
-    ts(LSUB, A("r128", 0, 4), 32.0, mul, col("lsub"), add_)
-    ts(LDUP, A("r128", 0, 8), 8.0, mul, col("j"), add_)
-    cp(LREP, A("r128", 0, 8))
-    ts(LR8, A("r128", 0, 4), 2.0, mul, col("k8"), add_)
-    ts(LNS, A("r128", 0, 8), 8.0, mul, col("lns"), add_)
-    lin(A("thr", 0, 1), A("ONE", 0, 1), 4096.0 + 14.5)
-    lin(A("N64"), ID32, -64.0)
-    lin(A("I4M"), ID32, 4194304.0)
-    lin(A("B4M"), A("ONE", 0, 64), -32768.0)
-    lin(A("NOBf"), A("OBf"), -1.0)
+    cp(A("LREP"), A("r", 0, 8))
+    iota(A("rj"), [[0, 8], [1, 8]], 0, 0)
+    lin(A("JK"), A("rj"), -2048.0, 7 * 2048.0 - 2127 * 16384.0 - 4194304.0)
+    ts(A("RS"), A("rj"), 0.5, OP_.is_gt)
+    mset(A("thr"), 256 * (4096.0 + 14.5))
     lin(newcol("d2k"), col("p"), 1.0, float(V - 2048))
-    lin(A("OBn"), A("OBf"), -1.0 / 16)
-    for g_ in range(8):
-        lin(A("NWIDE", 128 * g_, 128 * g_ + 128), A("ONE", 0, 128), A("OBn", g_, g_ + 1))
-    ts(A("LI"), A("r128", 0, V // 16), 16.0, mul, col("c16"), add_)
-    for k in range(3):
-        act(A("E", 640 * k, 640 * k + 640), IND(A("E0"), A("LI", 40 * k, 40 * k + 40)), AF.Copy)
+    ts(A("nL"), A("r", 0, 64), 16.0, mul, col("c16"), add_)
+    ts(A("DL"), A("nL", 0, 8), float(V), add_)
+    lin(newcol("t0"), col("c4"), 512.0, col("b2"))
+    lin(newcol("t1"), col("k8"), 4.0, col("t0"))
+    lin(newcol("pl"), col("t1"), 1.0, 1024.0)
+    ts(A("PL"), A("r", 0, 64), 8.0, mul, col("pl"), add_)
+    tt(A("C1n"), A("nL"), A("PL"), sub_)
+    lin(newcol("g15"), col("g"), 16.0, 15.0)
+    ts(A("OBW"), A("r", 0, 143), col("g15"), eq)
+    lin(A("WW"), A("OBW"), A("wf"))
+    lin(newcol("t3"), col("g"), 16.0, 14.0)
+    lin(newcol("wp"), col("k8"), 1.0, col("t3"))
+    ts(A("WP"), A("r", 0, 142), col("wp"), eq, A("wsf", 3, 4), mul)
+    for l2 in range(4):
+        ts(A("SH", 144 * l2, 144 * l2 + 132), A("IWh", 28 + 4 * l2, 160 + 4 * l2), A("MC", 4 + l2, 5 + l2), mul)
+    if "relu" in OPT["own"]:
+        lin(A("OBW2"), A("OBW"), 2.0)
+        lin(A("NOBW"), A("OBW"), -1.0)
+    lin(newcol("t2"), col("g"), -16.0, -10.0)
+    lin(newcol("fw"), col("k8"), -1.0, col("t2"))
+    act(A("fa"), A("r", 0, 134), AF.Abs, col("fw"))
+    ts(A("FW"), A("fa"), 4.0, eq)
+    iota(A("r8"), [[1, 17], [0, 8]], 0, 0)
+    lin(newcol("g2"), col("g"), 2.0, 1.0)
+    lin(newcol("nk"), col("k8"), 1.0, -1.0)
+    ts(A("M1W"), A("r8"), col("g2"), eq, col("nk"), mul)
+    sel(A("tri"), A("M1W"), [[1, 136]], OP_.is_gt, -8, -1)
+    ts(A("M3W"), A("IWh", 24, 160), low8, mul)
+    lin(A("m5"), A("M3W"), 512.0)
+    tt(A("M2W"), A("m5"), A("tri"), add_)
+    ts(A("t2"), A("r", 0, 128), 8.0, mul, col("c16"), add_)
+    for q in range(4):
+        ts(A("NN", 128 * q, 128 * q + 128), A("t2"), 1024.0 * q, add_, low8, mul)
+        lin(A("NMh", 128 * q, 128 * q + 128), A("NN", 128 * q, 128 * q + 128), 1.0, col("shift"))
+    sel(A("E", 0, V), A("E0"), [[0, V]], OP_.is_ge, 0, 0)
+    for k in range(4):
+        iota(A("X", 1024 * k, 1024 * k + 1024), [[0, 1024]], 128, 0)
+    dma("pool", A("X"), A("X0"), 2097152, True)
 
-    EW, XWIN = A("E", 0, V), A("X")
-    nscan = [0, 0]
+    def sublist(nodes):
+        shifted(OPT["n1"], A("N1s"), IND(nodes, A("VL")), 0.0)
+        mms(A(ps[7], 448, 512), [(PK[1][h], A("N1s", h, 128, 2)) for h in range(2)])
+        cp(A("LP", 64, 128), A(ps[7], 448, 512))
+
+    XWIN = A("X")
+    nscan, nsend = [0, 0], [0]
     for t in range(RO):
-        blk = 1024 * (t % 4)
+        blk, last, reset = 1024 * (t % 4), t == RO - 1, set()
         XR = "XR%d" % t
-        EW = A("E", 0, V) if t else A("E0")
-        add("pool", "send", None, [XWIN], t, 9000, 1500)
-        add(None, "arrive", A(XR), [], t, 0)
+        EW, XC, up = (A("E", 0, V), XWIN, 128.0) if t else (A("E0"), A("X0"), 0.0)
+        parts = [(t, blk - 1024, blk) if t % 4 else (t, 3072 if t else 0, XW)]
+        if not last:
+            parts += [(t + 1, a, b) for a, b in ((0, blk), (blk + 1024, XW)) if a < b]
+        for k, (to, a, b) in enumerate(parts):
+            par = (to, nsend[0])
+            nsend[0] += 1
+            add("pool", "send2" if k else "send", None, [A("X" if to else "X0", a, b)], par, 3000 + 1.5 * (b - a), 1500)
+            add(None, "arrive", A("XR%d" % to, a, b), [], par, 0)
         dma("sp", A("W", 0, 1024), A("X", blk, blk + 1024), 262144)
-        if t == RO - 1:
-            dma("sp", HB("yx", 1024, XW), A("X", 1024, XW), 786432)
-        ts(A("N1h"), IND(EW, A("VL")), col("shift"), add_)
-        for kind in range(2):
-            for h in range(2):
-                mm(A(ps[7], 64 * kind, 64 * kind + 64), PK[kind][h], A("N1h", h, 128, 2), h == 0, h == 1)
-        cp(A("LP", 64, 128), A(ps[7], 64, 128))
-        ts(A("LP", 0, 64), A(ps[7], 0, 64), 2048.0, add_)
-        ts(A("N2h"), IND(EW, A("LP", 64, 128)), col("shift"), add_)
-        for hf in range(2):
-            act(A("XP", 512 * hf, 512 * hf + 512), IND(XWIN, A("LP", 32 * hf, 32 * hf + 32)), AF.Copy)
-        add("dve", "tr", A("Th"), [A("N2h")], None, vcost(A("Th"), [A("N2h")]))
-        for c in range(2):
-            for i in range(1, 8):
-                for l2 in range(4):
-                    mm(A(ps[c], 32 * (i - 1), 32 * i), Q[c][l2], A("N2h", 8 * l2 + i, 1024, 32), l2 == 0, l2 == 3)
-            cp(A("AL", 224 * c, 224 * c + 224), A(ps[c], 0, 224))
-            for jj in range(4):
-                for yy in range(2):
-                    for e in range(2):
-                        mm(A(ps[2 + c], 64 * jj + yy, 64 * jj + 64, 2), R[e][yy],
-                           A("Th", 16 * e + 4 * c + jj, 1024, 32), e == 0, e == 1)
-                if c == 0 and jj == 0:
-                    ts(A("OP", 0, 64), A(ps[2], 0, 64), 2048.0, add_)
-            ts(A("OP", 256 * c + (0 if c else 64), 256 * c + 256), A(ps[2 + c], 0 if c else 64, 256), 2048.0, add_)
-        act(A("N1f"), IND(EW, A("VL")), AF.Copy)
-        mm(A(ps[7], 128, 256), A("N1f"), ID32)
-        act(A("N1T"), A(ps[7], 128, 256), AF.Copy)
-        cp(A("vr"), IND(A("IOT"), A("VL")))
+        if t == 1:
+            iota(A("X0", 1024, XW), [[0, 3072]], -128, 0)
+        if last:
+            dma("pool", A("X0", 1024, XW), A("X", 1024, XW), 1572864, True)
+            dma("sp", HB("yx", 1024, XW), A("X0", 1024, XW), 786432)
+        shifted("act" if "vr" in OPT["act"] else "dve", A("vr"), IND(A("IOT"), A("VL")), 0.0)
 
-        def same_node(bank):
-            for hf in range(2):
-                mm(A(ps[bank + hf]), A("vr"), A("NWIDE", 512 * hf, 512 * hf + 512), True, False)
+        def same(halves):
+            for hf in halves:
+                o0, o1, bank = 512 * hf, 512 * hf + 512, ps[(OPT["eq_bank"] if t else (5, 7))[hf]]
+                mm(A(bank), A("vr"), A("NWIDE", o0, o1), True, False)
                 for g4 in range(4):
                     g_ = 4 * hf + g4
-                    mm(A(ps[bank + hf], 128 * g4, 128 * g4 + 128), A("WIDE", 128 * g_, 128 * g_ + 128), A("vr"),
-                       False, g4 == 3)
-                o0, o1 = 512 * hf, 512 * hf + 512
-                if hf in EQ_ACT:
-                    act(A("EQa", o0, o1), A(ps[bank + hf]), AF.Abs)
+                    mm(A(bank, 128 * g4, 128 * g4 + 128), A("WIDE", 128 * g_, 128 * g_ + 128), A("vr"), False, g4 == 3)
+                if hf in OPT["eq_act"]:
+                    act(A("EQa", o0, o1), A(bank), AF.Abs)
                     ts(A("EQ", o0, o1), A("EQa", o0, o1), 0.0, eq, 2048.0, mul)
                 else:
-                    ts(A("EQ", o0, o1), A(ps[bank + hf]), 0.0, eq, 2048.0, mul)
+                    ts(A("EQ", o0, o1), A(bank), 0.0, eq, 2048.0, mul)
                 sel(A("EQm", o0, o1), A("EQ", o0, o1), [[0, 4], [1, 128]], OP_.is_gt, 0, -1)
-        if not EQ_LATE:
-            same_node(2)
-        lin(A("nT"), A("rn", 0, 64), 1.0, float(blk))
+        late = OPT["eq_late"] if t else [0, 1]
+        same([hf for hf in range(2) if hf not in late])
+        if OPT["early"]:
+            if t == 0:
+                sublist(EW)
+            shifted(OPT["n1"], A("N1h"), IND(EW, A("VL")), col("shift"))
+            mms(A(ps[7], 384, 448), [(PK[0][h], A("N1h", h, 128, 2)) for h in range(2)])
+            ts(A("LP", 0, 64), A(ps[7], 384, 448), 2048.0, add_)
+            if not last:
+                act(A("N1f"), IND(EW, A("VL")), AF.Copy)
+        else:
+            ts(A("N1h"), IND(EW, A("VL")), col("shift"), add_)
+            mms(A(ps[7], 448, 512), [(PK[1][h], A("N1h", h, 128, 2)) for h in range(2)])
+            mms(A(ps[7], 384, 448), [(A("I2K"), A("ONES", 0, 64))] + [(PK[0][h], A("N1h", h, 128, 2)) for h in range(2)])
+            cp(A("LP"), A(ps[7], 384, 512))
+        for hf in range(2):
+            o0, o1 = 512 * hf, 512 * hf + 512
+            shifted(OPT["n2"][hf], A("N2h", o0, o1), IND(EW, A("LP", 64 + 32 * hf, 96 + 32 * hf)), col("shift"))
+            act(A("XP", o0, o1), IND(XC, A("LP", 32 * hf, 32 * hf + 32)), AF.Copy)
+            add("dve", "tr", A("Th", o0, o1), [A("N2h", o0, o1)], None, vcost(A("Th", o0, o1), [A("N2h", o0, o1)]))
+            if hf == 0:
+                for yy in range(2):
+                    mms(A(ps[2], yy, 32, 2), [(R[e][yy], A("Th", 16 * e, 512, 32)) for e in range(2)])
+                ts(A("OP", 0, 32), A(ps[2], 0, 32), 2048.0, add_)
         for c in range(2):
-            top = 224 - 32 * sum(1 for x in FUSED if x[0] == c)
-            step = 2 * ((top + 7) // 8)
-            for k in range(0, top, step):
-                k1 = min(top, k + step)
-                act(A("a", 3584 * c + 16 * k, 3584 * c + 16 * k1), IND(XWIN, A("AL", 224 * c + k, 224 * c + k1)), AF.Copy)
             for jj in range(4):
-                j = 4 * c + jj
-                for l0, l1 in ([(0, 32), (32, 64)] if j in HALVES else [(0, 64)]):
-                    tt(A("m", 1024 * j + 16 * l0, 1024 * j + 16 * l1), IND(XWIN, A("OP", 64 * j + l0, 64 * j + l1)),
+                lo = 32 if c == 0 and jj == 0 else 0
+                for yy in range(2):
+                    mms(A(ps[2 + c], 64 * jj + lo + yy, 64 * jj + 64, 2),
+                        [(R[e][yy], A("Th", 16 * lo + 16 * e + 4 * c + jj, 1024, 32)) for e in range(2)])
+            lo = 0 if c else 32
+            ts(A("OP", 256 * c + lo, 256 * c + 256), A(ps[2 + c], lo, 256), 2048.0, add_)
+            for i in range(1, 8):
+                mms(A(ps[c], 32 * (i - 1), 32 * i), [(Q[c][l2], A("N2h", 8 * l2 + i, 1024, 32)) for l2 in range(4)])
+                if i == 3:
+                    cut()
+            cp(A("AL", 224 * c, 224 * c + 224), A(ps[c], 0, 224))
+        for pos in range(8):
+            pairs = [(A("N2h", 7 - pos, 1024, 8), A("SelS"))]
+            if pos < 7:
+                pairs.append((A("N2h", 6 - pos, 1024, 8), A("NSel")))
+            mms(A(ps[4], pos, 512, 8), pairs)
+        def subs(c):
+            k = 224 * c
+            for eng, width in OPT["a_cut"][c]:
+                out, src = A("a", 16 * k, 16 * (k + width)), IND(XC, A("AL", k, k + width))
+                act(out, src, AF.Copy) if eng == "act" else cp(out, src)
+                k += width
+
+        def cross(y0, y1):
+            w0, w1, o, n_ = 128 * y0, 128 * y1, 128 * (y0 & 1), y1 - y0
+            for j in range(2 * y0, 2 * y1):
+                for l0, l1 in ([(0, 32), (32, 64)] if j in OPT["halves"] else [(0, 64)]):
+                    tt(A("m", 1024 * j + 16 * l0, 1024 * j + 16 * l1), IND(XC, A("OP", 64 * j + l0, 64 * j + l1)),
                        A("XP", 16 * l0, 16 * l1), mn)
-                o = 128 * (jj >> 1) + 8 * (jj & 1)
+                oj = 128 * (j >> 1 & 1)
                 for i in range(8):
-                    mm(A(ps[5 + c], o + 7 - i, 128 * (jj >> 1) + 128, 16), A("m", 1024 * j + i, 1024 * j + 1024, 8), OBb)
-            w0, w1 = 256 * c, 256 * c + 256
-            mm(A(ps[4], w0, w1), A("ONES"), A("BIAS2"), True, False)
-            for i in range(8):
-                mm(A(ps[4], w0 + 7 - i, w1, 8), A("N2h", i, 1024, 8), A("SelS", 32 * c, 32 * c + 32), False, False)
-            ts(A("al", w0, w1), A(ps[5 + c], 0, 256), 80.0, OP_.is_ge, -8192.0, mul)
-            mm(A(ps[4], w0, w1), A("NIDb"), A("al", w0, w1), False, True)
-            scan(A("sc", w0, w1), A("al", w0, w1), A(ps[4], w0, w1), add_, mx)
-            tt(A("Rb", 128 * c, 128 * c + 128), IND(A("sc", w0, w1), LB), A("M4"), mul)
-            mm(A(ps[7], 320 + 32 * c, 352 + 32 * c), A("Rb", 128 * c, 128 * c + 128), A("Bm4"))
-            cp(A("BL", 32 * c, 32 * c + 32), A(ps[7], 320 + 32 * c, 352 + 32 * c))
-            act(A("b", 512 * c, 512 * c + 512), IND(XWIN, A("BL", 32 * c, 32 * c + 32)), AF.Copy)
-        act(A("NS", 64, 128), IND(A("sc"), LSUB), AF.Copy)
+                    mm(A(ps[5], oj + 8 * (j & 1) + 7 - i, oj + 128, 16), A("m", 1024 * j + i, 1024 * j + 1024, 8), OBb)
+                if j & 1:
+                    w0, w1 = 64 * j - 64, 64 * j + 64
+                    over(A("al", w0, w1), A(ps[5], oj, oj + 128), 16 * up + 79.5, False)
+                    scan(A("sc", w0, w1), A("al", w0, w1), A(ps[4], w0, w1), mul, add_)
+                    ts(ND("Zs", j >> 1, slice(7, 64, 8)), A("sc", w0 + 7, w1, 8), 0.0, mx, V - 1.0, mn)
+                    y, lb = j >> 1, A(ps[5], 256 + 16 * y0, 256 + 16 * y1) if n_ == 1 else A(ps[4], 0, 32)
+                    for x in range(8 // n_):
+                        mm(lb, ND("Zs", y, slice(7 - n_ * x - y + y0, 71 - n_ * x - y + y0)),
+                           A("IDb", x, 128, 8 // n_), y == y0 and x == 0, y == y1 - 1 and x == 8 // n_ - 1)
+            cp(A("BL", 16 * y0, 16 * y1), lb)
+            out, src = A("b", 256 * y0, 256 * y1), IND(XC, A("BL", 16 * y0, 16 * y1))
+            cp(out, src) if y0 in OPT["b_dve"] else act(out, src, AF.Copy)
 
-        def names(c):
-            sb = ps[4]
-            PI = A("W", 1024 + 512 * c, 1536 + 512 * c)
-            q0, q1, o0, o1 = 32 * c, 32 * c + 32, 512 * c, 512 * c + 512
-            for pb, l0, l1 in [(ps[4] if c == 0 else ps[0], 0, 128)]:
-                for jj in range(4):
-                    j = 4 * c + jj
-                    o = A(pb, jj, 4 * (l1 - l0), 4)
-                    mm(o, A("IDb"), A("s", 1024 * j + 8 * l0 + 7, 1024 * j + 8 * l1, 8), True, False)
-                    x = 16 + (j & 1)
-                    mm(o, A("BD", 128 * x, 128 * x + 128), A("penT", 128 * (j >> 1) + l0, 128 * (j >> 1) + l1), False, True)
-                o = A("W", 1024 + o0 + 4 * l0, 1024 + o0 + 4 * l1)
-                act(o, A(pb, 0, 4 * (l1 - l0)), AF.Relu, -128.0)
-            for jj in range(4):
-                j, o = 4 * c + jj, A(ps[5], jj, 32, 4)
-                if c == 0:
-                    mm(o, A("W", 1024 + o0 + jj, 1024 + o1, 4), A("WB", 0, 8))
-                else:
-                    pT = A("penT", 128 * (j >> 1), 128 * (j >> 1) + 128)
-                    mm(o, A("ONES"), A("WB", 8, 16), True, False)
-                    mm(o, pT, A("WS", 16 * (j & 1), 16 * (j & 1) + 8), False, False)
-                    mm(o, pT, A("WS", 16 * (j & 1) + 8, 16 * (j & 1) + 16), False, False)
-                    mm(o, A("s", 1024 * j + 7, 1024 * j + 1024, 8), A("WB", 0, 8), False, True)
-            cp(A("ui", q0, q1), A(ps[5], 0, 32))
-            ts(A("u", q0, q1), A("ui", q0, q1), 4095, band)
-            ts(A("u32", q0, q1), A("u", q0, q1), 32.0, add_)
-            tt(A("uw", q0, q1), A("u", q0, q1), A("u32", q0, q1), mul)
-            ts(A("h", q0, q1), A("uw", q0, q1), 5, shr, 4095, band)
-            tt(A("Rh", 128 * c, 128 * c + 128), IND(A("h", q0, q1), LH4), A("M4"), mul)
-            mm(A(ps[5], 32, 64), A("Rh", 128 * c, 128 * c + 128), A("Bm4f"))
-            cp(A("HL", q0, q1), A(ps[5], 32, 64))
-            if c in OWN_ACT:
-                act(A("xh"), IND(XWIN, A("HL", q0, q1)), AF.Copy)
-                mm(A(sb), A("NIDb"), PI, True, False)
-                mm(A(sb), A("IDb"), A("xh"), False, True)
-                act(A("ad2", o0, o1), A(sb), AF.Abs)
-            else:
-                for k in range(2):
-                    o = o0 + 256 * k
-                    tt(A("d2", o, o + 256), IND(XWIN, A("HL", q0 + 16 * k, q0 + 16 * k + 16)),
-                       A("W", 1024 + o, 1280 + o), sub_)
-                    act(A("ad2", o, o + 256), A("d2", o, o + 256), AF.Abs)
-            act(A("rec", o0, o1), IND(A(XR), A("HL", q0, q1)), AF.Copy)
-            mm(A(sb), A("IDb"), PI, True, False)
-            mm(A(sb), A("IDb"), A("rec", o0, o1), False, True)
-            act(A("F1", o0, o1), A(sb), AF.Identity, 127.75, 0.5)
-            act(A("W", 2048 + o0, 2048 + o1), A("F1", o0, o1), AF.Identity, -128.0)
-
-        for c in range(2):
-            w0, w1 = 256 * c, 256 * c + 256
-            mm(A(ps[5 + c], 256, 512), A("ONES"), A("BIAS"), True, False)
-            mm(A(ps[5 + c], 256, 512), A("IDb"), A("al", w0, w1), False, False)
-            mine = [i for i in range(1, 8) if (c, i) in BY_MIN]
-            rest = [i for i in range(1, 8) if (c, i) not in BY_MIN]
+        def misfits4(c):
+            w0, w1, zb, B = 256 * c, 256 * c + 256, ps[6], A("b", 512 * c, 512 * c + 512)
+            mm(A(zb, 0, 256), A("I8K"), A("al", w0, w1), True, False)
+            mine = list(range(8 - OPT["fused"], 8))
+            rest = list(range(1, 8 - OPT["fused"]))
             turn = []
             while mine or rest:
                 turn += [x.pop(0) for x in (rest, mine) if x]
-            held = ps[4] if c else ps[2]
-            for i in turn:
-                if (c, i) in BY_MIN:
-                    o = 3584 * c + 512 * (i - 1)
-                    for jj in range(4):
-                        oo = 256 + 128 * (jj >> 1)
-                        mm(A(ps[5 + c], oo + 8 * (jj & 1) + 7 - i, oo + 128, 16), A("a", o + jj, o + 512, 4),
-                           A("OB256", 0, 8), False, False)
-            if any((c, i) in BY_MIN for i in turn):
-                mm(A(held), A("IDb"), A("b", 512 * c, 512 * c + 512))
-                for jj in range(4):
-                    oo = 256 + 128 * (jj >> 1)
-                    mm(A(ps[5 + c], oo, oo + 128), A("b", 512 * c + jj, 512 * c + 512, 4),
-                       A("RB", 128 * (jj & 1), 128 * (jj & 1) + 128), False, False)
             nabs = 0
             for i in turn:
                 o = 3584 * c + 512 * (i - 1)
-                terms = [("ad", o, "OB256")]
-                if (c, i) in BY_MIN:
-                    tt(A("ad", o, o + 512), A("a", o, o + 512), A(held), mn)
-                    terms = [("ad", o, "OBm")]
-                elif (c, i) in FUSED:
+                terms = [("ad", "OB256")]
+                cut()
+                if i >= 8 - OPT["fused"]:
                     k = 224 * c + 32 * (i - 1)
-                    tt(A("a", o, o + 512), IND(XWIN, A("AL", k, k + 32)), A("b", 512 * c, 512 * c + 512), sub_)
-                    act(A("ad", o, o + 512), A("a", o, o + 512), AF.Abs)
+                    tt(A("a", o, o + 512), IND(XC, A("AL", k, k + 32)), B, sub_)
+                    if 7 - i < OPT["fused_abs"]:
+                        act(A("ad", o, o + 512), A("a", o, o + 512), AF.Abs)
+                    else:
+                        ts(A("ad", o, o + 512), A("a", o, o + 512), 0.0, mx)
+                        terms = [("a", "OBn"), ("ad", "OB512")]
                 else:
-                    bank = ps[nabs % (2 if c else 4)]
+                    bank = ps[OPT["banks4"][nabs % len(OPT["banks4"])]]
                     nabs += 1
-                    mm(A(bank), A("IDb"), A("a", o, o + 512), True, False)
-                    mm(A(bank), A("NIDb"), A("b", 512 * c, 512 * c + 512), False, True)
+                    mms(A(bank), [(ID, A("a", o, o + 512)), (NID, B)])
                     act(A("ad", o, o + 512), A(bank), AF.Abs)
-                for name, o2, rhs in terms:
+                for name, rhs in terms:
                     for jj in range(4):
-                        oo = 256 + 128 * (jj >> 1)
-                        mm(A(ps[5 + c], oo + 8 * (jj & 1) + 7 - i, oo + 128, 16), A(name, o2 + jj, o2 + 512, 4),
-                           A(rhs, 0, 8), False, i == turn[-1] and jj == 3 and name == "ad")
-            act(A("P", w0, w1), A(ps[5 + c], 256, 512), AF.Sign)
+                        oo = 128 * (jj >> 1)
+                        mm(A(zb, oo + 8 * (jj & 1) + 7 - i, oo + 128, 16), A(name, o + jj, o + 512, 4),
+                           A(rhs), False, i == turn[-1] and jj == 3 and name == "ad")
+            if OPT["split_p"]:
+                for yy in range(2):
+                    act(A("P", w0 + 128 * yy, w0 + 128 * yy + 128), A(zb, 128 * yy, 128 * yy + 128), AF.Sigmoid, -256 * 24.5)
+                for yy in range(2):
+                    o, tb = w0 + 128 * yy, ps[yy]
+                    mms(A(tb, 0, 128), [(A("al", o, o + 128), ID), (A("P", o, o + 128), A("IDa"))])
+                    lin(A("penT", o, o + 128), A(tb, 0, 128), 1.0, 128.0)
+                return
+            act(A("P", w0, w1), A(zb, 0, 256), AF.Sigmoid, -256 * 24.5)
             for yy in range(2):
                 o = w0 + 128 * yy
-                mm(A(ps[5 + c], 128 * yy, 128 * yy + 128), A("al", o, o + 128), A("IDc"), True, False)
-                mm(A(ps[5 + c], 128 * yy, 128 * yy + 128), A("P", o, o + 128), A("IDa"), False, True)
-            act(A("penT", w0, w1), A(ps[5 + c], 0, 256), AF.Identity, 96.5)
-            if c == 1:
-                names(0)
-                if EQ_LATE:
-                    same_node(0)
-            for jj in range(4):
-                j = 4 * c + jj
+                mms(A(zb, 256 + 128 * yy, 384 + 128 * yy), [(A("al", o, o + 128), ID), (A("P", o, o + 128), A("IDa"))])
+            lin(A("penT", w0, w1), A(zb, 256, 512), 1.0, 128.0)
+
+        def misfits(y):
+            w0, w1, zb = 128 * y, 128 * y + 128, ps[6 + (y & 1)]
+            mm(A(zb, 0, 128), A("I8K"), A("al", w0, w1), True, False)
+            for n_, pair in enumerate(OPT["pairs"]):
+                bank, o = ps[OPT["banks2"][(4 * y + n_) % len(OPT["banks2"])] if y < 1 else n_ & 1], 1792 * y + 256 * (pair[0] - 1)
+                both = [(i, j0, A("a", 3584 * (y >> 1) + 512 * (i - 1) + 2 * (y & 1) + j0, 3584 * (y >> 1) + 512 * i, 4),
+                         A("b", 256 * y + j0, 256 * y + 256, 2)) for i in pair for j0 in range(2)]
+                cut()
+                if (y, n_) in OPT["by_min"]:
+                    for j0 in range(2):
+                        mm(A(bank, 128 * j0, 128 * j0 + 128), ID, both[j0][3])
+                    for k, (i, j0, a, b) in enumerate(both):
+                        tt(A("ad", o + 128 * k, o + 128 * k + 128), a, A(bank, 128 * j0, 128 * j0 + 128), mn)
+                    for k, (i, j0, a, b) in enumerate(both):
+                        out = A(zb, 8 * j0 + 7 - i, 128, 16)
+                        mm(out, a, A("OB256"), False, False)
+                        mm(out, b, A("OB256"), False, False)
+                        mm(out, A("ad", o + 128 * k, o + 128 * k + 128), A("OBm"), False, i == 7 and j0 == 1)
+                    continue
+                for k, (i, j0, a, b) in enumerate(both):
+                    mms(A(bank, 128 * k, 128 * k + 128), [(ID, a), (NID, b)])
+                relu = (y, n_) in OPT["relu"]
+                if relu:
+                    ts(A("ad", o, o + 256 * len(pair)), A(bank, 0, 256 * len(pair)), 0.0, mx)
+                else:
+                    act(A("ad", o, o + 256 * len(pair)), A(bank, 0, 256 * len(pair)), AF.Abs)
+                for k, (i, j0, a, b) in enumerate(both):
+                    out = A(zb, 8 * j0 + 7 - i, 128, 16)
+                    if relu:
+                        mm(out, a, A("OBn"), False, False)
+                        mm(out, b, A("OB256"), False, False)
+                    mm(out, A("ad", o + 128 * k, o + 128 * k + 128), A("OB512" if relu else "OB256"), False,
+                       i == 7 and j0 == 1)
+            if "P" in OPT["act"]:
+                act(A("P", w0, w1), A(zb, 0, 128), AF.Sigmoid, -256 * 24.5)
+            else:
+                ts(A("P", w0, w1), A(zb, 0, 128), 256 * 24.5, OP_.is_gt)
+            mms(A(zb, 128, 256), [(A("al", w0, w1), ID), (A("P", w0, w1), A("IDa"))])
+            shifted("act" if "penT" in OPT["act"] else "dve", A("penT", w0, w1), A(zb, 128, 256), 128.0)
+
+        def greatest(y):
+            for j0 in range(2):
                 for hf in range(2):
-                    bank = ps[(2, 3, 1)[nscan[0] % 3]] if c else ps[2 + nscan[0] % 2]
-                    pT = A("penT", 128 * (j >> 1) + 64 * hf, 128 * (j >> 1) + 64 * hf + 64)
-                    for i in range(8):
-                        x = 8 * (j & 1) + 7 - i
+                    bank = ps[(2, 3, 1)[nscan[0] % 3]] if y == 3 or y == 2 and OPT["four"] else ps[2 + nscan[0] % 2]
+                    pT = A("penT", 128 * y + 64 * hf, 128 * y + 64 * hf + 64)
+                    cut()
+                    for i in range(1 if bank in reset else 0, 8):
+                        x = 8 * j0 + 7 - i
                         mm(A(bank, i, 512, 8), A("BD", 128 * x, 128 * x + 128), pT)
-                    o = 1024 * j + 512 * hf
+                    reset.add(bank)
+                    o = 2048 * y + 1024 * j0 + 512 * hf
                     src = A(bank)
-                    if (2 * j + hf) in VIA_ACT:
+                    if (o // 512) in OPT["via_act"]:
                         src = A("z%d" % (nscan[1] % 2))
                         nscan[1] += 1
                         act(src, A(bank), AF.Copy)
                     scan(A("s", o, o + 512), src, A("m", o, o + 512), add_, mx)
                     nscan[0] += 1
-        ST = A("st", 0, 8)
-        for y in range(4):
-            mm(A(ps[7], 384, 392), A("penT", 128 * y, 128 * y + 128), OBb, y == 0, y == 3)
-        lin(A("yn", 0, 8), A(ps[7], 384, 392), 1.0 / 64, 64.4375)
-        for y in range(4):
-            mm(A(ps[7], 416, 424), A("penT", 128 * y, 128 * y + 128), OBb, y == 0, False)
-        mm(A(ps[7], 416, 424), A("N64"), A("yn", 0, 8), False, True)
-        act(A("sg"), A(ps[7], 416, 424), AF.Sign, A("thr", 0, 1))
-        act(ST, A("sg"), AF.Relu)
-        mm(A(ps[7], 392, 400), A("vr"), A("OBh", 0, 8), True, False)
-        mm(A(ps[7], 392, 400), A("N2K"), ST, False, False)
+
+        def pi(c, bank):
+            for j in range(4 * c, 4 * c + 4):
+                y, x = j >> 1, 16 + (j & 1)
+                cut()
+                mms(A(bank, j & 3, 512, 4), [(A("BD", 128 * x, 128 * x + 128), A("penT", 128 * y, 128 * y + 128)),
+                                             (ID, A("s", 1024 * j + 7, 1024 * j + 1024, 8))])
+            lin(A("W", 1024 + 512 * c, 1536 + 512 * c), A(bank), 1.0, -up)
+
+        def hashes(c):
+            q0, q1, hb = 32 * c, 32 * c + 32, ps[4 + c]
+            win = [[A("WW", 15 - 4 * l2 - jj, 143 - 4 * l2 - jj) for l2 in range(4)] for jj in range(4)]
+            if c == 0:
+                mms(A(hb, 0, 32), [(win[jj][l2], A("W", 1024 + 4 * l2 + jj, 1536, 16)) for jj in range(4) for l2 in range(4)])
+            else:
+                pairs = []
+                for y in (2, 3):
+                    pairs += [(A("WP", 14 - 4 * l2 - 2 * (y & 1), 142 - 4 * l2 - 2 * (y & 1)),
+                               A("penT", 128 * y + l2, 128 * y + 128, 4)) for l2 in range(4)]
+                    for j in (2 * y, 2 * y + 1):
+                        pairs += [(win[j & 3][l2], A("s", 1024 * j + 8 * l2 + 7, 1024 * j + 1024, 32)) for l2 in range(4)]
+                for k, (lhsT, rhs) in enumerate(pairs):
+                    if k in (12, 20):
+                        cut()
+                    mm(A(hb, 0, 32), lhsT, rhs, k == 0, k == 23)
+            ts(A("ui", q0, q1), A(hb, 0, 32), A("wsf", 1, 2) if t and c else A("wsf", 4, 5), add_)
+            ts(A("u", q0, q1), A("ui", q0, q1), 4095, band)
+            ts(A("u32", q0, q1), A("u", q0, q1), 32.0, add_)
+            tt(A("uw", q0, q1), A("u", q0, q1), A("u32", q0, q1), mul)
+            ts(A("h", q0, q1), A("uw", q0, q1), 5, shr, 4095, band)
+            cp(A("HL", q0, q1), A("h", q0, q1))
+            ts(A("hq", q0, q1), A("h", q0, q1), -2048.0, add_)
+
+        def known(c):
+            q0, q1, o0, o1, sb = 32 * c, 32 * c + 32, 512 * c, 512 * c + 512, A(ps[4])
+            PI = A("W", 1024 + o0, 1024 + o1)
+            if OPT["own"][c] == "act":
+                act(A("xh", o0, o1), IND(XWIN, A("HL", q0, q1)), AF.Copy)
+                mms(sb, [(NID, PI), (ID, A("xh", o0, o1))])
+                act(A("ad2", o0, o1), sb, AF.Abs)
+            else:
+                for q, o, n_ in ([(q0, o0, 256), (q0 + 16, o0 + 256, 256)] if c else [(q0, o0, 512)]):
+                    tt(A("d2", o, o + n_), IND(XWIN, A("HL", q, q + n_ // 16)), A("W", 1024 + o, 1024 + o + n_), sub_)
+                    if OPT["own"][c] == "abs":
+                        act(A("ad2", o, o + n_), A("d2", o, o + n_), AF.Abs)
+                    else:
+                        ts(A("ad2", o, o + n_), A("d2", o, o + n_), 0.0, mx)
+            if c in OPT["rec_dve"]:
+                tt(A("sum", o0, o1), IND(A(XR), A("HL", q0, q1)), PI, add_)
+                lin(A("W", 2048 + o0, 2048 + o1), A("sum", o0, o1), 0.5, -0.25 if t else 63.75)
+                return
+            lin(A("rec", o0, o1), IND(A(XR), A("HL", q0, q1)), 1.0, 0.0 if t else 128.0)
+            mms(sb, [(ID, PI), (ID, A("rec", o0, o1))])
+            lin(A("W", 2048 + o0, 2048 + o1), sb, 0.5, -0.25)
+
+        subs(0)
+        cross(0, 1)
+        cross(1, 2)
+        misfits(0)
+        subs(1)
+        four = OPT["four"]
+        cross(2, 4 if four else 3)
+        greatest(0)
+        misfits(1)
+        if not four:
+            cross(3, 4)
+        greatest(1)
+        same([hf for hf in late if hf or not four])
+        misfits4(1) if four else misfits(2)
+        same([hf for hf in late if four and not hf])
+        pi(0, ps[4])
+        hashes(0)
+        known(0)
+        greatest(2)
+        if not four:
+            misfits(3)
+        greatest(3)
+        pens = [(A("penT", 128 * y, 128 * y + 128), A("BLK", 0, 128, 2)) for y in range(4)]
+        mms(A(ps[7], 0, 64), pens)
+        lin(A("yn"), A(ps[7], 0, 64), 1.0 / 64, 64.4375)
+        mms(A(ps[7], 128, 192), pens + [(A("N64"), A("yn"))])
+        ST8 = ND("st", slice(None), slice(0, 8))
+        act(ST8, A(ps[7], 128, 192), AF.Sigmoid, A("thr"), 256.0, acc=None if last else A("acc"))
+        mm(A(ps[7], 264, 272), A("vr"), A("OBh"), True, False)
+        mm(A(ps[7], 264, 272), A("N2K"), ND("st", slice(None), 0), False, False)
         for g_ in range(8):
-            mm(A(ps[7], 392 + g_, 393 + g_), A("EQm", 128 * g_, 128 * g_ + 128), A("st", g_, g_ + 1), False, g_ == 7)
-        act(A("ld"), A(ps[7], 392, 400), AF.Relu, col("d2k"), -1.0)
-        tt(A("Rs"), IND(A("ld"), LREP), A("CM"), mul)
-        mm(A(ps[7], 400, 408), A("DM"), A("OBf"), True, False)
-        mm(A(ps[7], 400, 408), A("Rs"), A("NOBf"), False, True)
-        cp(A("SL"), A(ps[7], 400, 408))
-        if t < RO - 1:
-            for g_ in range(8):
-                mm(A(ps[7], 408, 409), A("ONES"), A("st", g_, g_ + 1), g_ == 0, g_ == 7)
-            lin(A("yn", 8, 9), A(ps[7], 408, 409), -0.125, 255.5625)
-            lin(A("Af", 0, 1), A(ps[7], 408, 409), -1.0, 4096.0 + 14.5 + 1024.0)
-            act(A("Af", 1, 2), A("yn", 8, 9), AF.Relu, -128.0)
-            lin(A("thr", 0, 1), A("Af", 1, 2), -8.0, A("Af", 0, 1))
-        names(1)
-        mm(A(ps[2], 0, 64), A("NM"), A("Bm2"), True, False)
+            mm(A(ps[7], 264 + g_, 265 + g_), A("EQm", 128 * g_, 128 * g_ + 128), ND("st", g_, slice(0, 1)), False, g_ == 7)
+        act(A("ld"), A(ps[7], 264, 272), AF.Relu, col("d2k"), -1.0)
+        mms(A(ps[6], 0, 128), [(A("FW", 6 - 2 * y, 134 - 2 * y), A("penT", 128 * y, 128 * y + 128)) for y in range(4)]
+            + [(ND("st", slice(None)), A("I2K"))])
+        act(A("sf"), A(ps[6], 0, 128), AF.Sigmoid, col("sfb"), 256.0)
+        tt(A("Rs"), IND(A("ld"), A("LREP")), A("CM"), mul)
+        mms(A(ps[7], 272, 280), [(NID, A("DL")), (A("Rs"), OBb)])
+        ts(A("SL"), A(ps[7], 272, 280), -1.0, mul)
+        if not last:
+            mm(A(ps[7], 256, 257), A("ONE", 0, 128), A("acc"))
+            lin(A("yq"), A(ps[7], 256, 257), -1.0 / 64, 128 + 1100 - 0.4375)
+            lin(A("af"), A(ps[7], 256, 257), -32.0, 256 * (4096.0 + 14.5 + 1024 + 8800))
+            lin(A("thr"), A("yq"), -2048.0, A("af"))
+        pi(1, ps[0])
+        hashes(1)
+        known(1)
+        mm(A(ps[1], 64, 72), A("N1h"), A("IDb", 8 + t, 128, 16))
+        mm(A(ps[1], 0, 64), ID32, A("JK"), True, False)
+        mm(A(ps[1], 0, 64), A("I4M"), ST8, False, False)
         for j in range(8):
             o = 1024 + 512 * (j >> 2)
-            mm(A(ps[6], j, 64, 8), A("W", o + (j & 3), o + 512, 4), OBb)
-        act(A("full"), A(ps[6], 0, 64), AF.Sign)
-        mm(A(ps[6], 64, 128), A("IDb"), A("JK"), True, False)
-        mm(A(ps[6], 64, 128), ID32, A("NS", 64, 128), False, False)
-        mm(A(ps[6], 64, 128), A("ONES"), A("B4M"), False, False)
-        for j in range(8):
-            o = 1024 + 512 * (j >> 2)
-            mm(A(ps[6], 64 + j, 128, 8), A("W", o + (j & 3), o + 512, 4), A("OBk", 0, 8), False, False)
-        tt(A("sf"), IND(ST, LR8), A("full"), mul)
-        mm(A(ps[6], 64, 128), A("I4M"), A("sf"), False, True)
-        scan(A("k4"), A("RS"), A(ps[6], 64, 128), mul, mx)
-        tt(A("gi"), A("k4", 7, 64, 8), A("N1T", 8 + t, 128, 16), mx)
+            if j == 4:
+                cut()
+            mm(A(ps[1], j, 64, 8), A("W", o + (j & 3), o + 512, 4), A("OBk"), False, False)
+            mm(A(ps[1], j, 64, 8), ID, ND("Zs", j >> 1, slice(7, 64, 8), j & 1), False, j == 7)
+        scan(A("k4"), A("RS"), A(ps[1], 0, 64), mul, mx)
+        tt(A("gi"), A("k4", 7, 64, 8), A(ps[1], 64, 72), mx)
         ts(A("go"), A("gi"), 2047, band)
-        tt(A("Rv"), IND(A("go"), LREP), A("CM"), mul)
-        mm(A(ps[6], 128, 136), A("Rv"), A("OBf"))
-        if t < RO - 1:
-            cp(A("VL"), A(ps[6], 128, 136))
+        tt(A("Rv"), IND(A("go"), A("LREP")), A("CM"), mul)
+        mm(A(ps[1], 72, 80), A("Rv"), OBb)
+        if not last:
+            cp(A("VL"), A(ps[1], 72, 80))
         else:
-            cp(A("yvf"), A(ps[6], 128, 136))
+            cp(A("yvf"), A(ps[1], 72, 80))
             dma("sp", HB("yv"), A("yvf"), 4096)
-        act(A("NS", 0, 64), IND(A("h"), LHG), AF.Copy)
-        tt(A("nmh", 0, 64), A("nT"), A("NS", 0, 64), sub_)
-        tt(A("dl"), IND(A("NS"), LNS), A("N1T"), sub_)
-        tt(A("fr"), IND(A("full"), LDUP), A("dl"), mul)
-        mm(A(ps[7], 0, 128), A("fr"), ID32, True, False)
-        act(A("cn"), IND(A("nmh", 0, 65), LCN), AF.Copy)
-        mm(A(ps[5], 64, 128), A("I2K"), A("sf"), True, False)
+        mm(A(ps[6], 128, 256), NID, A("N1h"), True, False)
+        for y in range(4):
+            mm(A(ps[6], 128, 256), ND("Zs", y, slice(3 - y, 67 - y)), ID, False, False)
+        for c in range(2):
+            for l2 in range(4):
+                mm(A(ps[6], 128 + l2, 256, 4), A("SH", 144 * l2 + 4 - 4 * c, 144 * l2 + 132 - 4 * c),
+                   A("hq", 32 * c, 32 * c + 32), False, c == 1 and l2 == 3)
+            cut()
+        tt(A("e2"), A(ps[6], 128, 256), A("sf"), mul)
+        q = t % 4
+        mms(A(ps[6], 256, 384), [(ID, A("N1h")), (NID, A("NMh", 128 * q, 128 * q + 128)), (ID32, A("e2"))])
+        cut()
+        pairs = [(A("I2K"), A("sf"))]
         for j in range(8):
             o = 512 * (j >> 2)
-            mm(A(ps[5], 64 + j, 128, 8), A("ad2", o + (j & 3), o + 512, 4), OBb, False, j == 7)
-        ts(A("ask"), A(ps[5], 64, 128), 2048.0 + 24.0, OP_.is_gt)
-        tt(A("df"), IND(A("ask"), LDUP), A("cn"), mul)
-        mm(A(ps[7], 0, 128), A("df"), ID32, False, True)
-        tt(A("En"), A("N1f"), A(ps[7], 0, 128), add_)
-        cp(IND(A("E"), A("SL")), A("En"))
-        scan(A("incl"), A("RS"), A("ask"), mul, add_)
-        mm(A(ps[3], 0, 64), A("N2K"), A("ask"), True, False)
-        mm(A(ps[3], 0, 64), A("IDb"), A("incl"), False, False)
-        for j in range(8):
-            mm(A(ps[3], j, 64, 8), A("TRI"), A("incl", 7, 64, 8), False, j == 7)
-        tt(A("aD"), IND(A("ask"), LDUP), A("MD"), mul)
-        mm(A(ps[2], 0, 64), A("aD"), A("Bm2"), False, False)
-        ts(A("tq"), A(ps[3], 0, 64), 256.0 - 2048.0, OP_.is_le)
-        tt(A("Rc"), IND(A("tq"), LDUP), A("MK"), mul)
-        mm(A(ps[2], 0, 64), A("Rc"), A("Bm2"), False, True)
-        cp(A("CL"), A(ps[2], 0, 64))
-        xa = XA if t < RO - 1 else 512
-        act(A("X", blk, blk + xa), IND(A("W"), A("CL", 0, xa // 16)), AF.Copy)
+            if OPT["own"][j >> 2] == "relu":
+                pairs += [(A("NOBW", 15 - j, 143 - j), A("d2", o + (j & 3), o + 512, 4)),
+                          (A("OBW2", 15 - j, 143 - j), A("ad2", o + (j & 3), o + 512, 4))]
+            else:
+                pairs += [(A("OBW", 15 - j, 143 - j), A("ad2", o + (j & 3), o + 512, 4))]
+        pairs.sort(key=lambda x: (x[1][2] >= 512, x[1][1] == "ad2"))
+        half = len(pairs) - 4
+        for k, (lhsT, rhs) in enumerate(pairs):
+            if k == half:
+                cut()
+            mm(A(ps[3], 0, 128), lhsT, rhs, k == 0, k == len(pairs) - 1)
+        over(A("nask"), A(ps[3], 0, 128), 2048.0 + 24.5, False)
+        tt(A("t2"), A(ps[6], 256, 384), A("nask"), mul)
+        tt(IND(A("E"), A("SL")), A("t2"), A("NN", 128 * q, 128 * q + 128), add_)
+        scan(A("incl", 1, 129), A("ONES"), A("nask"), mul, add_)
+        mms(A(ps[2], 0, 64), [(A("M3W", 8 - 8 * l0, 136 - 8 * l0), A("nask", l0, 128, 2)) for l0 in range(2)])
+        cut()
+        mms(A(ps[3], 128, 192), [(ID, A("nL"))]
+            + [(A("M2W", 8 - 8 * l0, 136 - 8 * l0), A("nask", l0, 128, 2)) for l0 in range(2)]
+            + [(A("M1W", 8 - 8 * l0, 136 - 8 * l0), A("incl", l0, 128, 2)) for l0 in range(2)])
+        tt(A("u1"), A(ps[2], 0, 64), A("C1n"), mul)
+        ts(A("tq"), A(ps[3], 128, 192), 255.5, OP_.is_lt, 0.5, mul)
+        mms(A(ps[2], 64, 128), [(ID, A("PL")), (ID, A("u1")), (A("I2K"), A("tq"))])
+        cp(A("CL"), A(ps[2], 64, 128))
+        xa = 512 if last else OPT["xa"]
+        XO = "X0" if last else "X"
+        lin(A(XO, blk, blk + xa), IND(A("W"), A("CL", 0, xa // 16)), 1.0, -128.0 if last else 0.0)
         if xa < 1024:
-            cp(A("X", blk + xa, blk + 1024), IND(A("W"), A("CL", xa // 16, 64)))
+            ts(A(XO, blk + xa, blk + 1024), IND(A("W"), A("CL", xa // 16, 64)), -128.0 if last else 0.0, add_)
     dma("sp", HB("ye", 0, 960), A("E", 0, 960), 1000000)
     dma("sp", HB("ye", 960, V), A("E", 960, V), 1000000)
-    dma("sp", HB("yx", 0, 1024), A("X", 0, 1024), 262144)
-    seen = {}
-    for o in ops:
-        out = o["out"]
-        key = o["eng"] + ":" + (out[1] if out[0] != "ind" else out[1][1] + "!") if out and o["eng"] else "-"
-        if o["kind"] == "send":
-            seen.clear()
-        seen[key] = seen.get(key, 0) + 1
-        o["key"] = "%s#%d" % (key, seen[key])
+    dma("sp", HB("yx", 0, 1024), A("X0", 0, 1024), 262144)
     return ops
 
 
-def dependencies(ops):
-    seen = {}
-    for k, o in enumerate(ops):
-        hard, soft = set(), set()
+ASYNC = ("dma", "send", "send2", "arrive")
+
+
+def dependencies(flat):
+    ops, seen = [], {}
+    for o in flat:
+        if ops and ops[-1]["piece"] == o["piece"]:
+            p = ops[-1]
+            p["calls"].append(o)
+            p["ns"] += o["ns"]
+            p["hold"] += o["hold"]
+        else:
+            p = dict(o, calls=[o], hard=set(), soft=set())
+            ops.append(p)
+        k = len(ops) - 1
         reads = [s for x in o["ins"] for s in _spans(x)]
-        writes = []
+        writes = _spans(o["acc"])
+        whole = True
         if o["out"] is not None:
             if o["out"][0] == "ind":
-                writes, reads = _spans(o["out"][1]), reads + _spans(o["out"][2])
+                writes, reads = writes + _spans(o["out"][1]), reads + _spans(o["out"][2])
             else:
-                writes = _spans(o["out"])
-        asyn = o["kind"] in ("dma", "send", "arrive")
+                writes = writes + _spans(o["out"])
+                whole = o["out"][0] == "ap" and o["out"][4] == 1
         for isw, group in ((False, reads), (True, writes)):
             for name, lo, hi in group:
                 psum = SPEC[name][0] == "psum"
@@ -615,101 +748,39 @@ def dependencies(ops):
                     if k2 == k:
                         keep.append(rec)
                         continue
-                    o2 = ops[k2]
-                    same = o2["eng"] == o["eng"] and not asyn and o2["kind"] not in ("dma", "send", "arrive")
-                    over = lo < hi2 and lo2 < hi
-                    if psum and not same:
-                        hard.add(k2)
-                        continue
+                    same = ops[k2]["eng"] == o["eng"] and o["kind"] not in ASYNC and ops[k2]["kind"] not in ASYNC
                     if psum:
-                        soft.add(k2)
+                        p["soft" if same else "hard"].add(k2)
                         continue
-                    if over and (isw or w2):
-                        hard.add(k2)
-                        if isw and lo <= lo2 and hi2 <= hi and (not same or o["out"][0] == "ind" or o["out"][0] == "ap" and o["out"][4] == 1):
+                    if lo < hi2 and lo2 < hi and (isw or w2):
+                        p["hard"].add(k2)
+                        if isw and lo <= lo2 and hi2 <= hi and (whole or not same):
                             continue
                     keep.append(rec)
-                keep.append((k, isw, lo, hi))
+                if (k, isw, lo, hi) not in keep:
+                    keep.append((k, isw, lo, hi))
                 seen[name] = keep
-        o["hard"], o["soft"] = hard, soft - hard
-    send = {o["par"]: k for k, o in enumerate(ops) if o["kind"] == "send"}
+    send = {o["par"]: k for k, o in enumerate(ops) if o["kind"] in ("send", "send2")}
+    count = {}
     for o in ops:
+        o["soft"] -= o["hard"]
         o["time"] = set([send[o["par"]]]) if o["kind"] == "arrive" else set()
+        out = o["out"]
+        key = o["eng"] + ":" + (out[1] if out[0] != "ind" else out[1][1] + "!") if out and o["eng"] else "-"
+        key = {"act:X0": "act:X", "dve:yvf": "dve:VL"}.get(key, key)
+        if o["kind"] == "send":
+            count.clear()
+        count[key] = count.get(key, 0) + 1
+        o["key"] = "%s#%d" % (key, count[key])
+    return ops
 
 
-def schedule(ops):
-    n = len(ops)
-    LX, LS_ = LAG
-    after = [[] for _ in range(n)]
-    for k, o in enumerate(ops):
-        for d in o["hard"] | o["soft"] | o["time"]:
-            after[d].append(k)
-    rank = [0.0] * n
-    for k in range(n - 1, -1, -1):
-        rank[k] = ops[k]["ns"] + max([rank[x] + (LX if k in ops[x]["hard"] else 0.0) for x in after[k]] + [0.0])
-    left = [len(o["hard"] | o["soft"] | o["time"]) for o in ops]
-    ready_at = [0.0] * n
-    free = {e: 0.0 for e in ENG}
-    pool = {e: [] for e in ENG}
-    order = {e: [] for e in ENG}
-    start = [0.0] * n
-
-    def finish(k):
-        todo = [k]
-        while todo:
-            q = todo.pop()
-            for x in after[q]:
-                if q in ops[x]["soft"]:
-                    at = start[q] + ops[q]["hold"]
-                else:
-                    at = start[q] + ops[q]["ns"] + (LS_ if ops[q]["eng"] == ops[x]["eng"] else LX)
-                ready_at[x] = max(ready_at[x], at)
-                left[x] -= 1
-                if left[x] == 0:
-                    if ops[x]["eng"] is None:
-                        start[x] = ready_at[x]
-                        todo.append(x)
-                    else:
-                        pool[ops[x]["eng"]].append(x)
-    for k in range(n):
-        if left[k] == 0:
-            pool[ops[k]["eng"]].append(k)
-    while any(pool.values()):
-        best = None
-        for e in ENG:
-            if pool[e]:
-                at = max(free[e], min(ready_at[x] for x in pool[e]))
-                if best is None or at < best[0]:
-                    best = (at, e)
-        at, e = best
-        cand = [x for x in pool[e] if ready_at[x] <= at + 60.0]
-        k = max(cand, key=lambda x: (ops[x]["ns"] < 1000 and ops[x]["key"][4:6] not in ("EQ", "s#"), rank[x], -x))
-        pool[e].remove(k)
-        start[k] = max(at, ready_at[k])
-        free[e] = start[k] + ops[k]["hold"]
-        order[e].append(k)
-        finish(k)
-    return order, start
-
-
-HINT = {}
-for _e, _text in (
-        ("dve", "OP#1 .6 m#1 .9 AL#1 1.7 OP#2 1.75 m#2 1.9 m#3 2.8 AL#2 3.4 OP#3 3.5 m#4 4.5 m#5 6.2 al#1 8.5 m#6 8.9 sc#1 9.0 "
-                "Rb#1 9.3 m#7 9.9 BL#1 9.8 m#8 11 m#9 12 m#10 13 m#11 14.6 al#2 16.4 sc#2 17 Rb#2 17.3 BL#2 17.7 s#1 18 "
-                "s#2 18.6 s#3 19.2 a#1 19.3 a#2 19.5 ad#1 19.7 ad#2 20.3 ad#3 20.9 ad#4 21.2 s#4 21.5 s#5 22 s#6 22.6 s#7 23.2 s#8 23.8"),
-        ("act", "a#1 1.7 a#2 3.2 a#3 4.7 a#4 6.2 a#5 7.7 a#6 9.2 b#1 10.7 ad#1 11.6 ad#2 12.2 ad#3 12.8 ad#4 13.4 ad#5 14 "
-                "ad#6 14.6 ad#7 15.2 P#1 15.9 a#7 16.2 penT#1 16.1 b#2 17.8 a#8 18.7 ad#8 20.2 ad#9 20.8 ad#10 21.4 "
-                "ad#11 22 P#2 22.7 penT#2 23.2")):
-    _w = _text.split()
-    for _i in range(0, len(_w), 2):
-        HINT[_e + ":" + _w[_i]] = float(_w[_i + 1])
-
-
-def improve(ops, start, steps, seed=1):
+def schedule(ops, first, start, units, steps, slack, rng):
     n = len(ops)
     hold, ns, eng = [o["hold"] for o in ops], [o["ns"] for o in ops], [o["eng"] for o in ops]
-    pred = [[(d, hold[d]) for d in o["soft"]]
-            + [(d, ns[d] + (LAG[1] if eng[d] == o["eng"] else LAG[0])) for d in o["hard"] | o["time"]] for o in ops]
+    pred = [[(d - first, hold[d - first]) for d in o["soft"] if d >= first]
+            + [(d - first, ns[d - first] + (LAG[1] if eng[d - first] == o["eng"] else LAG[0]))
+               for d in o["hard"] | o["time"] if d >= first] for o in ops]
     back = [[] for _ in ops]
     for k in range(n):
         for d, lag in pred[k]:
@@ -730,18 +801,22 @@ def improve(ops, start, steps, seed=1):
                     at = st[d] + lag
             if eng[k] is not None:
                 lo, hi = busy[eng[k]]
-                a, b = 0, len(hi)
-                while a < b:
-                    mid = (a + b) // 2
-                    if hi[mid] <= at:
-                        a = mid + 1
-                    else:
-                        b = mid
-                while a < len(lo) and lo[a] < at + hold[k]:
-                    at = hi[a]
-                    a += 1
-                lo.insert(a, at)
-                hi.insert(a, at + hold[k])
+                if hi and hi[-1] > at:
+                    a, b = 0, len(hi)
+                    while a < b:
+                        mid = (a + b) // 2
+                        if hi[mid] <= at:
+                            a = mid + 1
+                        else:
+                            b = mid
+                    while a < len(lo) and lo[a] < at + hold[k]:
+                        at = hi[a]
+                        a += 1
+                    lo.insert(a, at)
+                    hi.insert(a, at + hold[k])
+                else:
+                    lo.append(at)
+                    hi.append(at + hold[k])
             st[k] = at
         return st
     zero, tail = [0.0] * n, [ns[k] - hold[k] for k in range(n)]
@@ -751,66 +826,196 @@ def improve(ops, start, steps, seed=1):
         return place([-(r[k] + hold[k]) for k in range(n)], pred, zero, True)
 
     def span(st):
-        return max(st[k] + ns[k] for k in range(n))
-    groups = {}
-    for k, o in enumerate(ops):
-        if eng[k] in ("dve", "act"):
-            groups.setdefault(o["key"], []).append(k)
-    names = sorted(x for x in groups if len(groups[x]) > 1)
-    second = [k for k, o in enumerate(ops) if o["kind"] == "send"][1]
-    early = [k for k in range(second) if eng[k] in ("dve", "act", "pool")]
-    rng = np.random.default_rng(seed)
-    cur = justify(start)
-    for _ in range(3):
-        key, base = list(cur), 0.0
-        for k, o in enumerate(ops):
-            if o["key"] == "dve:Th#1":
-                base = cur[k]
-            if o["key"] in HINT:
-                key[k] = base + 1000.0 * HINT[o["key"]]
-        first = min(k for k, o in enumerate(ops) if o["kind"] == "send")
-        for k in range(first):
-            key[k] = 1e9
-            name = ops[k]["key"].split("#")[0]
-            if name in ("dve:BLK", "dve:E16", "dve:CF", "dve:OBf") or (eng[k] == "pool" and name != "pool:IOT"):
-                key[k] = 1000.0 + k
-        for k in range(n - 1, -1, -1):
-            for d, lag in pred[k]:
-                if key[d] > key[k] - lag and (key[k] < cur[k] or d < first or k < first + 140):
-                    key[d] = key[k] - lag
-        cur = place(key, pred, zero, True)
+        return max(st[k] + ns[k] for k in range(n)) + OPT["mean"] * sum(st) / n
+    cur = place(start, pred, zero, True)
     best, cost = cur, span(cur)
     low = cost
+    shifts = (rng.choice([-1.0, 1.0], (steps, 2)) * np.exp(rng.uniform(5.0, 8.7, (steps, 2)))).tolist()
+    picks = rng.integers(len(units), size=(steps, 2)).tolist()
+    unit = {}
+    for u in units:
+        for k in u:
+            unit.setdefault(k, u)
+
+    def queued(st):
+        ends = {(eng[k], round(st[k] + hold[k], 2)): k for k in range(n)}
+        k, pairs = max(range(n), key=lambda q: st[q] + ns[q]), []
+        while k is not None:
+            u = [d for d, lag in pred[k] if st[d] + lag > st[k] - 0.01]
+            v, k = k, u[0] if u else ends.get((eng[k], round(st[k], 2)))
+            if not u and k in unit and v in unit:
+                pairs.append((k, v))
+        return pairs
+    pairs = queued(cur)
     for it in range(steps):
         key = list(cur)
-        for _ in range(int(rng.integers(1, 3))):
-            shift = float(rng.choice([-1.0, 1.0]) * np.exp(rng.uniform(5.0, 9.0)))
-            if rng.random() < 0.35:
-                key[early[int(rng.integers(len(early)))]] += shift
-                continue
-            for k in groups[names[int(rng.integers(len(names)))]]:
-                key[k] += shift
+        if it % 3 and pairs:
+            u, v = pairs[picks[it][0] % len(pairs)]
+            far = abs(shifts[it][0]) if shifts[it][1] > 0 else 1.0
+            for k in unit[v] if it % 3 == 1 else unit[u]:
+                key[k] += cur[u] - cur[v] - far if it % 3 == 1 else cur[v] - cur[u] + far
+        else:
+            for k in units[picks[it][1]]:
+                key[k] += shifts[it][1]
         for k in range(n - 1, -1, -1):
-            for d, lag in pred[k]:
-                if key[d] > key[k] - lag and key[k] < cur[k]:
-                    key[d] = key[k] - lag
+            if key[k] < cur[k]:
+                for d, lag in pred[k]:
+                    if key[d] > key[k] - lag:
+                        key[d] = key[k] - lag
         st = place(key, pred, zero, True)
-        if it % 4 == 0:
+        if it % 5 == 0:
             st = justify(st)
         c = span(st)
-        if c <= cost + 400.0 * (1.0 - it / steps):
-            cur, cost = st, c
+        if c <= cost + slack * (1.0 - it / steps):
+            cur, cost, pairs = st, c, queued(st)
             if c < low:
                 best, low = st, c
-    order = {e: sorted((k for k in range(n) if eng[k] == e), key=lambda q: (best[q], q)) for e in ENG}
-    return order, best
+    return best
 
 
-def plan(steps=3500, seed=3):
-    ops = program()
-    dependencies(ops)
-    order, start = schedule(ops)
-    order, start = improve(ops, start, steps, seed)
+ORDER = {
+    "dve": "N1h LP EQ N2h Th OP EQ Th OP AL m m m AL m OP m m sc Zs m BL m m m m sc Zs BL s s a ad s s a ad s s s s "
+           "ui u u32 uw h Zh HL s s s s Rs s s SL s s ui u u32 uw h Zh k4 HL gi d2 d2 go e2 Rv nask VL incl t2 E! u1 "
+           "tq CL",
+    "act": "vr N2h XP XP a a a a al a b ad ad ad ad ad ad ad al P a penT b a ad ad ad ad ad P W penT yn xh st ad2 ld "
+           "sf W rec ad2 ad2 rec W W yq thr X"}
+
+
+def first_keys(ops, lo, edge):
+    key = {}
+    for t, (a, b) in enumerate(zip(edge[:-1], edge[1:])):
+        at = {ops[k]["key"]: k for k in range(a, b)}
+        for e, text in ORDER.items():
+            time, seen = 36000.0 * t, {}
+            for w in text.split():
+                seen[w] = seen.get(w, 0) + 1
+                k = at.get("%s:%s#%d" % (e, w, seen[w]))
+                if k is not None:
+                    key[k] = time
+                    time += ops[k]["ns"] * 1.1
+    out = [key.get(k, 1e9) for k in range(lo, edge[-1])]
+    for k in range(edge[-1] - 1, lo - 1, -1):
+        for d in ops[k]["hard"] | ops[k]["soft"] | ops[k]["time"]:
+            if d >= lo and d not in key:
+                out[d - lo] = min(out[d - lo], out[k - lo] - ops[d]["ns"])
+    return out
+
+
+def searched(steps=STEPS, seed=SEED):
+    ops = dependencies(program())
+    rng = np.random.default_rng(seed)
+    n = len(ops)
+    edge = [k for k, o in enumerate(ops) if o["kind"] == "send"] + [n]
+
+    def alike(lo, hi):
+        groups = {}
+        for k in range(lo, hi):
+            if ops[k]["eng"] in ("dve", "act", "pe"):
+                groups.setdefault(ops[k]["key"], []).append(k - lo)
+        return [groups[x] for x in sorted(groups)]
+    lo, mid, hi = edge[1:4]
+    two = schedule(ops[lo:hi], lo, first_keys(ops, lo, edge[1:4]), alike(lo, hi), steps[0], 250.0, rng)
+    at = [{ops[k]["key"]: two[k - lo] for k in range(a, b)} for a, b in ((lo, mid), (mid, hi))]
+    period = at[1]["dve:sc#2"] - at[0]["dve:sc#2"]
+    start = [float(k) for k in range(n)]
+    for t in range(RO):
+        for k in range(edge[t], edge[t + 1]):
+            x = ops[k]["key"]
+            late = at[0].get(x, 0.0) > at[0]["dve:sc#2"]
+            start[k] = 10000.0 + t * period + (at[0][x] if late else at[1].get(x, at[1]["dve:N1h#1"]) - period)
+    for k in range(edge[0] - 1, -1, -1):
+        start[k] = min([start[x] - 500.0 for x in range(k + 1, n) if k in ops[x]["hard"]] + [start[edge[1]]])
+    ends = [[k] for k in list(range(edge[1])) + list(range(edge[4], n)) if ops[k]["eng"] in ("dve", "act", "pe", "pool")]
+    start = schedule(ops, 0, start, ends + alike(edge[0], n), steps[1], 200.0, rng)
+    order = {e: sorted((k for k in range(n) if ops[k]["eng"] == e), key=lambda q: (start[q], q)) for e in ENG}
+    return order
+
+
+ROUND = {
+    "dve": "N1h#1 tq#1' LP#1 N2h#1 CL#1' Th#1 Th#2 OP#1 AL#1 EQ#1 OP#3 OP#2 m#1 m#2 m#3 m#5 al#1 sc#1 AL#2 Zs#1 m#4 BL#1 m#6 m#8 al#2 sc#2 Zs#2 m#7 BL#2 m#9 m#10 al#3 m#11 sc#3 Zs#3 s#1 al#4 sc#4 Zs#4 s#2 BL#3 s#3 s#4 a#1 a#2 s#5 ad#2 ad#1 s#6 s#7 EQ#2 s#8 s#9 s#11 ui#1 s#10 u#1 s#13 u32#1 s#12 uw#1 s#14 h#1 s#15 HL#1 s#16 d2#1 ui#2 hq#1 u#2 u32#2 uw#2 h#2 HL#2 hq#2 d2#2 d2#3 k4#1 Rs#1 gi#1 e2#1 go#1 SL#1 Rv#1 nask#1 incl#1 t2#1 VL#1 E!#1 u1#1",
+    "act": "vr#1 N2h#1 X#1' XP#1 XP#2 a#2 a#3 a#4 thr#1' a#1 b#1 a#6 ad#1 ad#2 ad#3 b#2 ad#4 P#1 ad#5 ad#6 penT#1 ad#7 ad#8 P#2 a#5 penT#2 b#3 a#7 ad#9 ad#10 ad#11 ad#12 ad#13 P#3 P#4 penT#3 penT#4 W#1 yn#1 z0#1 z1#1 z0#2 st#1 z1#2 W#3 sf#1 ad2#1 rec#1 ld#1 ad2#2 ad2#3 rec#2 W#2 yq#1 af#1 W#4"}
+ANCHOR = ("dve:m#1", "act:XP#2")
+LOOSE = ("act:vr#1", "dve:EQ#1", "dve:EQ#2")
+PERIOD, START, LOOK = 40000.0, 10000.0, 120.0
+
+
+def arrange(ops, rounds=None):
+    n = len(ops)
+    edge = [k for k, o in enumerate(ops) if o["kind"] == "send"] + [n]
+    at = [{ops[k]["key"]: k for k in range(a, b)} for a, b in zip(edge[:-1], edge[1:])]
+    after = [[] for _ in ops]
+    left = [0] * n
+    for k, o in enumerate(ops):
+        for d in o["hard"] | o["soft"] | o["time"]:
+            p = ops[d]
+            lag = 0.0 if p["eng"] is None else LAG[1] if p["eng"] == o["eng"] else LAG[0]
+            after[d].append((k, p["hold"] if d in o["soft"] else p["ns"] + lag))
+            left[k] += 1
+    due, fixed = [None] * n, {e: [] for e in ENG}
+    for e, text in (rounds or ROUND).items():
+        names = [(e + ":" + w.rstrip("'"), w.count("'")) for w in text.split()]
+        size = [ops[at[2][x]]["hold"] for x, _ in names]
+        off = np.concatenate([[0.0], np.cumsum(size)]) * PERIOD / sum(size)
+        zero = [off[i] + PERIOD * back for i, (x, back) in enumerate(names) if x in ANCHOR][0]
+        for t in range(RO + 1):
+            for i, (x, back) in enumerate(names):
+                if 0 <= t - back < RO and x in at[t - back] and (t or x not in LOOSE):
+                    k = at[t - back][x]
+                    fixed[e].append(k)
+                    due[k] = START + PERIOD * t + float(off[i]) - zero
+    listed = set(k for e in ENG for k in fixed[e])
+    for k in range(n - 1, -1, -1):
+        if due[k] is None:
+            due[k] = min([due[x] - w for x, w in after[k]] + [START + PERIOD * RO])
+    turn = [due[k] + (0.0 if ops[k]["eng"] == "pe" else ops[k]["ns"]) for k in range(n)]
+    for k in range(n):
+        if ops[k]["eng"] == "pool" and (ops[k]["ns"] < 700 or ops[k]["kind"] == "send"):
+            turn[k] = due[k] / 100
+    ready, start = [0.0] * n, [0.0] * n
+    free, head = {e: 0.0 for e in ENG}, {e: 0 for e in ENG}
+    pool, order = {e: [] for e in ENG}, {e: [] for e in ENG}
+
+    def release(k):
+        for x, w in after[k]:
+            ready[x] = max(ready[x], start[k] + w)
+            left[x] -= 1
+            if left[x] == 0 and ops[x]["eng"] is None:
+                start[x] = ready[x]
+                release(x)
+            elif left[x] == 0 and x not in listed:
+                pool[ops[x]["eng"]].append(x)
+    for k in range(n):
+        if left[k] == 0 and k not in listed:
+            pool[ops[k]["eng"]].append(k)
+    while True:
+        best = None
+        for e in ENG:
+            h = fixed[e][head[e]] if head[e] < len(fixed[e]) else None
+            pick = h if h is not None and left[h] == 0 else None
+            if pool[e]:
+                soon = max(free[e], min(ready[x] for x in pool[e])) + LOOK
+                d = min((x for x in pool[e] if ready[x] <= soon), key=lambda x: (turn[x], x))
+                if pick is None or due[d] < due[h] or max(free[e], ready[d]) + ops[d]["hold"] <= max(free[e], ready[h]) + 60:
+                    pick = d
+            if pick is not None and (best is None or max(free[e], ready[pick]) < best[0]):
+                best = (max(free[e], ready[pick]), e, pick)
+        if best is None:
+            break
+        time, e, k = best
+        if k in listed:
+            head[e] += 1
+        else:
+            pool[e].remove(k)
+        start[k], free[e] = time, time + ops[k]["hold"]
+        order[e].append(k)
+        release(k)
+    assert sum(len(x) for x in order.values()) == sum(1 for o in ops if o["eng"])
+    return order, start
+
+
+def plan():
+    ops = dependencies(program())
+    order, start = arrange(ops)
     pos = {}
     for e in ENG:
         for i, k in enumerate(order[e]):
@@ -824,7 +1029,7 @@ def plan(steps=3500, seed=3):
         waits = []
         for d in sorted(o["hard"], key=lambda d: -start[d]):
             od = ops[d]
-            if od["kind"] in ("dma", "send", "arrive"):
+            if od["kind"] in ASYNC:
                 if ("x", d) not in kn:
                     waits.append(d)
                     kn[("x", d)] = 1
@@ -842,7 +1047,7 @@ def plan(steps=3500, seed=3):
     for e in ENG:
         c = 0
         for k in order[e]:
-            if k in needed and ops[k]["kind"] not in ("dma", "send"):
+            if k in needed and ops[k]["kind"] not in ASYNC:
                 c += 1
                 count[k] = c
     return ops, order, count, needed, start
@@ -868,6 +1073,8 @@ def rank_program(g, core, T, topo):
             return ap(x[1]).indirect(ap(x[2]))
         if x[0] == "hbm":
             return T[x[1]][:] if x[2] is None else T[x[1]][:, x[2]:x[3]]
+        if x[0] == "nd":
+            return T[x[1]][(slice(None),) + x[2]]
         buf, at = SPEC[x[1]][3:]
         if x[4] == 1:
             return T[buf][:, at + x[2]:at + x[3]]
@@ -876,65 +1083,65 @@ def rank_program(g, core, T, topo):
     def sem_of(d):
         o = ops[d]
         if o["kind"] == "dma":
-            return T.sem[o["par"]], 16
-        if o["kind"] == "send":
-            dst = T.cores[(rank - 1 - o["par"] % (n - 1)) % n]
-            return T.sem["snt%d" % o["par"]], len(topo.engines(core, dst))
+            return T.sem[o["par"][0]], 16
+        if o["kind"] in ("send", "send2"):
+            dst = T.cores[(rank - 1 - o["par"][0] % (n - 1)) % n]
+            return T.sem["snt%d" % o["par"][1]], len(topo.engines(core, dst))
         if o["kind"] == "arrive":
-            src = T.cores[(rank + 1 + o["par"] % (n - 1)) % n]
-            return T.sem["arr%d" % o["par"]], len(topo.engines(src, core))
+            src = T.cores[(rank + 1 + o["par"][0] % (n - 1)) % n]
+            return T.sem["arr%d" % o["par"][1]], len(topo.engines(src, core))
         return T.sem["c_" + o["eng"]], count[d]
+
+    def call(q, o):
+        kind, par = o["kind"], o["par"]
+        out = ap(o["out"]) if o["out"] is not None else None
+        ins = [ap(x) for x in o["ins"]]
+        if kind in ("send", "send2"):
+            dst = T.cores[(rank - 1 - par[0] % (n - 1)) % n]
+            rid, pid, _ = topo.addr(dst)
+            return g.remote_dma(T["XR%d" % par[0]][:, o["ins"][0][2]:o["ins"][0][3]], ins[0], T.sem["arr%d" % par[1]],
+                                T.sem["snt%d" % par[1]], pid, rid, topo.mask(core, dst))
+        if kind == "dma":
+            if par[1]:
+                return q.dma_start(out, ins[0], accum_op=OP_.add, max_dma_last_dim=4096).then_inc(T.sem[par[0]], 16)
+            return q.dma_start(out, ins[0]).then_inc(T.sem[par[0]], 16)
+        if kind == "mm":
+            return q.matmul(out, ins[0], ins[1], par[0], par[1])
+        if kind == "copy":
+            return q.tensor_copy(out, ins[0])
+        if kind == "ts":
+            if par[1] is None:
+                return q.tensor_scalar(out, ins[0], ins[1], None, par[0])
+            return q.tensor_scalar(out, ins[0], ins[1], ins[2], par[0], par[1])
+        if kind == "tt":
+            return q.tensor_tensor(out, ins[0], ins[1], par)
+        if kind == "scan":
+            return q.tensor_tensor_scan(out, ins[0], ins[1], 0.0, par[0], par[1])
+        if kind == "memset":
+            return q.memset(out, par)
+        if kind == "tr":
+            return q.transpose(out, ins[0])
+        if kind == "act":
+            if o["acc"] is not None:
+                return q.activation(out, ins[0], par, ins[1], ins[2], accum_out=ap(o["acc"]))
+            return q.activation(out, ins[0], par, ins[1], ins[2])
+        if kind == "iota":
+            if SPEC[o["out"][1]][2] == "int32":
+                return g.iota(out, par[0], par[1], par[2])
+            return g.iota(out, par[0], par[1], par[2], allow_small_or_imprecise_dtypes=True)
+        return g.affine_select(out, ins[0], par[0], par[1], 0.0, par[2], par[3])
 
     for e in ENG:
         q = queue[e]
         for k in order[e]:
-            o = ops[k]
-            for d in o["waits"]:
+            for d in ops[k]["waits"]:
                 s, val = sem_of(d)
                 q.wait_ge(s, val)
-            kind, par = o["kind"], o["par"]
-            out = ap(o["out"]) if o["out"] is not None else None
-            ins = [ap(x) for x in o["ins"]]
-            if kind == "send":
-                dst = T.cores[(rank - 1 - par % (n - 1)) % n]
-                rid, pid, _ = topo.addr(dst)
-                g.remote_dma(T["XR%d" % par][:], ins[0], T.sem["arr%d" % par], T.sem["snt%d" % par], pid, rid,
-                             topo.mask(core, dst))
-                continue
-            if kind == "dma":
-                q.dma_start(out, ins[0]).then_inc(T.sem[par], 16)
-                continue
-            if kind == "mm":
-                r = q.matmul(out, ins[0], ins[1], par[0], par[1])
-            elif kind == "copy":
-                r = q.tensor_copy(out, ins[0])
-            elif kind == "ts":
-                if par[1] is None:
-                    r = q.tensor_scalar(out, ins[0], ins[1], None, par[0])
-                else:
-                    r = q.tensor_scalar(out, ins[0], ins[1], ins[2], par[0], par[1])
-            elif kind == "tt":
-                r = q.tensor_tensor(out, ins[0], ins[1], par)
-            elif kind == "scan":
-                r = q.tensor_tensor_scan(out, ins[0], ins[1], 0.0, par[0], par[1])
-            elif kind == "memset":
-                r = q.memset(out, par)
-            elif kind == "tr":
-                r = q.transpose(out, ins[0])
-            elif kind == "red":
-                r = q.tensor_reduce(out, ins[0], AxisListType.X, OP_.add)
-            elif kind == "act":
-                r = q.activation(out, ins[0], par, ins[1], ins[2])
-            elif kind == "iota":
-                if SPEC[o["out"][1]][2] == "int32":
-                    r = g.iota(out, par[0], par[1], par[2])
-                else:
-                    r = g.iota(out, par[0], par[1], par[2], allow_small_or_imprecise_dtypes=True)
-            else:
-                r = g.affine_select(out, ins[0], par[0], par[1], 0.0, par[2], par[3])
+            for o in ops[k]["calls"]:
+                r = call(q, o)
             if k in count:
                 r.then_inc(T.sem["c_" + e], 1)
     for k, o in enumerate(ops):
-        if o["kind"] in ("dma", "send", "arrive") and k not in needed:
+        if o["kind"] in ASYNC and k not in needed:
             s, val = sem_of(k)
             g.sync.wait_ge(s, val)

@@ -4,26 +4,15 @@ from concourse.mybir import AluOpType, ActivationFunctionType
 H = "float16"
 V, XW, RO = 1920, 4096, 5
 LAG = (220.0, 130.0)
-STEPS, SEED = (16000, 2500), 1
+BIG = 1.5 * 2.0 ** 35
 OPT = {
-    "halves": [0, 2, 4, 6],
-    "pairs": [(1, 2), (3, 4), (5, 6), (7,)],
-    "relu": [],
-    "direct": False, "four": False, "fused": 0, "fused_abs": 0, "b_dve": (), "by_min": [], "rec_dve": (),
-    "via_act": (),
-    "own": ("act", "act", "abs", "relu"),
-    "hash_cut": 2, "early": False, "n1": "dve",
-    "n2": ("dve", "act"),
-    "eq_act": [],
-    "eq_bank": (5, 6), "eq_late": [], "mean": 0.5,
-    "a_cut": ([("act", 64)] * 3 + [("act", 32)],) * 2,
-    "act": ("vr", "sf", "P", "penT"),
-    "xa": 1024,
+    "halves": (0, 2, 4),
+    "runs": ((1, 5), (5, 8)),
+    "fused": (6, 7),
+    "via_act": (9, 11, 13, 15),
+    "a_cut": ((64, 64, 64, 32), (64, 64, 32)),
+    "act": ("vr", "hq0", "AL0", "AL1", "CL", "tq", "BL0", "BL1", "BL2", "ui1"),
 }
-
-OPT.update(four=True, fused=2, fused_abs=0, halves=[0, 2, 4], via_act=(9, 11, 13, 15), own=("abs", "abs"),
-           a_cut=([("act", 64)] * 3 + [("act", 32)], [("act", 64)] * 2 + [("act", 32)]), eq_late=[1], eq_bank=(5, 7),
-           banks4=(0, 1, 5), banks2=(0, 1, 2, 3), split_p=True)
 
 SCRATCH = {}
 SPEC = {}
@@ -45,27 +34,25 @@ def _decl(where, dtype, spec):
         SCRATCH[pool] = (where, [128, at], dtype)
 
 
-_decl("psum", "float32", {"ps%d" % k: 512 for k in range(8)})
+BANKS = ["ps%d" % k for k in range(8)]
+_decl("psum", "float32", {b: 512 for b in BANKS})
 _decl("sbuf", "bfloat16", {
     "X": XW, "X0": XW, "XR0": XW, "XR1": XW, "XR2": XW, "XR3": XW, "XR4": XW, "m": 8192, "s": 8192, "a": 7168,
-    "ad": 7168, "W": 3072, "XP": 1024, "b": 1024, "d2": 1024, "ad2": 1024, "rec": 1024, "al": 512, "P": 512,
-    "penT": 512, "EQ": 1024, "EQm": 1024, "EQa": 1024, "z0": 512, "z1": 512, "xh": 1024, "BD": 18 * 128,
-    "WIDE": 1024, "NWIDE": 1024, "rgw": 1024, "BIAS": 128,
-    "IDb": 128, "NIDb": 128, "IDa": 128, "I8K": 128, "I2K": 128, "N2K": 128, "N64": 128, "I4M": 128, "BLK": 128,
-    "ONES": 128, "OBb": 8, "OB256": 8, "OB512": 8, "OBn": 8, "OBk": 8, "OBh": 8, "OBm": 8, "WB": 8, "WW": 143, "wb": 1, "SH": 8 * 144,
-    "SelS": 64, "NSel": 64, "yn": 64, "st": (8, 16), "sf": 128, "nask": 128, "incl": 129, "tq": 64, "RS": 64,
-    "OBW": 143, "OBW2": 143, "NOBW": 143, "FW": 134, "M1W": 136, "M2W": 136, "M3W": 136, "tri": 136})
-_decl("sbuf", H, {"N1h": 128, "N2h": 1024, "Th": 1024, "IWh": 192, "PM": 16 * 128, "vr": 128, "Zs": (4, 72, 2),
-                  "Zh": (4, 72, 2), "NMh": 512, "Rv": 128, "Rs": 128, "DL": 8, "nL": 64, "PL": 64, "u1": 64, "yq": 1,
-                  "hq": 64, "WP": 142, "WS": 16, "N1s": 128, "sum": 1024})
+    "ad": 7168, "W": 3072, "XP": 1024, "b": 1024, "d2": 1024, "ad2": 512, "rec": 1024, "al": 512, "P": 512,
+    "penT": 512, "EQ": 1024, "EQm": 1024, "z": 1536, "xh": 1024, "BD": 16 * 128, "WIDE": 1024, "NWIDE": 1024,
+    "rgw": 1024, "NIDb": 128, "IDa": 128, "I2K": 128, "I1K": 128, "N2K": 128, "N64": 128, "I8M": 128, "BLK": 128,
+    "ONES": 128, "OBb": 8, "OB256": 8, "OB512": 8, "OBn": 8, "OBk": 8, "WW": 143, "wb": 1, "SelS": 64, "NSel": 64,
+    "yn": 64, "st": (8, 16), "sf": 128, "nask": 128, "incl": 129, "tq": 64, "RS": 72, "OBW": 143, "OBW2": 143,
+    "FW": 134, "M1W": 136, "M2W": 136, "tri": 136})
+_decl("sbuf", H, {"N1h": 128, "N2h": 1024, "Th": 1024, "IWh": 192, "PM": 8 * 192, "vr": 128, "Zs": (4, 72, 2),
+                  "NMh": 512, "Zv": 143, "Zl": 143, "DL": 8, "vh": 8, "nL": 64, "PL": 64, "u1": 64, "yq": 1, "hq": 64,
+                  "WP": 142})
 _decl("sbuf", "float32", {
-    "E": 2048, "IOT": V, "sc": 512, "NN": 512, "e2": 128, "t2": 128, "k4": 64, "ld": 8, "thr": 1, "acc": 1, "af": 1, "yvf": 8,
-    "wf": 1, "wsf": 5, "wl": 64, "N1f": 128, "e1": 128, "ONE": 192, "IW": 192, "NID32": 128, "FC": 40, "MC": 24, "E16": 24, "CF": 24, "r": 144,
-    "rc": 128, "rg": 128, "r8": 136, "rj": 64, "CM": 128, "OBf": 8, "Sel32": 64, "JK": 64, "C1n": 64, "fa": 134,
-    "m5": 136})
-_decl("sbuf", "int32", {"E0": V, "vi": 8, "wi": 1, "IC": 16, "ui": 64, "u": 64, "u32": 64, "uw": 64, "h": 64,
-                        "gi": 8, "go": 8, "wsi": 3})
-_decl("sbuf", "uint16", {"VL": 8, "SL": 8, "LP": 128, "OP": 512, "AL": 448, "BL": 64, "HL": 64, "CL": 64, "LREP": 8})
+    "E": 2048, "sc": 512, "NN": 512, "e2": 128, "t2": 128, "k4": 72, "kr": 8, "thr": 1, "acc": 1, "af": 1, "yvf": 8,
+    "wf": 1, "wsf": 5, "ONE": 192, "IW": 192, "FC": 24, "MC": 4, "E16": 24, "CF": 24, "r": 160, "rg": 128, "r8": 144, "rj": 72,
+    "r1k": 64, "JK": 72, "C1n": 64, "fa": 134, "m5": 136})
+_decl("sbuf", "int32", {"E0": V, "vi": 8, "wi": 1, "IC": 16, "ui": 64, "u": 64, "u32": 64, "uw": 64, "h": 64, "wsi": 3})
+_decl("sbuf", "uint16", {"VL": 8, "SL": 8, "LP": 128, "OP": 512, "AL": 448, "BL": 64, "HL": 64, "CL": 64})
 
 ENG = ("pe", "dve", "act", "pool", "sp")
 SEMAPHORES = (["c_" + e for e in ENG[:4]] + ["dma%d" % k for k in range(24)] + ["arr%d" % k for k in range(11)]
@@ -114,20 +101,29 @@ def _spans(x):
     return [(x[1], int(c[0]), int(c[-1]) + 1)]
 
 
-def program(CY=0.95, G=1.56, PE=0.48, BW=330.0):
+def program(CY=0.87, G=1.56, PE=0.44, BW=400.0):
     ops = []
-    piece = [0]
+    piece, nbank, tag = [0], [0], [None, False]
 
     def cut():
         piece[0] += 1
 
-    def add(eng, kind, out, ins, par, ns, hold=None, acc=None):
-        if eng != "pe":
+    def bank(use):
+        name = "%s.%d" % (use, nbank[0])
+        nbank[0] += 1
+        SPEC[name] = ("psum", [128, 512], "float32", None, 0)
+        return name
+
+    def add(eng, kind, out, ins, par, ns, hold=None, acc=None, once=False):
+        if eng != "pe" or ops[-1]["eng"] != "pe" or ops[-1]["out"][1] != out[1]:
             cut()
         ops.append({"eng": eng, "kind": kind, "out": out, "ins": ins, "par": par, "ns": ns, "acc": acc,
-                    "hold": ns if hold is None else hold, "piece": piece[0]})
-        if eng != "pe":
-            cut()
+                    "hold": ns if hold is None else hold, "piece": piece[0], "once": once, "tag": tag[0], "any": tag[1]})
+        tag[:] = [None, False]
+
+    def named(text, anyorder=False):
+        cut()
+        tag[:] = [text, anyorder]
 
     def vcost(out, ins, rate=None):
         full = [x for x in ins if isinstance(x, tuple)]
@@ -162,22 +158,22 @@ def program(CY=0.95, G=1.56, PE=0.48, BW=330.0):
     def lin(out, in_, scale, bias=0.0):
         act(out, in_, AF.Identity, bias, scale)
 
-    def over(out, in_, bound, above=True):
+    def under(out, in_, bound):
         if out[1] in OPT["act"]:
-            sg = 256.0 if above else -256.0
-            act(out, in_, AF.Sigmoid, -sg * bound, sg)
+            act(out, in_, AF.Sigmoid, 256.0 * bound, -256.0)
         else:
-            ts(out, in_, bound, OP_.is_gt if above else OP_.is_lt)
+            ts(out, in_, bound, OP_.is_lt)
 
-    def shifted(eng, out, in_, by):
-        if eng == "act":
+    def moved(name, out, in_, by=0.0):
+        named(name)
+        if name in OPT["act"]:
             lin(out, in_, 1.0, by)
         else:
             ts(out, in_, by, add_)
 
-    def mm(out, lhsT, rhs, start=True, stop=True):
+    def mm(out, lhsT, rhs, start=True, stop=True, once=False):
         f = 4 if SPEC[rhs[1]][2] == "float32" else 1
-        add("pe", "mm", out, [lhsT, rhs], (start, stop), PE * f * max(64, _n(rhs)))
+        add("pe", "mm", out, [lhsT, rhs], (start, stop), PE * f * max(64, _n(rhs)), once=once)
 
     def mms(out, pairs):
         for k, (lhsT, rhs) in enumerate(pairs):
@@ -198,7 +194,6 @@ def program(CY=0.95, G=1.56, PE=0.48, BW=330.0):
 
     add_, sub_, mul, mx, mn = OP_.add, OP_.subtract, OP_.mult, OP_.max, OP_.min
     eq, shr, band = OP_.is_equal, OP_.arith_shift_right, OP_.bitwise_and
-    ps = ["ps%d" % k for k in range(8)]
 
     dma("sp", A("vi"), HB("v0"), 4096)
     dma("sp", A("E0", 0, 960), HB("e0", 0, 960), 500000)
@@ -210,8 +205,7 @@ def program(CY=0.95, G=1.56, PE=0.48, BW=330.0):
 
     iota(A("IC", 0, 1), [[0, 1]], 0, 1)
     cols = {"p": 0}
-    for name, sh, msk in (("k8", 3, 1), ("q4", 2, 3), ("e16", 4, 1), ("c16", 0, 15), ("b2", 0, 3), ("g", 4, 7),
-                          ("c4", 2, 1)):
+    for name, sh, msk in (("k8", 3, 1), ("c16", 0, 15), ("g", 4, 7), ("q4", 2, 3)):
         cols[name] = len(cols)
         ts(A("IC", cols[name], cols[name] + 1), A("IC", 0, 1), sh, shr, msk, band)
     cp(A("FC", 0, len(cols)), A("IC", 0, len(cols)))
@@ -226,119 +220,119 @@ def program(CY=0.95, G=1.56, PE=0.48, BW=330.0):
     mset(A("ONE"), 1.0)
     sel(A("IW"), A("ONE"), [[-1, 192]], eq, 32, 1)
     cp(A("IWh"), A("IW"))
-    iota(A("r"), [[1, 144]], 0, 0)
-    ts(newcol("shift"), col("k8"), 2048.0, mul, -2048.0, add_)
-    ts(A("MC", 0, 2), A("r", 0, 2), col("k8"), eq)
-    ts(A("MC", 4, 8), A("r", 0, 4), col("q4"), eq)
-    ts(A("MC", 8, 10), A("r", 0, 2), col("e16"), eq)
-    low8 = A("MC", 0, 1)
-    npm = [0]
+    iota(A("r"), [[1, 160]], -16, 0)
 
-    def perm(shift, mcol):
-        o = A("PM", 128 * npm[0], 128 * npm[0] + 128)
-        npm[0] += 1
-        ts(o, A("IWh", 32 - shift, 160 - shift), A("MC", mcol, mcol + 1), mul)
-        return o
-    PK = [[perm(8 * (h - kind), kind) for h in range(2)] for kind in range(2)]
-    R = [[perm(16 * (e - yy), 8 + yy) for yy in range(2)] for e in range(2)]
-    Q = [[perm(4 * l2 - 8 - 4 * c, 6 + c) for l2 in range(4)] for c in range(2)]
-    ID32, ID, NID = A("IW", 32, 160), A("IDb"), A("NIDb")
-    for name, scale in (("I2K", 2048.0), ("IDb", 1.0), ("NIDb", -1.0), ("IDa", -65.0), ("I8K", 8192.0),
-                        ("N2K", -2048.0), ("N64", -64.0), ("I4M", 4194304.0)):
+    def run(a, b):
+        return A("r", 16 + a, 16 + b)
+    ts(newcol("shift"), col("k8"), 2048.0, mul, -2048.0, add_)
+    ts(A("MC"), run(0, 4), col("q4"), eq)
+    wide = {}
+
+    def perm(shift, unit, ways, want):
+        key = (unit, want)
+        if key not in wide:
+            wide[key] = 192 * len(wide)
+            o = A("PM", wide[key], wide[key] + 192)
+            if unit == 4 and want > 1:
+                ts(o, A("IWh"), A("MC", want, want + 1), mul)
+            else:
+                sel(o, A("ONE"), [[-unit * ways, 192 // (unit * ways)], [1000 - unit, ways], [-1, unit]], eq,
+                    32 - 1000 * want, 1)
+        return A("PM", wide[key] + 32 - shift, wide[key] + 160 - shift)
+    PK = [[perm(8 * (h - kind), 8, 2, kind) for h in range(2)] for kind in range(2)]
+    R = [[perm(16 * (e - yy), 16, 2, yy) for yy in range(2)] for e in range(2)]
+    Q = [[perm(4 * l2 - 8 - 4 * c, 4, 4, 2 + c) for l2 in range(4)] for c in range(2)]
+    SH = [[perm(4 * (c - l2), 4, 4, l2) for l2 in range(4)] for c in range(2)]
+    M3 = [perm(8 * l0, 8, 2, 0) for l0 in range(2)]
+    ID32, ID, NID = A("IW", 32, 160), A("IWh", 32, 160), A("NIDb")
+    for name, scale in (("I2K", 2048.0), ("NIDb", -1.0), ("IDa", -65.0), ("N2K", -2048.0), ("N64", -64.0),
+                        ("I8M", 8388608.0), ("I1K", 1024.0)):
         lin(A(name), ID32, scale)
-    lin(A("ONES"), A("ONE", 0, 128), 1.0)
-    sel(A("Sel32"), A("ONE", 0, 64), [[2, 4], [16, 8], [1, 2]], eq, 8, -1)
-    lin(A("SelS"), A("Sel32"), 1.0)
-    lin(A("NSel"), A("Sel32"), -1.0)
+    iota(A("ONES"), [[0, 128]], 1, 0)
+    sel(A("SelS"), A("ONE", 0, 64), [[2, 4], [16, 8], [1, 2]], eq, 8, -1)
+    lin(A("NSel"), A("SelS"), -1.0)
     iota(A("rg"), [[1, 8], [0, 16]], 0, 0)
     ts(A("BLK"), A("rg"), col("g"), eq)
-    ts(A("OBf"), A("r", 0, 8), col("g"), eq)
     OBb = A("OBb")
-    for name, scale in (("OBb", 1.0), ("OB256", 256.0), ("OB512", 512.0), ("OBn", -256.0), ("OBk", 16384.0),
-                        ("OBh", 1.0 / 16)):
-        lin(A(name), A("OBf"), scale)
+    ts(OBb, run(0, 8), col("g"), eq)
+    for name, scale in (("OB256", 256.0), ("OB512", 512.0), ("OBn", -256.0), ("OBk", 32768.0)):
+        lin(A(name), OBb, scale)
     cp(A("wf"), A("wi"))
-    mset(ND("st", slice(None)), 0.0)
+    iota(ND("st", slice(None)), [[0, 128]], 0, 0)
     lin(newcol("sfb"), col("k8"), 256 * 2048.0, -256 * (2048.0 + 540.5))
-    ts(A("E16", 0, 17), A("r", 0, 17), col("c16"), eq)
+    ts(A("E16", 0, 17), run(0, 17), col("c16"), eq)
     tt(A("CF", 0, 16), A("E16", 1, 17), A("E16", 0, 16), sub_)
-    ts(A("CF", 7, 16, 8), A("E16", 7, 16, 8), -2.0, mul)
-    cp(A("CF", 16, 18), A("E16", 0, 9, 8))
-    for x in range(18):
-        if x % 3:
-            lin(A("BD", 128 * x, 128 * x + 128), A("BLK"), A("CF", x, x + 1))
+    for x in range(16):
+        o, factor = A("BD", 128 * x, 128 * x + 128), A("E16", x - 7, x - 6) if x % 8 == 7 else A("CF", x, x + 1)
+        if x % 3 == 1:
+            lin(o, A("BLK"), factor)
         else:
-            ts(A("BD", 128 * x, 128 * x + 128), A("BLK"), A("CF", x, x + 1), mul)
+            ts(o, A("BLK"), factor, mul)
     iota(A("rgw"), [[1, 8], [0, 128]], 0, 0)
-    ts(A("WIDE"), A("rgw"), col("g"), eq, 1.0 / 16, mul)
-    ts(A("NWIDE"), A("rgw"), col("g"), eq, -1.0 / 16, mul)
-    iota(A("IOT"), [[1, V]], 0, 0)
-    lin(A("wb"), A("wf"), 1.0)
-    mm(A(ps[6], 0, 1), A("BLK"), A("wb"))
-    ts(A("wsi", 0, 1), A(ps[6], 0, 1), 2048.0, add_)
-    ts(A("wsf", 1, 2), A(ps[6], 0, 1), -256.0, mul, 2097152.0, add_)
-    ts(A("wsf", 4, 5), A(ps[6], 0, 1), -128.0, mul, 2097152.0, add_)
+    ts(A("WIDE"), A("rgw"), col("g"), eq)
+    ts(A("NWIDE"), A("rgw"), col("g"), eq, -1.0, mul)
+    cp(A("vh"), A("vi"))
+    pb = bank("v0")
+    for x in range(16):
+        mm(A(pb, x, 128, 16), A("IWh", 32 + x, 160 + x), A("vh"))
+    lin(A("vr"), A(pb, 0, 128), A("E16", 0, 1))
+    lin(A("wb"), A("wi"), 1.0)
+    pb = bank("ws")
+    mm(A(pb, 0, 1), A("BLK"), A("wb"))
+    lin(A("wsi", 0, 1), A(pb, 0, 1), 1.0, 2048.0)
+    lin(A("wsf", 1, 2), A(pb, 0, 1), -256.0, 2097152.0)
+    lin(A("wsf", 4, 5), A(pb, 0, 1), -128.0, 2097152.0)
     ts(A("wsi", 1, 2), A("wsi", 0, 1), 4095, band)
     tt(A("wsf", 2, 3), A("E16", 0, 1), A("E16", 8, 9), add_)
     ts(A("wsf", 3, 4), A("wsi", 1, 2), -2048.0, add_, A("wsf", 2, 3), mul)
     mset(ND("Zs", slice(None)), 0.0)
-    mset(A("incl", 0, 1), 0.0)
-    iota(A("rc"), [[0, 8], [1, 16]], 0, 0)
-    ts(A("CM"), A("rc"), col("c16"), eq)
-    cp(A("LREP"), A("r", 0, 8))
-    iota(A("rj"), [[0, 8], [1, 8]], 0, 0)
-    lin(A("JK"), A("rj"), -2048.0, 7 * 2048.0 - 2127 * 16384.0 - 4194304.0)
-    ts(A("RS"), A("rj"), 0.5, OP_.is_gt)
-    mset(A("thr"), 256 * (4096.0 + 14.5))
+    iota(A("incl", 0, 1), [[0, 1]], 0, 0)
+    for name in ("Zv", "Zl"):
+        sel(A(name), A("ONE", 0, 143), [[0, 143]], eq, 1, 0)
+    iota(A("rj"), [[0, 8], [1, 9]], 0, 0)
+    lin(A("rj"), A("rj"), -4096.0, 7 * 4096.0 - 2127 * 32768.0 - 8388608.0)
+    sel(A("JK"), A("rj"), [[0, 8], [1, 9]], OP_.not_equal, -8, 0)
+    sel(A("RS"), A("ONE", 0, 72), [[0, 8], [1, 9]], OP_.is_gt, 0, 0)
+    iota(A("thr"), [[0, 1]], 256 * 4096 + 256 * 14 + 128, 0)
     lin(newcol("d2k"), col("p"), 1.0, float(V - 2048))
-    ts(A("nL"), A("r", 0, 64), 16.0, mul, col("c16"), add_)
+    ts(A("nL"), run(0, 64), 16.0, mul, col("c16"), add_)
     ts(A("DL"), A("nL", 0, 8), float(V), add_)
-    lin(newcol("t0"), col("c4"), 512.0, col("b2"))
-    lin(newcol("t1"), col("k8"), 4.0, col("t0"))
-    lin(newcol("pl"), col("t1"), 1.0, 1024.0)
-    ts(A("PL"), A("r", 0, 64), 8.0, mul, col("pl"), add_)
+    lin(newcol("t0"), col("q4"), 508.0, col("c16"))
+    lin(newcol("pl"), col("k8"), -1020.0, col("t0"))
+    iota(A("r1k"), [[8, 64]], 1024, 0)
+    lin(A("PL"), A("r1k"), 1.0, col("pl"))
     tt(A("C1n"), A("nL"), A("PL"), sub_)
-    lin(newcol("g15"), col("g"), 16.0, 15.0)
-    ts(A("OBW"), A("r", 0, 143), col("g15"), eq)
+    ts(A("OBW"), run(-15, 128), col("c16"), add_, col("p"), eq)
     lin(A("WW"), A("OBW"), A("wf"))
-    lin(newcol("t3"), col("g"), 16.0, 14.0)
-    lin(newcol("wp"), col("k8"), 1.0, col("t3"))
-    ts(A("WP"), A("r", 0, 142), col("wp"), eq, A("wsf", 3, 4), mul)
-    for l2 in range(4):
-        ts(A("SH", 144 * l2, 144 * l2 + 132), A("IWh", 28 + 4 * l2, 160 + 4 * l2), A("MC", 4 + l2, 5 + l2), mul)
-    if "relu" in OPT["own"]:
-        lin(A("OBW2"), A("OBW"), 2.0)
-        lin(A("NOBW"), A("OBW"), -1.0)
-    lin(newcol("t2"), col("g"), -16.0, -10.0)
-    lin(newcol("fw"), col("k8"), -1.0, col("t2"))
-    act(A("fa"), A("r", 0, 134), AF.Abs, col("fw"))
+    lin(A("OBW2"), A("OBW"), -2.0)
+    lin(newcol("wp"), col("k8"), -7.0, col("p"))
+    ts(A("WP"), run(-14, 128), col("wp"), eq, A("wsf", 3, 4), mul)
+    lin(newcol("fw"), col("g"), 16.0, col("k8"))
+    act(A("fa"), run(-10, 124), AF.Abs, col("fw"), -1.0)
     ts(A("FW"), A("fa"), 4.0, eq)
-    iota(A("r8"), [[1, 17], [0, 8]], 0, 0)
-    lin(newcol("g2"), col("g"), 2.0, 1.0)
+    iota(A("r8"), [[1, 9], [-1000, 2], [0, 8]], 1000, 0)
     lin(newcol("nk"), col("k8"), 1.0, -1.0)
-    ts(A("M1W"), A("r8"), col("g2"), eq, col("nk"), mul)
+    ts(A("M1W"), A("r8", 0, 136), col("g"), eq, col("nk"), mul)
     sel(A("tri"), A("M1W"), [[1, 136]], OP_.is_gt, -8, -1)
-    ts(A("M3W"), A("IWh", 24, 160), low8, mul)
-    lin(A("m5"), A("M3W"), 512.0)
+    lin(A("m5"), A("PM", 24, 160), 512.0)
     tt(A("M2W"), A("m5"), A("tri"), add_)
-    ts(A("t2"), A("r", 0, 128), 8.0, mul, col("c16"), add_)
-    for q in range(4):
-        ts(A("NN", 128 * q, 128 * q + 128), A("t2"), 1024.0 * q, add_, low8, mul)
-        lin(A("NMh", 128 * q, 128 * q + 128), A("NN", 128 * q, 128 * q + 128), 1.0, col("shift"))
+    iota(A("sc"), [[1024, 4], [8, 128]], 0, 0)
+    lin(newcol("cn"), col("c16"), col("nk"))
+    lin(A("NN"), A("sc"), col("nk"), col("cn"))
+    lin(A("NMh"), A("NN"), -1.0, col("shift"))
     sel(A("E", 0, V), A("E0"), [[0, V]], OP_.is_ge, 0, 0)
-    for k in range(4):
-        iota(A("X", 1024 * k, 1024 * k + 1024), [[0, 1024]], 128, 0)
+    iota(A("X", 0, 1024), [[0, 1024]], 128, 0)
+    for k in range(1, 4):
+        dma("sp", A("X", 1024 * k, 1024 * k + 1024), A("X", 0, 1024), 262144)
     dma("pool", A("X"), A("X0"), 2097152, True)
 
-    def sublist(nodes):
-        shifted(OPT["n1"], A("N1s"), IND(nodes, A("VL")), 0.0)
-        mms(A(ps[7], 448, 512), [(PK[1][h], A("N1s", h, 128, 2)) for h in range(2)])
-        cp(A("LP", 64, 128), A(ps[7], 448, 512))
+    def lanes(Z, rhs):
+        return [(A(Z, 15 - x, 143 - x), A(rhs[1], rhs[2] + x, rhs[3], 16)) for x in range(16)]
 
     XWIN = A("X")
-    nscan, nsend = [0, 0], [0]
+    nscan, nsend = [0], [0]
     for t in range(RO):
-        blk, last, reset = 1024 * (t % 4), t == RO - 1, set()
+        blk, last = 1024 * (t % 4), t == RO - 1
         XR = "XR%d" % t
         EW, XC, up = (A("E", 0, V), XWIN, 128.0) if t else (A("E0"), A("X0"), 0.0)
         parts = [(t, blk - 1024, blk) if t % 4 else (t, 3072 if t else 0, XW)]
@@ -355,362 +349,325 @@ def program(CY=0.95, G=1.56, PE=0.48, BW=330.0):
         if last:
             dma("pool", A("X0", 1024, XW), A("X", 1024, XW), 1572864, True)
             dma("sp", HB("yx", 1024, XW), A("X0", 1024, XW), 786432)
-        shifted("act" if "vr" in OPT["act"] else "dve", A("vr"), IND(A("IOT"), A("VL")), 0.0)
-
-        def same(halves):
-            for hf in halves:
-                o0, o1, bank = 512 * hf, 512 * hf + 512, ps[(OPT["eq_bank"] if t else (5, 7))[hf]]
-                mm(A(bank), A("vr"), A("NWIDE", o0, o1), True, False)
-                for g4 in range(4):
-                    g_ = 4 * hf + g4
-                    mm(A(bank, 128 * g4, 128 * g4 + 128), A("WIDE", 128 * g_, 128 * g_ + 128), A("vr"), False, g4 == 3)
-                if hf in OPT["eq_act"]:
-                    act(A("EQa", o0, o1), A(bank), AF.Abs)
-                    ts(A("EQ", o0, o1), A("EQa", o0, o1), 0.0, eq, 2048.0, mul)
-                else:
-                    ts(A("EQ", o0, o1), A(bank), 0.0, eq, 2048.0, mul)
-                sel(A("EQm", o0, o1), A("EQ", o0, o1), [[0, 4], [1, 128]], OP_.is_gt, 0, -1)
-        late = OPT["eq_late"] if t else [0, 1]
-        same([hf for hf in range(2) if hf not in late])
-        if OPT["early"]:
-            if t == 0:
-                sublist(EW)
-            shifted(OPT["n1"], A("N1h"), IND(EW, A("VL")), col("shift"))
-            mms(A(ps[7], 384, 448), [(PK[0][h], A("N1h", h, 128, 2)) for h in range(2)])
-            ts(A("LP", 0, 64), A(ps[7], 384, 448), 2048.0, add_)
-            if not last:
-                act(A("N1f"), IND(EW, A("VL")), AF.Copy)
-        else:
-            ts(A("N1h"), IND(EW, A("VL")), col("shift"), add_)
-            mms(A(ps[7], 448, 512), [(PK[1][h], A("N1h", h, 128, 2)) for h in range(2)])
-            mms(A(ps[7], 384, 448), [(A("I2K"), A("ONES", 0, 64))] + [(PK[0][h], A("N1h", h, 128, 2)) for h in range(2)])
-            cp(A("LP"), A(ps[7], 384, 512))
+        for hf in range(2):
+            o0, o1, pb = 512 * hf, 512 * hf + 512, bank("eq")
+            mm(A(pb), A("vr"), A("NWIDE", o0, o1), True, False)
+            for g4 in range(4):
+                g_ = 4 * hf + g4
+                mm(A(pb, 128 * g4, 128 * g4 + 128), A("WIDE", 128 * g_, 128 * g_ + 128), A("vr"), False, g4 == 3)
+            ts(A("EQ", o0, o1), A(pb), 0.0, eq, 2048.0, mul)
+            sel(A("EQm", o0, o1), A("EQ", o0, o1), [[0, 4], [1, 128]], OP_.is_gt, 0, -1)
+        ts(A("N1h"), IND(EW, A("VL")), col("shift"), add_)
+        pb = bank("lp")
+        mms(A(pb, 64, 128), [(PK[1][h], A("N1h", h, 128, 2)) for h in range(2)])
+        mms(A(pb, 0, 64), [(A("I2K"), A("ONES", 0, 64))] + [(PK[0][h], A("N1h", h, 128, 2)) for h in range(2)])
+        moved("LP", A("LP"), A(pb, 0, 128))
         for hf in range(2):
             o0, o1 = 512 * hf, 512 * hf + 512
-            shifted(OPT["n2"][hf], A("N2h", o0, o1), IND(EW, A("LP", 64 + 32 * hf, 96 + 32 * hf)), col("shift"))
+            ts(A("N2h", o0, o1), IND(EW, A("LP", 64 + 32 * hf, 96 + 32 * hf)), col("shift"), add_)
             act(A("XP", o0, o1), IND(XC, A("LP", 32 * hf, 32 * hf + 32)), AF.Copy)
             add("dve", "tr", A("Th", o0, o1), [A("N2h", o0, o1)], None, vcost(A("Th", o0, o1), [A("N2h", o0, o1)]))
             if hf == 0:
+                pb = bank("op")
                 for yy in range(2):
-                    mms(A(ps[2], yy, 32, 2), [(R[e][yy], A("Th", 16 * e, 512, 32)) for e in range(2)])
-                ts(A("OP", 0, 32), A(ps[2], 0, 32), 2048.0, add_)
+                    mms(A(pb, yy, 32, 2), [(R[e][yy], A("Th", 16 * e, 512, 32)) for e in range(2)])
+                moved("OPa", A("OP", 0, 32), A(pb, 0, 32), 2048.0)
         for c in range(2):
+            pb = bank("op")
             for jj in range(4):
                 lo = 32 if c == 0 and jj == 0 else 0
                 for yy in range(2):
-                    mms(A(ps[2 + c], 64 * jj + lo + yy, 64 * jj + 64, 2),
+                    mms(A(pb, 64 * jj + lo + yy, 64 * jj + 64, 2),
                         [(R[e][yy], A("Th", 16 * lo + 16 * e + 4 * c + jj, 1024, 32)) for e in range(2)])
             lo = 0 if c else 32
-            ts(A("OP", 256 * c + lo, 256 * c + 256), A(ps[2 + c], lo, 256), 2048.0, add_)
+            moved("OP%d" % c, A("OP", 256 * c + lo, 256 * c + 256), A(pb, lo, 256), 2048.0)
+            pb = bank("al")
             for i in range(1, 8):
-                mms(A(ps[c], 32 * (i - 1), 32 * i), [(Q[c][l2], A("N2h", 8 * l2 + i, 1024, 32)) for l2 in range(4)])
-                if i == 3:
+                mms(A(pb, 32 * (i - 1), 32 * i), [(Q[c][l2], A("N2h", 8 * l2 + i, 1024, 32)) for l2 in range(4)])
+                if i in (3, 5, 6):
                     cut()
-            cp(A("AL", 224 * c, 224 * c + 224), A(ps[c], 0, 224))
+            moved("AL%d" % c, A("AL", 224 * c, 224 * c + 224), A(pb, 0, 224))
+        df = bank("df")
         for pos in range(8):
             pairs = [(A("N2h", 7 - pos, 1024, 8), A("SelS"))]
             if pos < 7:
                 pairs.append((A("N2h", 6 - pos, 1024, 8), A("NSel")))
-            mms(A(ps[4], pos, 512, 8), pairs)
+            mms(A(df, pos, 512, 8), pairs)
+
         def subs(c):
             k = 224 * c
-            for eng, width in OPT["a_cut"][c]:
-                out, src = A("a", 16 * k, 16 * (k + width)), IND(XC, A("AL", k, k + width))
-                act(out, src, AF.Copy) if eng == "act" else cp(out, src)
+            for width in OPT["a_cut"][c]:
+                named("a%d" % (k // 32 + c + 1))
+                act(A("a", 16 * k, 16 * (k + width)), IND(XC, A("AL", k, k + width)), AF.Copy)
                 k += width
 
         def cross(y0, y1):
-            w0, w1, o, n_ = 128 * y0, 128 * y1, 128 * (y0 & 1), y1 - y0
-            for j in range(2 * y0, 2 * y1):
-                for l0, l1 in ([(0, 32), (32, 64)] if j in OPT["halves"] else [(0, 64)]):
-                    tt(A("m", 1024 * j + 16 * l0, 1024 * j + 16 * l1), IND(XC, A("OP", 64 * j + l0, 64 * j + l1)),
-                       A("XP", 16 * l0, 16 * l1), mn)
-                oj = 128 * (j >> 1 & 1)
-                for i in range(8):
-                    mm(A(ps[5], oj + 8 * (j & 1) + 7 - i, oj + 128, 16), A("m", 1024 * j + i, 1024 * j + 1024, 8), OBb)
-                if j & 1:
-                    w0, w1 = 64 * j - 64, 64 * j + 64
-                    over(A("al", w0, w1), A(ps[5], oj, oj + 128), 16 * up + 79.5, False)
-                    scan(A("sc", w0, w1), A("al", w0, w1), A(ps[4], w0, w1), mul, add_)
-                    ts(ND("Zs", j >> 1, slice(7, 64, 8)), A("sc", w0 + 7, w1, 8), 0.0, mx, V - 1.0, mn)
-                    y, lb = j >> 1, A(ps[5], 256 + 16 * y0, 256 + 16 * y1) if n_ == 1 else A(ps[4], 0, 32)
-                    for x in range(8 // n_):
-                        mm(lb, ND("Zs", y, slice(7 - n_ * x - y + y0, 71 - n_ * x - y + y0)),
-                           A("IDb", x, 128, 8 // n_), y == y0 and x == 0, y == y1 - 1 and x == 8 // n_ - 1)
-            cp(A("BL", 16 * y0, 16 * y1), lb)
-            out, src = A("b", 256 * y0, 256 * y1), IND(XC, A("BL", 16 * y0, 16 * y1))
-            cp(out, src) if y0 in OPT["b_dve"] else act(out, src, AF.Copy)
+            n_ = y1 - y0
+            lb = A(bank("bl"), 0, 16 * n_)
+            for y in range(y0, y1):
+                pb = bank("cr")
+                for j in (2 * y, 2 * y + 1):
+                    for l0, l1 in ([(0, 32), (32, 64)] if j in OPT["halves"] else [(0, 64)]):
+                        named("m%d%s" % (j, "b" if l0 else ""))
+                        tt(A("m", 1024 * j + 16 * l0, 1024 * j + 16 * l1), IND(XC, A("OP", 64 * j + l0, 64 * j + l1)),
+                           A("XP", 16 * l0, 16 * l1), mn)
+                    named("cr%d" % j, j > 2 * y)
+                    for i in range(8):
+                        mm(A(pb, 8 * (j & 1) + 7 - i, 128, 16), A("m", 1024 * j + i, 1024 * j + 1024, 8), OBb)
+                w0, w1 = 128 * y, 128 * y + 128
+                named("al%d" % y)
+                under(A("al", w0, w1), A(pb, 0, 128), 16 * up + 79.5)
+                named("sc%d" % y)
+                scan(A("sc", w0, w1), A("al", w0, w1), A(df, w0, w1), mul, add_)
+                named("Zs%d" % y)
+                ts(ND("Zs", y, slice(7, 64, 8)), A("sc", w0 + 7, w1, 8), 0.0, mx, V - 1.0, mn)
+                named("bl%d" % y)
+                for x in range(8 // n_):
+                    mm(lb, ND("Zs", y, slice(7 - n_ * x - y + y0, 71 - n_ * x - y + y0)),
+                       A("IWh", 32 + x, 160, 8 // n_), y == y0 and x == 0, False)
+            moved("BL%d" % y0, A("BL", 16 * y0, 16 * y1), lb)
+            named("b%d" % y0)
+            act(A("b", 256 * y0, 256 * y1), IND(XC, A("BL", 16 * y0, 16 * y1)), AF.Copy)
 
-        def misfits4(c):
-            w0, w1, zb, B = 256 * c, 256 * c + 256, ps[6], A("b", 512 * c, 512 * c + 512)
-            mm(A(zb, 0, 256), A("I8K"), A("al", w0, w1), True, False)
-            mine = list(range(8 - OPT["fused"], 8))
-            rest = list(range(1, 8 - OPT["fused"]))
-            turn = []
-            while mine or rest:
-                turn += [x.pop(0) for x in (rest, mine) if x]
-            nabs = 0
-            for i in turn:
-                o = 3584 * c + 512 * (i - 1)
-                terms = [("ad", "OB256")]
-                cut()
-                if i >= 8 - OPT["fused"]:
-                    k = 224 * c + 32 * (i - 1)
-                    tt(A("a", o, o + 512), IND(XC, A("AL", k, k + 32)), B, sub_)
-                    if 7 - i < OPT["fused_abs"]:
-                        act(A("ad", o, o + 512), A("a", o, o + 512), AF.Abs)
-                    else:
-                        ts(A("ad", o, o + 512), A("a", o, o + 512), 0.0, mx)
-                        terms = [("a", "OBn"), ("ad", "OB512")]
+        def penalties(y, zb, o):
+            w0, w1, tb = 128 * y, 128 * y + 128, bank("pt")
+            act(A("P", w0, w1), A(zb, o, o + 128), AF.Sigmoid, -256 * 24.5)
+            mms(A(tb, 0, 128), [(A("al", w0, w1), ID), (A("P", w0, w1), A("IDa"))])
+            lin(A("penT", w0, w1), A(tb, 0, 128), 1.0, 128.0)
+
+        def misfits(y):
+            zb, o = bank("z"), 1792 * y
+            named("z%d" % y)
+            mm(A(zb, 0, 128), A("I8M"), A("al", 128 * y, 128 * y + 128), True, False)
+            for i0, i1 in OPT["runs"]:
+                for j0 in range(2):
+                    pb, n_, nm = bank("ab"), 128 * (i1 - i0), "%d%d" % (2 * y + j0, i0)
+                    named("da" + nm)
+                    mm(A(pb, 0, n_), ID, A("a", 2 * y + j0 + 512 * (i0 - 1), 512 * (i1 - 1), 4), True, False)
+                    named("db" + nm)
+                    for k in range(i1 - i0):
+                        mm(A(pb, 128 * k, 128 * k + 128), NID, A("b", 256 * y + j0, 256 * y + 256, 2), False, False)
+                    named("ad" + nm)
+                    act(A("ad", o, o + n_), A(pb, 0, n_), AF.Abs)
+                    named("z" + nm, True)
+                    for k in range(i1 - i0):
+                        mm(A(zb, 8 * j0 + 7 - i0 - k, 128, 16), A("ad", o + 128 * k, o + 128 * k + 128), A("OB256"),
+                           False, False)
+                    o += n_
+            penalties(y, zb, 0)
+
+        def misfits4():
+            zb, B = bank("z"), A("b", 512, 1024)
+            named("z4")
+            mm(A(zb, 0, 256), A("I8M"), A("al", 256, 512), True, False)
+            for i in range(1, 8):
+                o, nm, terms = 3584 + 512 * (i - 1), "q%d" % i, [("ad", "OB256")]
+                if i in OPT["fused"]:
+                    named("a" + nm)
+                    tt(A("a", o, o + 512), IND(XC, A("AL", 192 + 32 * i, 224 + 32 * i)), B, sub_)
+                    named("ad" + nm)
+                    ts(A("ad", o, o + 512), A("a", o, o + 512), 0.0, mx)
+                    terms = [("a", "OBn"), ("ad", "OB512")]
                 else:
-                    bank = ps[OPT["banks4"][nabs % len(OPT["banks4"])]]
-                    nabs += 1
-                    mms(A(bank), [(ID, A("a", o, o + 512)), (NID, B)])
-                    act(A("ad", o, o + 512), A(bank), AF.Abs)
+                    pb = bank("ab")
+                    named("da" + nm)
+                    mm(A(pb), ID, A("a", o, o + 512), True, False)
+                    named("db" + nm)
+                    mm(A(pb), NID, B, False, True)
+                    named("ad" + nm)
+                    act(A("ad", o, o + 512), A(pb), AF.Abs)
                 for name, rhs in terms:
+                    named("z" + name + nm, True)
                     for jj in range(4):
                         oo = 128 * (jj >> 1)
                         mm(A(zb, oo + 8 * (jj & 1) + 7 - i, oo + 128, 16), A(name, o + jj, o + 512, 4),
-                           A(rhs), False, i == turn[-1] and jj == 3 and name == "ad")
-            if OPT["split_p"]:
-                for yy in range(2):
-                    act(A("P", w0 + 128 * yy, w0 + 128 * yy + 128), A(zb, 128 * yy, 128 * yy + 128), AF.Sigmoid, -256 * 24.5)
-                for yy in range(2):
-                    o, tb = w0 + 128 * yy, ps[yy]
-                    mms(A(tb, 0, 128), [(A("al", o, o + 128), ID), (A("P", o, o + 128), A("IDa"))])
-                    lin(A("penT", o, o + 128), A(tb, 0, 128), 1.0, 128.0)
-                return
-            act(A("P", w0, w1), A(zb, 0, 256), AF.Sigmoid, -256 * 24.5)
+                           A(rhs), False, False)
             for yy in range(2):
-                o = w0 + 128 * yy
-                mms(A(zb, 256 + 128 * yy, 384 + 128 * yy), [(A("al", o, o + 128), ID), (A("P", o, o + 128), A("IDa"))])
-            lin(A("penT", w0, w1), A(zb, 256, 512), 1.0, 128.0)
-
-        def misfits(y):
-            w0, w1, zb = 128 * y, 128 * y + 128, ps[6 + (y & 1)]
-            mm(A(zb, 0, 128), A("I8K"), A("al", w0, w1), True, False)
-            for n_, pair in enumerate(OPT["pairs"]):
-                bank, o = ps[OPT["banks2"][(4 * y + n_) % len(OPT["banks2"])] if y < 1 else n_ & 1], 1792 * y + 256 * (pair[0] - 1)
-                both = [(i, j0, A("a", 3584 * (y >> 1) + 512 * (i - 1) + 2 * (y & 1) + j0, 3584 * (y >> 1) + 512 * i, 4),
-                         A("b", 256 * y + j0, 256 * y + 256, 2)) for i in pair for j0 in range(2)]
-                cut()
-                if (y, n_) in OPT["by_min"]:
-                    for j0 in range(2):
-                        mm(A(bank, 128 * j0, 128 * j0 + 128), ID, both[j0][3])
-                    for k, (i, j0, a, b) in enumerate(both):
-                        tt(A("ad", o + 128 * k, o + 128 * k + 128), a, A(bank, 128 * j0, 128 * j0 + 128), mn)
-                    for k, (i, j0, a, b) in enumerate(both):
-                        out = A(zb, 8 * j0 + 7 - i, 128, 16)
-                        mm(out, a, A("OB256"), False, False)
-                        mm(out, b, A("OB256"), False, False)
-                        mm(out, A("ad", o + 128 * k, o + 128 * k + 128), A("OBm"), False, i == 7 and j0 == 1)
-                    continue
-                for k, (i, j0, a, b) in enumerate(both):
-                    mms(A(bank, 128 * k, 128 * k + 128), [(ID, a), (NID, b)])
-                relu = (y, n_) in OPT["relu"]
-                if relu:
-                    ts(A("ad", o, o + 256 * len(pair)), A(bank, 0, 256 * len(pair)), 0.0, mx)
-                else:
-                    act(A("ad", o, o + 256 * len(pair)), A(bank, 0, 256 * len(pair)), AF.Abs)
-                for k, (i, j0, a, b) in enumerate(both):
-                    out = A(zb, 8 * j0 + 7 - i, 128, 16)
-                    if relu:
-                        mm(out, a, A("OBn"), False, False)
-                        mm(out, b, A("OB256"), False, False)
-                    mm(out, A("ad", o + 128 * k, o + 128 * k + 128), A("OB512" if relu else "OB256"), False,
-                       i == 7 and j0 == 1)
-            if "P" in OPT["act"]:
-                act(A("P", w0, w1), A(zb, 0, 128), AF.Sigmoid, -256 * 24.5)
-            else:
-                ts(A("P", w0, w1), A(zb, 0, 128), 256 * 24.5, OP_.is_gt)
-            mms(A(zb, 128, 256), [(A("al", w0, w1), ID), (A("P", w0, w1), A("IDa"))])
-            shifted("act" if "penT" in OPT["act"] else "dve", A("penT", w0, w1), A(zb, 128, 256), 128.0)
+                penalties(2 + yy, zb, 128 * yy)
 
         def greatest(y):
             for j0 in range(2):
                 for hf in range(2):
-                    bank = ps[(2, 3, 1)[nscan[0] % 3]] if y == 3 or y == 2 and OPT["four"] else ps[2 + nscan[0] % 2]
+                    pb = bank("mx")
                     pT = A("penT", 128 * y + 64 * hf, 128 * y + 64 * hf + 64)
-                    cut()
-                    for i in range(1 if bank in reset else 0, 8):
+                    for i in range(8):
                         x = 8 * j0 + 7 - i
-                        mm(A(bank, i, 512, 8), A("BD", 128 * x, 128 * x + 128), pT)
-                    reset.add(bank)
+                        mm(A(pb, i, 512, 8), A("BD", 128 * x, 128 * x + 128) if i else A("N64"), pT, once=i == 0)
                     o = 2048 * y + 1024 * j0 + 512 * hf
-                    src = A(bank)
+                    src = A(pb)
                     if (o // 512) in OPT["via_act"]:
-                        src = A("z%d" % (nscan[1] % 2))
-                        nscan[1] += 1
-                        act(src, A(bank), AF.Copy)
+                        src = A("z", 512 * (nscan[0] % 3), 512 * (nscan[0] % 3) + 512)
+                        nscan[0] += 1
+                        named("z%d" % (o // 512 + 1))
+                        act(src, A(pb), AF.Copy)
                     scan(A("s", o, o + 512), src, A("m", o, o + 512), add_, mx)
-                    nscan[0] += 1
 
-        def pi(c, bank):
+        def pi(c):
+            pb = bank("pi")
             for j in range(4 * c, 4 * c + 4):
-                y, x = j >> 1, 16 + (j & 1)
-                cut()
-                mms(A(bank, j & 3, 512, 4), [(A("BD", 128 * x, 128 * x + 128), A("penT", 128 * y, 128 * y + 128)),
-                                             (ID, A("s", 1024 * j + 7, 1024 * j + 1024, 8))])
-            lin(A("W", 1024 + 512 * c, 1536 + 512 * c), A(bank), 1.0, -up)
+                y, x = j >> 1, 7 + 8 * (j & 1)
+                named(None, j & 3 > 0)
+                mms(A(pb, j & 3, 512, 4), [(A("BD", 128 * x, 128 * x + 128), A("penT", 128 * y, 128 * y + 128)),
+                                           (ID, A("s", 1024 * j + 7, 1024 * j + 1024, 8))])
+            lin(A("W", 1024 + 512 * c, 1536 + 512 * c), A(pb), 1.0, -up)
 
         def hashes(c):
-            q0, q1, hb = 32 * c, 32 * c + 32, ps[4 + c]
-            win = [[A("WW", 15 - 4 * l2 - jj, 143 - 4 * l2 - jj) for l2 in range(4)] for jj in range(4)]
-            if c == 0:
-                mms(A(hb, 0, 32), [(win[jj][l2], A("W", 1024 + 4 * l2 + jj, 1536, 16)) for jj in range(4) for l2 in range(4)])
-            else:
-                pairs = []
-                for y in (2, 3):
-                    pairs += [(A("WP", 14 - 4 * l2 - 2 * (y & 1), 142 - 4 * l2 - 2 * (y & 1)),
-                               A("penT", 128 * y + l2, 128 * y + 128, 4)) for l2 in range(4)]
-                    for j in (2 * y, 2 * y + 1):
-                        pairs += [(win[j & 3][l2], A("s", 1024 * j + 8 * l2 + 7, 1024 * j + 1024, 32)) for l2 in range(4)]
-                for k, (lhsT, rhs) in enumerate(pairs):
-                    if k in (12, 20):
-                        cut()
-                    mm(A(hb, 0, 32), lhsT, rhs, k == 0, k == 23)
-            ts(A("ui", q0, q1), A(hb, 0, 32), A("wsf", 1, 2) if t and c else A("wsf", 4, 5), add_)
+            q0, q1, hb, pairs = 32 * c, 32 * c + 32, A(bank("ha"), 0, 32), []
+            for y in (2 * c, 2 * c + 1):
+                pairs += [(A("WP", 14 - 4 * l2 - 2 * (y & 1), 142 - 4 * l2 - 2 * (y & 1)),
+                           A("penT", 128 * y + l2, 128 * y + 128, 4)) for l2 in range(4)]
+                for j in (2 * y, 2 * y + 1):
+                    pairs += [(A("WW", 15 - 4 * l2 - (j & 3), 143 - 4 * l2 - (j & 3)),
+                               A("s", 1024 * j + 8 * l2 + 7, 1024 * j + 1024, 32)) for l2 in range(4)]
+            for k, (lhsT, rhs) in enumerate(pairs):
+                if k in (8, 12, 20):
+                    named(None, True)
+                mm(hb, lhsT, rhs, k == 0, False)
+            moved("ui%d" % c, A("ui", q0, q1), hb, A("wsf", 1, 2) if t else A("wsf", 4, 5))
             ts(A("u", q0, q1), A("ui", q0, q1), 4095, band)
             ts(A("u32", q0, q1), A("u", q0, q1), 32.0, add_)
             tt(A("uw", q0, q1), A("u", q0, q1), A("u32", q0, q1), mul)
             ts(A("h", q0, q1), A("uw", q0, q1), 5, shr, 4095, band)
             cp(A("HL", q0, q1), A("h", q0, q1))
-            ts(A("hq", q0, q1), A("h", q0, q1), -2048.0, add_)
+            moved("hq%d" % c, A("hq", q0, q1), A("h", q0, q1), -2048.0)
 
         def known(c):
-            q0, q1, o0, o1, sb = 32 * c, 32 * c + 32, 512 * c, 512 * c + 512, A(ps[4])
+            q0, q1, o0, o1 = 32 * c, 32 * c + 32, 512 * c, 512 * c + 512
             PI = A("W", 1024 + o0, 1024 + o1)
-            if OPT["own"][c] == "act":
-                act(A("xh", o0, o1), IND(XWIN, A("HL", q0, q1)), AF.Copy)
-                mms(sb, [(NID, PI), (ID, A("xh", o0, o1))])
-                act(A("ad2", o0, o1), sb, AF.Abs)
+            if c == 0:
+                named("d20")
+                tt(A("d2", 0, 512), IND(XWIN, A("HL", 0, 32)), PI, sub_)
+                named("ad20")
+                act(A("ad2"), A("d2", 0, 512), AF.Abs)
             else:
-                for q, o, n_ in ([(q0, o0, 256), (q0 + 16, o0 + 256, 256)] if c else [(q0, o0, 512)]):
-                    tt(A("d2", o, o + n_), IND(XWIN, A("HL", q, q + n_ // 16)), A("W", 1024 + o, 1024 + o + n_), sub_)
-                    if OPT["own"][c] == "abs":
-                        act(A("ad2", o, o + n_), A("d2", o, o + n_), AF.Abs)
-                    else:
-                        ts(A("ad2", o, o + n_), A("d2", o, o + n_), 0.0, mx)
-            if c in OPT["rec_dve"]:
-                tt(A("sum", o0, o1), IND(A(XR), A("HL", q0, q1)), PI, add_)
-                lin(A("W", 2048 + o0, 2048 + o1), A("sum", o0, o1), 0.5, -0.25 if t else 63.75)
-                return
+                for hf in range(2):
+                    o, src = 512 + 256 * hf, IND(XWIN, A("HL", 32 + 16 * hf, 48 + 16 * hf))
+                    named("d21" + "b" * hf)
+                    tt(A("d2", o, o + 256), src, A("W", 1024 + o, 1280 + o), mn)
+                    named("xh1" + "b" * hf)
+                    act(A("xh", o, o + 256), src, AF.Copy)
             lin(A("rec", o0, o1), IND(A(XR), A("HL", q0, q1)), 1.0, 0.0 if t else 128.0)
-            mms(sb, [(ID, PI), (ID, A("rec", o0, o1))])
-            lin(A("W", 2048 + o0, 2048 + o1), sb, 0.5, -0.25)
+            pb = A(bank("me"))
+            named("mp%d" % c)
+            mm(pb, ID, PI, True, False)
+            named("mr%d" % c)
+            mm(pb, ID, A("rec", o0, o1), False, True)
+            lin(A("W", 2048 + o0, 2048 + o1), pb, 0.5, -0.25)
 
         subs(0)
         cross(0, 1)
         cross(1, 2)
         misfits(0)
-        subs(1)
-        four = OPT["four"]
-        cross(2, 4 if four else 3)
-        greatest(0)
         misfits(1)
-        if not four:
-            cross(3, 4)
+        subs(1)
+        cross(2, 4)
+        greatest(0)
         greatest(1)
-        same([hf for hf in late if hf or not four])
-        misfits4(1) if four else misfits(2)
-        same([hf for hf in late if four and not hf])
-        pi(0, ps[4])
+        misfits4()
+        pi(0)
         hashes(0)
         known(0)
         greatest(2)
-        if not four:
-            misfits(3)
         greatest(3)
         pens = [(A("penT", 128 * y, 128 * y + 128), A("BLK", 0, 128, 2)) for y in range(4)]
-        mms(A(ps[7], 0, 64), pens)
-        lin(A("yn"), A(ps[7], 0, 64), 1.0 / 64, 64.4375)
-        mms(A(ps[7], 128, 192), pens + [(A("N64"), A("yn"))])
-        ST8 = ND("st", slice(None), slice(0, 8))
-        act(ST8, A(ps[7], 128, 192), AF.Sigmoid, A("thr"), 256.0, acc=None if last else A("acc"))
-        mm(A(ps[7], 264, 272), A("vr"), A("OBh"), True, False)
-        mm(A(ps[7], 264, 272), A("N2K"), ND("st", slice(None), 0), False, False)
+        pb = A(bank("yn"), 0, 64)
+        mms(pb, pens)
+        lin(A("yn"), pb, 1.0 / 64, 64.4375)
+        pb = A(bank("st"), 0, 64)
+        mms(pb, pens + [(A("N64"), A("yn"))])
+        act(ND("st", slice(None), slice(0, 8)), pb, AF.Sigmoid, A("thr"), 256.0, acc=None if last else A("acc"))
+        pb = bank("ld")
+        mm(A(pb, 0, 8), A("vr"), OBb, True, False)
+        mm(A(pb, 0, 8), A("N2K"), ND("st", slice(None), 0), False, False)
         for g_ in range(8):
-            mm(A(ps[7], 264 + g_, 265 + g_), A("EQm", 128 * g_, 128 * g_ + 128), ND("st", g_, slice(0, 1)), False, g_ == 7)
-        act(A("ld"), A(ps[7], 264, 272), AF.Relu, col("d2k"), -1.0)
-        mms(A(ps[6], 0, 128), [(A("FW", 6 - 2 * y, 134 - 2 * y), A("penT", 128 * y, 128 * y + 128)) for y in range(4)]
+            mm(A(pb, g_, g_ + 1), A("EQm", 128 * g_, 128 * g_ + 128), ND("st", g_, slice(0, 1)), False, g_ == 7)
+        act(A("Zl", 15, 143, 16), A(pb, 0, 8), AF.Relu, col("d2k"), -1.0)
+        pb = A(bank("sf"), 0, 128)
+        mms(pb, [(A("FW", 6 - 2 * y, 134 - 2 * y), A("penT", 128 * y, 128 * y + 128)) for y in range(4)]
             + [(ND("st", slice(None)), A("I2K"))])
-        act(A("sf"), A(ps[6], 0, 128), AF.Sigmoid, col("sfb"), 256.0)
-        tt(A("Rs"), IND(A("ld"), A("LREP")), A("CM"), mul)
-        mms(A(ps[7], 272, 280), [(NID, A("DL")), (A("Rs"), OBb)])
-        ts(A("SL"), A(ps[7], 272, 280), -1.0, mul)
+        act(A("sf"), pb, AF.Sigmoid, col("sfb"), 256.0)
+        pb = A(bank("sl"), 0, 8)
+        mms(pb, [(ID, A("DL"))] + lanes("Zl", NID))
+        moved("SL", A("SL"), pb)
         if not last:
-            mm(A(ps[7], 256, 257), A("ONE", 0, 128), A("acc"))
-            lin(A("yq"), A(ps[7], 256, 257), -1.0 / 64, 128 + 1100 - 0.4375)
-            lin(A("af"), A(ps[7], 256, 257), -32.0, 256 * (4096.0 + 14.5 + 1024 + 8800))
+            pb = A(bank("ac"), 0, 1)
+            mm(pb, A("ONE", 0, 128), A("acc"))
+            lin(A("yq"), pb, -1.0 / 64, 128 + 1100 - 0.4375)
+            lin(A("af"), pb, -32.0, 256 * (4096.0 + 14.5 + 1024 + 8800))
             lin(A("thr"), A("yq"), -2048.0, A("af"))
-        pi(1, ps[0])
+        pi(1)
         hashes(1)
         known(1)
-        mm(A(ps[1], 64, 72), A("N1h"), A("IDb", 8 + t, 128, 16))
-        mm(A(ps[1], 0, 64), ID32, A("JK"), True, False)
-        mm(A(ps[1], 0, 64), A("I4M"), ST8, False, False)
+        pb = bank("ky")
+        mm(A(pb, 0, 72), ID32, A("JK"), True, False)
+        mm(A(pb, 0, 72), A("I8M"), ND("st", slice(None), slice(0, 9)), False, False)
+        mm(A(pb, 8, 72, 9), A("N1h"), A("IWh", 40 + t, 160, 16), False, False)
         for j in range(8):
             o = 1024 + 512 * (j >> 2)
             if j == 4:
                 cut()
-            mm(A(ps[1], j, 64, 8), A("W", o + (j & 3), o + 512, 4), A("OBk"), False, False)
-            mm(A(ps[1], j, 64, 8), ID, ND("Zs", j >> 1, slice(7, 64, 8), j & 1), False, j == 7)
-        scan(A("k4"), A("RS"), A(ps[1], 0, 64), mul, mx)
-        tt(A("gi"), A("k4", 7, 64, 8), A(ps[1], 64, 72), mx)
-        ts(A("go"), A("gi"), 2047, band)
-        tt(A("Rv"), IND(A("go"), A("LREP")), A("CM"), mul)
-        mm(A(ps[1], 72, 80), A("Rv"), OBb)
+            mm(A(pb, j, 72, 9), A("W", o + (j & 3), o + 512, 4), A("OBk"), False, False)
+            mm(A(pb, j, 72, 9), ID, ND("Zs", j >> 1, slice(7, 64, 8), j & 1), False, j == 7)
+        scan(A("k4"), A("RS"), A(pb, 0, 72), mul, mx)
+        ts(A("kr"), A("k4", 8, 72, 9), BIG, add_, BIG, sub_)
+        tt(A("Zv", 15, 143, 16), A("k4", 8, 72, 9), A("kr"), sub_)
+        pb = A(bank("vl"), 0, 8)
+        mms(pb, lanes("Zv", ID))
+        moved("VL", A("yvf" if last else "VL"), pb)
         if not last:
-            cp(A("VL"), A(ps[1], 72, 80))
-        else:
-            cp(A("yvf"), A(ps[1], 72, 80))
-            dma("sp", HB("yv"), A("yvf"), 4096)
-        mm(A(ps[6], 128, 256), NID, A("N1h"), True, False)
+            pb = A(bank("vr"), 0, 128)
+            mm(pb, A("Zv", 15, 143), ID)
+            moved("vr", A("vr"), pb)
+        pb = bank("nm")
+        mm(A(pb, 0, 128), NID, A("N1h"), True, False)
         for y in range(4):
-            mm(A(ps[6], 128, 256), ND("Zs", y, slice(3 - y, 67 - y)), ID, False, False)
+            mm(A(pb, 0, 128), ND("Zs", y, slice(3 - y, 67 - y)), ID, False, False)
         for c in range(2):
             for l2 in range(4):
-                mm(A(ps[6], 128 + l2, 256, 4), A("SH", 144 * l2 + 4 - 4 * c, 144 * l2 + 132 - 4 * c),
-                   A("hq", 32 * c, 32 * c + 32), False, c == 1 and l2 == 3)
+                mm(A(pb, l2, 128, 4), SH[c][l2], A("hq", 32 * c, 32 * c + 32), False, c == 1 and l2 == 3)
             cut()
-        tt(A("e2"), A(ps[6], 128, 256), A("sf"), mul)
+        tt(A("e2"), A(pb, 0, 128), A("sf"), mul)
         q = t % 4
-        mms(A(ps[6], 256, 384), [(ID, A("N1h")), (NID, A("NMh", 128 * q, 128 * q + 128)), (ID32, A("e2"))])
-        cut()
-        pairs = [(A("I2K"), A("sf"))]
-        for j in range(8):
-            o = 512 * (j >> 2)
-            if OPT["own"][j >> 2] == "relu":
-                pairs += [(A("NOBW", 15 - j, 143 - j), A("d2", o + (j & 3), o + 512, 4)),
-                          (A("OBW2", 15 - j, 143 - j), A("ad2", o + (j & 3), o + 512, 4))]
-            else:
-                pairs += [(A("OBW", 15 - j, 143 - j), A("ad2", o + (j & 3), o + 512, 4))]
-        pairs.sort(key=lambda x: (x[1][2] >= 512, x[1][1] == "ad2"))
-        half = len(pairs) - 4
-        for k, (lhsT, rhs) in enumerate(pairs):
-            if k == half:
-                cut()
-            mm(A(ps[3], 0, 128), lhsT, rhs, k == 0, k == len(pairs) - 1)
-        over(A("nask"), A(ps[3], 0, 128), 2048.0 + 24.5, False)
-        tt(A("t2"), A(ps[6], 256, 384), A("nask"), mul)
-        tt(IND(A("E"), A("SL")), A("t2"), A("NN", 128 * q, 128 * q + 128), add_)
+        nb = A(bank("n2"), 0, 128)
+        mms(nb, [(ID, A("N1h")), (NID, A("NMh", 128 * q, 128 * q + 128)), (ID32, A("e2"))])
+        pb = bank("ak")
+        mm(A(pb, 0, 128), A("I2K"), A("sf"), True, False)
+        terms = [("ad2", 0, 0, "OBW", 0, 128), ("W", 1, 1536, "OBW", 0, 128)]
+        terms += [(name, 1, 512, win, 64 * hf, 64 * hf + 64) for name, win in (("xh", "OBW"), ("d2", "OBW2"))
+                  for hf in range(2)]
+        for name, c, at, win, l0, l1 in terms:
+            named("k%s%d%s" % (name, c, "b" if l0 else ""), True)
+            for jj in range(4):
+                mm(A(pb, l0, l1), A(win, 15 - 4 * c - jj, 143 - 4 * c - jj), A(name, at + 4 * l0 + jj, at + 4 * l1, 4),
+                   False, False)
+        under(A("nask"), A(pb, 0, 128), 2048.0 + 24.5)
+        tt(A("t2"), nb, A("nask"), mul)
+        tt(IND(A("E"), A("SL")), A("t2"), A("NN", 128 * q, 128 * q + 128), sub_)
         scan(A("incl", 1, 129), A("ONES"), A("nask"), mul, add_)
-        mms(A(ps[2], 0, 64), [(A("M3W", 8 - 8 * l0, 136 - 8 * l0), A("nask", l0, 128, 2)) for l0 in range(2)])
+        pb = A(bank("u1"), 0, 64)
+        mms(pb, [(M3[l0], A("nask", l0, 128, 2)) for l0 in range(2)])
+        tt(A("u1"), pb, A("C1n"), mul)
+        pb = A(bank("tq"), 0, 64)
+        mm(pb, ID, A("nL"), True, False)
+        for name, win in (("nask", "M2W"), ("incl", "M1W")):
+            for l0 in range(2):
+                mm(pb, A(win, 8 - 8 * l0, 136 - 8 * l0), A(name, l0, 128, 2), False, False)
+            cut()
+        under(A("tq"), pb, 255.5)
+        pb = A(bank("cl"), 0, 64)
+        mm(pb, ID, A("PL"), True, False)
+        mm(pb, ID, A("u1"), False, False)
         cut()
-        mms(A(ps[3], 128, 192), [(ID, A("nL"))]
-            + [(A("M2W", 8 - 8 * l0, 136 - 8 * l0), A("nask", l0, 128, 2)) for l0 in range(2)]
-            + [(A("M1W", 8 - 8 * l0, 136 - 8 * l0), A("incl", l0, 128, 2)) for l0 in range(2)])
-        tt(A("u1"), A(ps[2], 0, 64), A("C1n"), mul)
-        ts(A("tq"), A(ps[3], 128, 192), 255.5, OP_.is_lt, 0.5, mul)
-        mms(A(ps[2], 64, 128), [(ID, A("PL")), (ID, A("u1")), (A("I2K"), A("tq"))])
-        cp(A("CL"), A(ps[2], 64, 128))
-        xa = 512 if last else OPT["xa"]
-        XO = "X0" if last else "X"
-        lin(A(XO, blk, blk + xa), IND(A("W"), A("CL", 0, xa // 16)), 1.0, -128.0 if last else 0.0)
-        if xa < 1024:
-            ts(A(XO, blk + xa, blk + 1024), IND(A("W"), A("CL", xa // 16, 64)), -128.0 if last else 0.0, add_)
+        mm(pb, A("I1K"), A("tq"), False, True)
+        moved("CL", A("CL"), pb)
+        if not last:
+            lin(A("X", blk, blk + 1024), IND(A("W"), A("CL")), 1.0)
+        else:
+            lin(A("X0", 0, 512), IND(A("W"), A("CL", 0, 32)), 1.0, -128.0)
+            ts(A("X0", 512, 1024), IND(A("W"), A("CL", 32, 64)), -128.0, add_)
     dma("sp", HB("ye", 0, 960), A("E", 0, 960), 1000000)
     dma("sp", HB("ye", 960, V), A("E", 960, V), 1000000)
+    dma("sp", HB("yv"), A("yvf"), 4096)
     dma("sp", HB("yx", 0, 1024), A("X0", 0, 1024), 262144)
     return ops
 
@@ -719,7 +676,7 @@ ASYNC = ("dma", "send", "send2", "arrive")
 
 
 def dependencies(flat):
-    ops, seen = [], {}
+    ops, seen, user = [], {}, {}
     for o in flat:
         if ops and ops[-1]["piece"] == o["piece"]:
             p = ops[-1]
@@ -727,7 +684,7 @@ def dependencies(flat):
             p["ns"] += o["ns"]
             p["hold"] += o["hold"]
         else:
-            p = dict(o, calls=[o], hard=set(), soft=set())
+            p = dict(o, calls=[o], hard=set(), soft=set(), opens=None, closes=None)
             ops.append(p)
         k = len(ops) - 1
         reads = [s for x in o["ins"] for s in _spans(x)]
@@ -742,6 +699,10 @@ def dependencies(flat):
         for isw, group in ((False, reads), (True, writes)):
             for name, lo, hi in group:
                 psum = SPEC[name][0] == "psum"
+                if psum:
+                    if name not in user:
+                        p["opens"] = name
+                    user[name] = k
                 keep = []
                 for rec in seen.get(name, []):
                     k2, w2, lo2, hi2 = rec
@@ -750,7 +711,10 @@ def dependencies(flat):
                         continue
                     same = ops[k2]["eng"] == o["eng"] and o["kind"] not in ASYNC and ops[k2]["kind"] not in ASYNC
                     if psum:
-                        p["soft" if same else "hard"].add(k2)
+                        if not (p["any"] and ops[k2]["any"]):
+                            p["soft" if same else "hard"].add(k2)
+                        if p["any"]:
+                            keep.append(rec)
                         continue
                     if lo < hi2 and lo2 < hi and (isw or w2):
                         p["hard"].add(k2)
@@ -760,189 +724,97 @@ def dependencies(flat):
                 if (k, isw, lo, hi) not in keep:
                     keep.append((k, isw, lo, hi))
                 seen[name] = keep
+    for name, k in user.items():
+        ops[k]["closes"] = name
     send = {o["par"]: k for k, o in enumerate(ops) if o["kind"] in ("send", "send2")}
     count = {}
     for o in ops:
         o["soft"] -= o["hard"]
         o["time"] = set([send[o["par"]]]) if o["kind"] == "arrive" else set()
         out = o["out"]
-        key = o["eng"] + ":" + (out[1] if out[0] != "ind" else out[1][1] + "!") if out and o["eng"] else "-"
-        key = {"act:X0": "act:X", "dve:yvf": "dve:VL"}.get(key, key)
+        key = o["eng"][0] + (out[1].split(".")[0] if out[0] != "ind" else out[1][1] + "!") if out and o["eng"] else "-"
+        key = "g" + key[1:] if o["eng"] == "pool" else "aX" if key == "aX0" else key
         if o["kind"] == "send":
             count.clear()
+            first = send[o["par"]]
+        if o["kind"] == "send2":
+            o["soft"].add(first)
+        if o["tag"]:
+            o["key"] = key[0] + o["tag"]
+            continue
         count[key] = count.get(key, 0) + 1
         o["key"] = "%s#%d" % (key, count[key])
     return ops
 
 
-def schedule(ops, first, start, units, steps, slack, rng):
+ROUND = """
+dN1h#1 pvr#1' ptq#1' ptq#2' pmp1' atq#1' pmr1' pu1#1' plp#1 du1#1' avr' dLP dN2h#1 dN2h#2 dTh#1 aW#4' pcl#1' pcl#2'
+aCL' aX#1' pac#1' peq#1 dTh#2 aXP#1 aXP#2 pal#1 pop#1 dEQ#1 pal#2 pal#3 pal#4 aAL0 aa5 dOPa pop#2 dm0 aa7 pop#3 dOP0
+dm0b dm1 dm2b pdf#1 pal#5 pal#6 pal#7 pal#8 aAL1 pcr0 pcr1 dal0 pda15 dm2 pcr2 aa1 dsc0 pda05 pz0 dOP1 aa3 dZs0 ayq#1'
+pbl0 aBL0 aaf#1' dm3 pda01 dm4 pcr3 dal1 ab0 aa11 pdb01 pdb15 aad01 pdb05 aad05 pda11 pda31 dsc1 dZs1 pbl1 aBL1 dm4b
+dm5 dm6 pda35 pdb11 pda25 pz01 pz05 aad15 ab1 pcr4 dm7 aad11 pda21 pdb35 aad35 pdb21 pdb25 pz15 pdaq3 aad25 pz11 aP#1
+pdb31 pz1 aad21 pdaq4 ppt#1 apenT#1 pz25 aad31 pcr5 dal2 pz21 pmx#1 ds#1 pcr6 pcr7 dal3 dsc2 pz35 pmx#2 dsc3 dZs2 aa9
+pz31 dZs3 pmx#4 pmx#3 pbl2 pbl3 aP#2 ppt#2 ds#2 pdaq1 aBL2 apenT#2 pha#1 ds#3 ds#4 pdaq2 pmx#5 ab2 pmx#7 pdbq3 pdbq4
+pdbq1 aa13 ds#5 aadq3 pmx#8 aadq4 peq#2 aadq1 daq6 dadq6 pdaq5 pdbq5 aadq5 pdbq2 aadq2 pz4 pzadq6 pzadq1 daq7 ds#7
+pzadq3 pmx#6 dadq7 pzaq7 pzaq6 pzadq4 pzadq5 pzadq7 pzadq2 aP#3 ppi#1 ds#6 pha#2 ds#8 athr#1' dEQ#2 aP#4 pha#3 ppt#3
+ppi#2 pha#4 ppi#3 apenT#3 dui0 du#1 du32#1 ppt#4 pmx#10 duw#1 apenT#4 pmx#9 az10 pmx#12 pyn#1 ayn#1 pmx#11 ds#9 dh#1
+pmx#16 pst#1 ds#10 az12 pmx#14 pmx#13 ast#1 pmx#15 ds#11 az16 pld#1 psf#1 ppi#4 ds#12 ppi#5 ds#13 dHL#1 pha#5 az14
+pha#6 aZl#1 ppi#6 psl#1 ds#16 asf#1 ds#14 pha#7 aW#1 ds#15 pha#8 ppi#7 dd20 ppi#8 arec#1 aui1 pmp0 du#2 du32#2 duw#2
+dh#2 dHL#2 dhq1 pky#1 pmr0 pak#1 ahq0 aW#3 pkW1 pnm#1 pnm#2 pky#2 aad20 dd21 axh1b axh1 pkad20 pkxh1b pkd21 dd21b
+de2#1 dk4#1 dkr#1 dSL dZv#1 pkd21b arec#2 pkxh1 pn2#1 dnask#1 dt2#1 dincl#1 aW#2 pvl#1 dE!#1 dVL
+"""
+LAST = ("pn2#1 pmp1 dnask#1 dt2#1 dincl#1 pu1#1 ptq#1 aW#2 pmr1 ptq#2 dE!#1 du1#1 atq#1 pcl#1 aW#4 pcl#2 aCL aX#1 "
+        "pvl#1 dX0#1 dVL").split()
+FIRST = "IC IW r rg rgw ONES PM PM#2 sc PM#3 PM#4 SelS rj".split()
+LOOK = 120.0
+
+
+def serial(ops, text):
     n = len(ops)
-    hold, ns, eng = [o["hold"] for o in ops], [o["ns"] for o in ops], [o["eng"] for o in ops]
-    pred = [[(d - first, hold[d - first]) for d in o["soft"] if d >= first]
-            + [(d - first, ns[d - first] + (LAG[1] if eng[d - first] == o["eng"] else LAG[0]))
-               for d in o["hard"] | o["time"] if d >= first] for o in ops]
-    back = [[] for _ in ops]
-    for k in range(n):
-        for d, lag in pred[k]:
-            back[d].append((k, hold[k] + lag - hold[d]))
-
-    def place(key, pre, rel, fwd):
-        key = list(key)
-        for k in (range(n) if fwd else range(n - 1, -1, -1)):
-            for d, _ in pre[k]:
-                if key[d] >= key[k]:
-                    key[k] = key[d] + 1e-3
-        st = [0.0] * n
-        busy = {e: ([], []) for e in ENG}
-        for k in sorted(range(n), key=lambda q: key[q]):
-            at = rel[k]
-            for d, lag in pre[k]:
-                if st[d] + lag > at:
-                    at = st[d] + lag
-            if eng[k] is not None:
-                lo, hi = busy[eng[k]]
-                if hi and hi[-1] > at:
-                    a, b = 0, len(hi)
-                    while a < b:
-                        mid = (a + b) // 2
-                        if hi[mid] <= at:
-                            a = mid + 1
-                        else:
-                            b = mid
-                    while a < len(lo) and lo[a] < at + hold[k]:
-                        at = hi[a]
-                        a += 1
-                    lo.insert(a, at)
-                    hi.insert(a, at + hold[k])
-                else:
-                    lo.append(at)
-                    hi.append(at + hold[k])
-            st[k] = at
-        return st
-    zero, tail = [0.0] * n, [ns[k] - hold[k] for k in range(n)]
-
-    def justify(st):
-        r = place([-(st[k] + hold[k]) for k in range(n)], back, tail, False)
-        return place([-(r[k] + hold[k]) for k in range(n)], pred, zero, True)
-
-    def span(st):
-        return max(st[k] + ns[k] for k in range(n)) + OPT["mean"] * sum(st) / n
-    cur = place(start, pred, zero, True)
-    best, cost = cur, span(cur)
-    low = cost
-    shifts = (rng.choice([-1.0, 1.0], (steps, 2)) * np.exp(rng.uniform(5.0, 8.7, (steps, 2)))).tolist()
-    picks = rng.integers(len(units), size=(steps, 2)).tolist()
-    unit = {}
-    for u in units:
-        for k in u:
-            unit.setdefault(k, u)
-
-    def queued(st):
-        ends = {(eng[k], round(st[k] + hold[k], 2)): k for k in range(n)}
-        k, pairs = max(range(n), key=lambda q: st[q] + ns[q]), []
-        while k is not None:
-            u = [d for d, lag in pred[k] if st[d] + lag > st[k] - 0.01]
-            v, k = k, u[0] if u else ends.get((eng[k], round(st[k], 2)))
-            if not u and k in unit and v in unit:
-                pairs.append((k, v))
-        return pairs
-    pairs = queued(cur)
-    for it in range(steps):
-        key = list(cur)
-        if it % 3 and pairs:
-            u, v = pairs[picks[it][0] % len(pairs)]
-            far = abs(shifts[it][0]) if shifts[it][1] > 0 else 1.0
-            for k in unit[v] if it % 3 == 1 else unit[u]:
-                key[k] += cur[u] - cur[v] - far if it % 3 == 1 else cur[v] - cur[u] + far
+    edge = [k for k, o in enumerate(ops) if o["kind"] == "send"] + [n]
+    names = text.split()
+    place = {w.rstrip("'"): i + len(names) * w.count("'") for i, w in enumerate(names)}
+    key, listed = [0.0] * n, set()
+    for k, o in enumerate(ops):
+        t = sum(1 for e in edge if e <= k) - 1
+        if t == RO - 1 and o["key"] in LAST:
+            listed.add(k)
+            key[k] = len(names) * t + place[LAST[0]] + LAST.index(o["key"]) / 100
+        elif t >= 0 and o["key"] in place:
+            listed.add(k)
+            key[k] = len(names) * t + place[o["key"]]
         else:
-            for k in units[picks[it][1]]:
-                key[k] += shifts[it][1]
-        for k in range(n - 1, -1, -1):
-            if key[k] < cur[k]:
-                for d, lag in pred[k]:
-                    if key[d] > key[k] - lag:
-                        key[d] = key[k] - lag
-        st = place(key, pred, zero, True)
-        if it % 5 == 0:
-            st = justify(st)
-        c = span(st)
-        if c <= cost + slack * (1.0 - it / steps):
-            cur, cost, pairs = st, c, queued(st)
-            if c < low:
-                best, low = st, c
-    return best
+            key[k] = -1.0
+        for d in o["hard"] | o["soft"] | o["time"]:
+            key[k] = max(key[k], key[d] + 1e-4)
+    return sorted(range(n), key=lambda k: (key[k], k)), listed
 
 
-ORDER = {
-    "dve": "N1h LP EQ N2h Th OP EQ Th OP AL m m m AL m OP m m sc Zs m BL m m m m sc Zs BL s s a ad s s a ad s s s s "
-           "ui u u32 uw h Zh HL s s s s Rs s s SL s s ui u u32 uw h Zh k4 HL gi d2 d2 go e2 Rv nask VL incl t2 E! u1 "
-           "tq CL",
-    "act": "vr N2h XP XP a a a a al a b ad ad ad ad ad ad ad al P a penT b a ad ad ad ad ad P W penT yn xh st ad2 ld "
-           "sf W rec ad2 ad2 rec W W yq thr X"}
+def allot(ops, seq):
+    free, held, lastuse, final = list(BANKS), {}, {}, {}
+    for k in seq:
+        if ops[k]["eng"] == "pe":
+            final[ops[k]["out"][1]] = ops[k]["calls"][-1]
+    for c in final.values():
+        c["par"] = (c["par"][0], True)
+    for k in seq:
+        o = ops[k]
+        if o["opens"]:
+            b = free.pop(0)
+            held[o["opens"]] = b
+            SPEC[o["opens"]] = SPEC[o["opens"]][:3] + (b, 0)
+            if b in lastuse:
+                d, name = lastuse[b]
+                o["soft" if ops[d]["eng"] == o["eng"] else "hard"].add(d)
+                if name.split(".")[0] == o["opens"].split(".")[0]:
+                    o["calls"] = [c for c in o["calls"] if not c["once"]]
+        if o["closes"]:
+            free.append(held[o["closes"]])
+            lastuse[held[o["closes"]]] = (k, o["closes"])
 
 
-def first_keys(ops, lo, edge):
-    key = {}
-    for t, (a, b) in enumerate(zip(edge[:-1], edge[1:])):
-        at = {ops[k]["key"]: k for k in range(a, b)}
-        for e, text in ORDER.items():
-            time, seen = 36000.0 * t, {}
-            for w in text.split():
-                seen[w] = seen.get(w, 0) + 1
-                k = at.get("%s:%s#%d" % (e, w, seen[w]))
-                if k is not None:
-                    key[k] = time
-                    time += ops[k]["ns"] * 1.1
-    out = [key.get(k, 1e9) for k in range(lo, edge[-1])]
-    for k in range(edge[-1] - 1, lo - 1, -1):
-        for d in ops[k]["hard"] | ops[k]["soft"] | ops[k]["time"]:
-            if d >= lo and d not in key:
-                out[d - lo] = min(out[d - lo], out[k - lo] - ops[d]["ns"])
-    return out
-
-
-def searched(steps=STEPS, seed=SEED):
-    ops = dependencies(program())
-    rng = np.random.default_rng(seed)
+def arrange(ops, seq, listed):
     n = len(ops)
-    edge = [k for k, o in enumerate(ops) if o["kind"] == "send"] + [n]
-
-    def alike(lo, hi):
-        groups = {}
-        for k in range(lo, hi):
-            if ops[k]["eng"] in ("dve", "act", "pe"):
-                groups.setdefault(ops[k]["key"], []).append(k - lo)
-        return [groups[x] for x in sorted(groups)]
-    lo, mid, hi = edge[1:4]
-    two = schedule(ops[lo:hi], lo, first_keys(ops, lo, edge[1:4]), alike(lo, hi), steps[0], 250.0, rng)
-    at = [{ops[k]["key"]: two[k - lo] for k in range(a, b)} for a, b in ((lo, mid), (mid, hi))]
-    period = at[1]["dve:sc#2"] - at[0]["dve:sc#2"]
-    start = [float(k) for k in range(n)]
-    for t in range(RO):
-        for k in range(edge[t], edge[t + 1]):
-            x = ops[k]["key"]
-            late = at[0].get(x, 0.0) > at[0]["dve:sc#2"]
-            start[k] = 10000.0 + t * period + (at[0][x] if late else at[1].get(x, at[1]["dve:N1h#1"]) - period)
-    for k in range(edge[0] - 1, -1, -1):
-        start[k] = min([start[x] - 500.0 for x in range(k + 1, n) if k in ops[x]["hard"]] + [start[edge[1]]])
-    ends = [[k] for k in list(range(edge[1])) + list(range(edge[4], n)) if ops[k]["eng"] in ("dve", "act", "pe", "pool")]
-    start = schedule(ops, 0, start, ends + alike(edge[0], n), steps[1], 200.0, rng)
-    order = {e: sorted((k for k in range(n) if ops[k]["eng"] == e), key=lambda q: (start[q], q)) for e in ENG}
-    return order
-
-
-ROUND = {
-    "dve": "N1h#1 tq#1' LP#1 N2h#1 CL#1' Th#1 Th#2 OP#1 AL#1 EQ#1 OP#3 OP#2 m#1 m#2 m#3 m#5 al#1 sc#1 AL#2 Zs#1 m#4 BL#1 m#6 m#8 al#2 sc#2 Zs#2 m#7 BL#2 m#9 m#10 al#3 m#11 sc#3 Zs#3 s#1 al#4 sc#4 Zs#4 s#2 BL#3 s#3 s#4 a#1 a#2 s#5 ad#2 ad#1 s#6 s#7 EQ#2 s#8 s#9 s#11 ui#1 s#10 u#1 s#13 u32#1 s#12 uw#1 s#14 h#1 s#15 HL#1 s#16 d2#1 ui#2 hq#1 u#2 u32#2 uw#2 h#2 HL#2 hq#2 d2#2 d2#3 k4#1 Rs#1 gi#1 e2#1 go#1 SL#1 Rv#1 nask#1 incl#1 t2#1 VL#1 E!#1 u1#1",
-    "act": "vr#1 N2h#1 X#1' XP#1 XP#2 a#2 a#3 a#4 thr#1' a#1 b#1 a#6 ad#1 ad#2 ad#3 b#2 ad#4 P#1 ad#5 ad#6 penT#1 ad#7 ad#8 P#2 a#5 penT#2 b#3 a#7 ad#9 ad#10 ad#11 ad#12 ad#13 P#3 P#4 penT#3 penT#4 W#1 yn#1 z0#1 z1#1 z0#2 st#1 z1#2 W#3 sf#1 ad2#1 rec#1 ld#1 ad2#2 ad2#3 rec#2 W#2 yq#1 af#1 W#4"}
-ANCHOR = ("dve:m#1", "act:XP#2")
-LOOSE = ("act:vr#1", "dve:EQ#1", "dve:EQ#2")
-PERIOD, START, LOOK = 40000.0, 10000.0, 120.0
-
-
-def arrange(ops, rounds=None):
-    n = len(ops)
-    edge = [k for k, o in enumerate(ops) if o["kind"] == "send"] + [n]
-    at = [{ops[k]["key"]: k for k in range(a, b)} for a, b in zip(edge[:-1], edge[1:])]
     after = [[] for _ in ops]
     left = [0] * n
     for k, o in enumerate(ops):
@@ -951,27 +823,24 @@ def arrange(ops, rounds=None):
             lag = 0.0 if p["eng"] is None else LAG[1] if p["eng"] == o["eng"] else LAG[0]
             after[d].append((k, p["hold"] if d in o["soft"] else p["ns"] + lag))
             left[k] += 1
-    due, fixed = [None] * n, {e: [] for e in ENG}
-    for e, text in (rounds or ROUND).items():
-        names = [(e + ":" + w.rstrip("'"), w.count("'")) for w in text.split()]
-        size = [ops[at[2][x]]["hold"] for x, _ in names]
-        off = np.concatenate([[0.0], np.cumsum(size)]) * PERIOD / sum(size)
-        zero = [off[i] + PERIOD * back for i, (x, back) in enumerate(names) if x in ANCHOR][0]
-        for t in range(RO + 1):
-            for i, (x, back) in enumerate(names):
-                if 0 <= t - back < RO and x in at[t - back] and (t or x not in LOOSE):
-                    k = at[t - back][x]
-                    fixed[e].append(k)
-                    due[k] = START + PERIOD * t + float(off[i]) - zero
-    listed = set(k for e in ENG for k in fixed[e])
-    for k in range(n - 1, -1, -1):
-        if due[k] is None:
-            due[k] = min([due[x] - w for x, w in after[k]] + [START + PERIOD * RO])
-    turn = [due[k] + (0.0 if ops[k]["eng"] == "pe" else ops[k]["ns"]) for k in range(n)]
+    fixed = {e: [k for k in seq if k in listed and ops[k]["eng"] == e] for e in ENG}
+    due, free = [0.0] * n, {e: 0.0 for e in ENG}
+    for k in seq:
+        if k in listed:
+            due[k] = max(due[k], free[ops[k]["eng"]])
+            free[ops[k]["eng"]] = due[k] + ops[k]["hold"]
+        for x, w in after[k]:
+            due[x] = max(due[x], due[k] + w)
+    end = max(due) + 5000.0
+    for k in reversed(seq):
+        if k not in listed:
+            due[k] = min([due[x] - w for x, w in after[k]] + [end])
+    turn = [due[k] + ops[k]["ns"] * (-1 if ops[k]["eng"] == "sp" and k > 6 else 1) for k in range(n)]
     for k in range(n):
-        if ops[k]["eng"] == "pool" and (ops[k]["ns"] < 700 or ops[k]["kind"] == "send"):
-            turn[k] = due[k] / 100
-    ready, start = [0.0] * n, [0.0] * n
+        if ops[k]["eng"] == "pool":
+            name = ops[k]["key"][1:].replace("#1", "")
+            turn[k] = FIRST.index(name) - 99.0 if name in FIRST else due[k] / 100 if ops[k]["kind"] == "send" else due[k]
+    ready, start = [max(0.0, due[k] - 60000.0) if ops[k]["kind"] == "iota" else 0.0 for k in range(n)], [0.0] * n
     free, head = {e: 0.0 for e in ENG}, {e: 0 for e in ENG}
     pool, order = {e: [] for e in ENG}, {e: [] for e in ENG}
 
@@ -995,7 +864,8 @@ def arrange(ops, rounds=None):
             if pool[e]:
                 soon = max(free[e], min(ready[x] for x in pool[e])) + LOOK
                 d = min((x for x in pool[e] if ready[x] <= soon), key=lambda x: (turn[x], x))
-                if pick is None or due[d] < due[h] or max(free[e], ready[d]) + ops[d]["hold"] <= max(free[e], ready[h]) + 60:
+                fits = pick is not None and max(free[e], ready[d]) + ops[d]["hold"] <= max(free[e], ready[h]) + 60
+                if pick is None or due[d] < due[h] or fits:
                     pick = d
             if pick is not None and (best is None or max(free[e], ready[pick]) < best[0]):
                 best = (max(free[e], ready[pick]), e, pick)
@@ -1013,9 +883,11 @@ def arrange(ops, rounds=None):
     return order, start
 
 
-def plan():
+def plan(text=None):
     ops = dependencies(program())
-    order, start = arrange(ops)
+    seq, listed = serial(ops, text or ROUND)
+    allot(ops, seq)
+    order, start = arrange(ops, seq, listed)
     pos = {}
     for e in ENG:
         for i, k in enumerate(order[e]):

import numpy as np
from concourse.mybir import AluOpType, ActivationFunctionType

H = "float16"
V, XW, RO = 1920, 4096, 5
LAG = (220.0, 130.0)
BIG = 1.5 * 2.0 ** 35
OPT = {
    "halves": (0, 2, 4),
    "runs": ((1, 5), (5, 8)),
    "fused": (6, 7),
    "via_act": (9, 11, 13, 15),
    "a_cut": ((64, 64, 64, 32), (64, 64, 32)),
    "act": ("vr", "hq0", "AL0", "AL1", "CL", "tq", "BL0", "BL1", "BL2", "ui1"),
}

SCRATCH = {}
SPEC = {}


def _decl(where, dtype, spec):
    pool, at = "pool_" + dtype, 0
    for name, cols in spec.items():
        if isinstance(cols, tuple):
            SPEC[name] = (where, [128] + list(cols), dtype, name, 0)
            SCRATCH[name] = (where, [128] + list(cols), dtype)
        elif where == "sbuf" and cols <= 144:
            SPEC[name] = (where, [128, cols], dtype, pool, at)
            at += (cols + 15) // 16 * 16
        else:
            SPEC[name] = (where, [128, cols], dtype, name, 0)
            SCRATCH[name] = (where, [128, cols], dtype)
    if at:
        SCRATCH[pool] = (where, [128, at], dtype)


BANKS = ["ps%d" % k for k in range(8)]
_decl("psum", "float32", {b: 512 for b in BANKS})
_decl("sbuf", "bfloat16", {
    "X": XW, "X0": XW, "XR0": XW, "XR1": XW, "XR2": XW, "XR3": XW, "XR4": XW, "m": 8192, "s": 8192, "a": 7168,
    "ad": 7168, "W": 3072, "XP": 1024, "b": 1024, "d2": 1024, "ad2": 512, "rec": 1024, "al": 512, "P": 512,
    "penT": 512, "EQ": 1024, "EQm": 1024, "z": 1536, "xh": 1024, "BD": 16 * 128, "WIDE": 1024, "NWIDE": 1024,
    "rgw": 1024, "NIDb": 128, "IDa": 128, "I2K": 128, "I1K": 128, "N2K": 128, "N64": 128, "I8M": 128, "BLK": 128,
    "ONES": 128, "OBb": 8, "OB256": 8, "OB512": 8, "OBn": 8, "OBk": 8, "WW": 143, "wb": 1, "SelS": 64, "NSel": 64,
    "yn": 64, "st": (8, 16), "sf": 128, "nask": 128, "incl": 129, "tq": 64, "RS": 72, "OBW": 143, "OBW2": 143,
    "FW": 134, "M1W": 136, "M2W": 136, "tri": 136})
_decl("sbuf", H, {"N1h": 128, "N2h": 1024, "Th": 1024, "IWh": 192, "PM": 8 * 192, "vr": 128, "Zs": (4, 72, 2),
                  "NMh": 512, "Zv": 143, "Zl": 143, "DL": 8, "vh": 8, "nL": 64, "PL": 64, "u1": 64, "yq": 1, "hq": 64,
                  "WP": 142})
_decl("sbuf", "float32", {
    "E": 2048, "sc": 512, "NN": 512, "e2": 128, "t2": 128, "k4": 72, "kr": 8, "thr": 1, "acc": 1, "af": 1, "yvf": 8,
    "wf": 1, "wsf": 5, "ONE": 192, "IW": 192, "FC": 24, "MC": 4, "E16": 24, "CF": 24, "r": 160, "rg": 128, "r8": 144, "rj": 72,
    "r1k": 64, "JK": 72, "C1n": 64, "fa": 134, "m5": 136})
_decl("sbuf", "int32", {"E0": V, "vi": 8, "wi": 1, "IC": 16, "ui": 64, "u": 64, "u32": 64, "uw": 64, "h": 64, "wsi": 3})
_decl("sbuf", "uint16", {"VL": 8, "SL": 8, "LP": 128, "OP": 512, "AL": 448, "BL": 64, "HL": 64, "CL": 64})

ENG = ("pe", "dve", "act", "pool", "sp")
SEMAPHORES = (["c_" + e for e in ENG[:4]] + ["dma%d" % k for k in range(24)] + ["arr%d" % k for k in range(11)]
              + ["snt%d" % k for k in range(11)])
OP_ = AluOpType
AF = ActivationFunctionType


def A(name, c0=0, c1=None, step=1):
    return ("ap", name, c0, SPEC[name][1][1] if c1 is None else c1, step)


def ND(name, *index):
    return ("nd", name, index)


def IND(win, off):
    return ("ind", win, off)


def HB(name, c0=None, c1=None):
    return ("hbm", name, c0, c1)


def columns(x):
    if x[0] == "nd":
        shape = SPEC[x[1]][1][1:]
        return np.arange(int(np.prod(shape))).reshape(shape)[x[2]].reshape(-1)
    return np.arange(x[2], x[3], x[4])


def _n(x):
    return 16 * _n(x[2]) if x[0] == "ind" else len(columns(x))


def _two(x):
    return SPEC[x[1]][2] in ("bfloat16", "float16", "uint16")


def _spans(x):
    if not isinstance(x, tuple) or x[0] == "hbm":
        return []
    if x[0] == "ind":
        return _spans(x[1]) + _spans(x[2])
    c = columns(x)
    return [(x[1], int(c[0]), int(c[-1]) + 1)]


def program(CY=0.87, G=1.56, PE=0.44, BW=400.0):
    ops = []
    piece, nbank, tag = [0], [0], [None, False]

    def cut():
        piece[0] += 1

    def bank(use):
        name = "%s.%d" % (use, nbank[0])
        nbank[0] += 1
        SPEC[name] = ("psum", [128, 512], "float32", None, 0)
        return name

    def add(eng, kind, out, ins, par, ns, hold=None, acc=None, once=False):
        if eng != "pe" or ops[-1]["eng"] != "pe" or ops[-1]["out"][1] != out[1]:
            cut()
        ops.append({"eng": eng, "kind": kind, "out": out, "ins": ins, "par": par, "ns": ns, "acc": acc,
                    "hold": ns if hold is None else hold, "piece": piece[0], "once": once, "tag": tag[0], "any": tag[1]})
        tag[:] = [None, False]

    def named(text, anyorder=False):
        cut()
        tag[:] = [text, anyorder]

    def vcost(out, ins, rate=None):
        full = [x for x in ins if isinstance(x, tuple)]
        if out[0] == "ind":
            return 60 + 3.5 * CY * _n(out)
        if full and full[0][0] == "ind":
            return 60 + G * CY * _n(out)
        if rate is None:
            rate = 0.5 if all(_two(x) for x in [out] + [y for y in full if _n(y) > 1]) else 1.0
        return 40 + CY * max(64, rate * _n(out))

    def cp(out, in_):
        add("dve", "copy", out, [in_], None, vcost(out, [in_]))

    def ts(out, in0, s1, op0, s2=None, op1=None):
        add("dve", "ts", out, [in0, s1, s2], (op0, op1), vcost(out, [in0]))

    def tt(out, in0, in1, op):
        sb = all(x[0] == "ind" or SPEC[x[1]][0] == "sbuf" for x in (in0, in1))
        add("dve", "tt", out, [in0, in1], op, vcost(out, [in0, in1], 2.0 if sb else 1.0))

    def scan(out, d0, d1, op0, op1):
        add("dve", "scan", out, [d0, d1], (op0, op1), vcost(out, [d0, d1]))

    def mset(out, c):
        add("dve", "memset", out, [], c, vcost(out, []))

    def act(out, in_, func, bias=0.0, scale=1.0, acc=None):
        ns = (80 + G * CY * _n(out)) if in_[0] == "ind" else 60 + CY * max(64, _n(out))
        add("act", "act", out, [in_, bias, scale], func, ns, acc=acc)

    def lin(out, in_, scale, bias=0.0):
        act(out, in_, AF.Identity, bias, scale)

    def under(out, in_, bound):
        if out[1] in OPT["act"]:
            act(out, in_, AF.Sigmoid, 256.0 * bound, -256.0)
        else:
            ts(out, in_, bound, OP_.is_lt)

    def moved(name, out, in_, by=0.0):
        named(name)
        if name in OPT["act"]:
            lin(out, in_, 1.0, by)
        else:
            ts(out, in_, by, add_)

    def mm(out, lhsT, rhs, start=True, stop=True, once=False):
        f = 4 if SPEC[rhs[1]][2] == "float32" else 1
        add("pe", "mm", out, [lhsT, rhs], (start, stop), PE * f * max(64, _n(rhs)), once=once)

    def mms(out, pairs):
        for k, (lhsT, rhs) in enumerate(pairs):
            mm(out, lhsT, rhs, k == 0, k == len(pairs) - 1)

    def iota(out, pattern, base, cm):
        add("pool", "iota", out, [], (pattern, base, cm), 160 + 2 * CY * _n(out))

    def sel(out, in_, pattern, op, base, cm):
        add("pool", "sel", out, [in_], (pattern, op, base, cm), 200 + 2 * CY * _n(out))

    ndma = [0]

    def dma(q, out, in_, nbytes, accum=False):
        ins = [in_, out] if accum else [in_]
        add(q, "dma", out, ins, ("dma%d" % ndma[0], accum), 2000 + nbytes / BW, 1500 if q == "pool" else 60)
        ndma[0] += 1

    add_, sub_, mul, mx, mn = OP_.add, OP_.subtract, OP_.mult, OP_.max, OP_.min
    eq, shr, band = OP_.is_equal, OP_.arith_shift_right, OP_.bitwise_and

    dma("sp", A("vi"), HB("v0"), 4096)
    dma("sp", A("E0", 0, 960), HB("e0", 0, 960), 500000)
    dma("act", A("E0", 960, V), HB("e0", 960, V), 1000000)
    dma("sp", A("X0", 0, 2048), HB("x0", 0, 2048), 1500000)
    dma("act", A("X0", 2048, XW), HB("x0", 2048, XW), 2000000)
    dma("sp", A("wi"), HB("wt"), 512)
    cp(A("VL"), A("vi"))

    iota(A("IC", 0, 1), [[0, 1]], 0, 1)
    cols = {"p": 0}
    for name, sh, msk in (("k8", 3, 1), ("c16", 0, 15), ("g", 4, 7), ("q4", 2, 3)):
        cols[name] = len(cols)
        ts(A("IC", cols[name], cols[name] + 1), A("IC", 0, 1), sh, shr, msk, band)
    cp(A("FC", 0, len(cols)), A("IC", 0, len(cols)))

    def col(name):
        return A("FC", cols[name], cols[name] + 1)

    def newcol(name):
        cols[name] = len(cols)
        return col(name)

    mset(A("ONE"), 1.0)
    sel(A("IW"), A("ONE"), [[-1, 192]], eq, 32, 1)
    cp(A("IWh"), A("IW"))
    iota(A("r"), [[1, 160]], -16, 0)

    def run(a, b):
        return A("r", 16 + a, 16 + b)
    ts(newcol("shift"), col("k8"), 2048.0, mul, -2048.0, add_)
    ts(A("MC"), run(0, 4), col("q4"), eq)
    wide = {}

    def perm(shift, unit, ways, want):
        key = (unit, want)
        if key not in wide:
            wide[key] = 192 * len(wide)
            o = A("PM", wide[key], wide[key] + 192)
            if unit == 4 and want > 1:
                ts(o, A("IWh"), A("MC", want, want + 1), mul)
            else:
                sel(o, A("ONE"), [[-unit * ways, 192 // (unit * ways)], [1000 - unit, ways], [-1, unit]], eq,
                    32 - 1000 * want, 1)
        return A("PM", wide[key] + 32 - shift, wide[key] + 160 - shift)
    PK = [[perm(8 * (h - kind), 8, 2, kind) for h in range(2)] for kind in range(2)]
    R = [[perm(16 * (e - yy), 16, 2, yy) for yy in range(2)] for e in range(2)]
    Q = [[perm(4 * l2 - 8 - 4 * c, 4, 4, 2 + c) for l2 in range(4)] for c in range(2)]
    SH = [[perm(4 * (c - l2), 4, 4, l2) for l2 in range(4)] for c in range(2)]
    M3 = [perm(8 * l0, 8, 2, 0) for l0 in range(2)]
    ID32, ID, NID = A("IW", 32, 160), A("IWh", 32, 160), A("NIDb")
    for name, scale in (("I2K", 2048.0), ("NIDb", -1.0), ("IDa", -65.0), ("N2K", -2048.0), ("N64", -64.0),
                        ("I8M", 8388608.0), ("I1K", 1024.0)):
        lin(A(name), ID32, scale)
    iota(A("ONES"), [[0, 128]], 1, 0)
    sel(A("SelS"), A("ONE", 0, 64), [[2, 4], [16, 8], [1, 2]], eq, 8, -1)
    lin(A("NSel"), A("SelS"), -1.0)
    iota(A("rg"), [[1, 8], [0, 16]], 0, 0)
    ts(A("BLK"), A("rg"), col("g"), eq)
    OBb = A("OBb")
    ts(OBb, run(0, 8), col("g"), eq)
    for name, scale in (("OB256", 256.0), ("OB512", 512.0), ("OBn", -256.0), ("OBk", 32768.0)):
        lin(A(name), OBb, scale)
    cp(A("wf"), A("wi"))
    iota(ND("st", slice(None)), [[0, 128]], 0, 0)
    lin(newcol("sfb"), col("k8"), 256 * 2048.0, -256 * (2048.0 + 540.5))
    ts(A("E16", 0, 17), run(0, 17), col("c16"), eq)
    tt(A("CF", 0, 16), A("E16", 1, 17), A("E16", 0, 16), sub_)
    for x in range(16):
        o, factor = A("BD", 128 * x, 128 * x + 128), A("E16", x - 7, x - 6) if x % 8 == 7 else A("CF", x, x + 1)
        if x % 3 == 1:
            lin(o, A("BLK"), factor)
        else:
            ts(o, A("BLK"), factor, mul)
    iota(A("rgw"), [[1, 8], [0, 128]], 0, 0)
    ts(A("WIDE"), A("rgw"), col("g"), eq)
    ts(A("NWIDE"), A("rgw"), col("g"), eq, -1.0, mul)
    cp(A("vh"), A("vi"))
    pb = bank("v0")
    for x in range(16):
        mm(A(pb, x, 128, 16), A("IWh", 32 + x, 160 + x), A("vh"))
    lin(A("vr"), A(pb, 0, 128), A("E16", 0, 1))
    lin(A("wb"), A("wi"), 1.0)
    pb = bank("ws")
    mm(A(pb, 0, 1), A("BLK"), A("wb"))
    lin(A("wsi", 0, 1), A(pb, 0, 1), 1.0, 2048.0)
    lin(A("wsf", 1, 2), A(pb, 0, 1), -256.0, 2097152.0)
    lin(A("wsf", 4, 5), A(pb, 0, 1), -128.0, 2097152.0)
    ts(A("wsi", 1, 2), A("wsi", 0, 1), 4095, band)
    tt(A("wsf", 2, 3), A("E16", 0, 1), A("E16", 8, 9), add_)
    ts(A("wsf", 3, 4), A("wsi", 1, 2), -2048.0, add_, A("wsf", 2, 3), mul)
    mset(ND("Zs", slice(None)), 0.0)
    iota(A("incl", 0, 1), [[0, 1]], 0, 0)
    for name in ("Zv", "Zl"):
        sel(A(name), A("ONE", 0, 143), [[0, 143]], eq, 1, 0)
    iota(A("rj"), [[0, 8], [1, 9]], 0, 0)
    lin(A("rj"), A("rj"), -4096.0, 7 * 4096.0 - 2127 * 32768.0 - 8388608.0)
    sel(A("JK"), A("rj"), [[0, 8], [1, 9]], OP_.not_equal, -8, 0)
    sel(A("RS"), A("ONE", 0, 72), [[0, 8], [1, 9]], OP_.is_gt, 0, 0)
    iota(A("thr"), [[0, 1]], 256 * 4096 + 256 * 14 + 128, 0)
    lin(newcol("d2k"), col("p"), 1.0, float(V - 2048))
    ts(A("nL"), run(0, 64), 16.0, mul, col("c16"), add_)
    ts(A("DL"), A("nL", 0, 8), float(V), add_)
    lin(newcol("t0"), col("q4"), 508.0, col("c16"))
    lin(newcol("pl"), col("k8"), -1020.0, col("t0"))
    iota(A("r1k"), [[8, 64]], 1024, 0)
    lin(A("PL"), A("r1k"), 1.0, col("pl"))
    tt(A("C1n"), A("nL"), A("PL"), sub_)
    ts(A("OBW"), run(-15, 128), col("c16"), add_, col("p"), eq)
    lin(A("WW"), A("OBW"), A("wf"))
    lin(A("OBW2"), A("OBW"), -2.0)
    lin(newcol("wp"), col("k8"), -7.0, col("p"))
    ts(A("WP"), run(-14, 128), col("wp"), eq, A("wsf", 3, 4), mul)
    lin(newcol("fw"), col("g"), 16.0, col("k8"))
    act(A("fa"), run(-10, 124), AF.Abs, col("fw"), -1.0)
    ts(A("FW"), A("fa"), 4.0, eq)
    iota(A("r8"), [[1, 9], [-1000, 2], [0, 8]], 1000, 0)
    lin(newcol("nk"), col("k8"), 1.0, -1.0)
    ts(A("M1W"), A("r8", 0, 136), col("g"), eq, col("nk"), mul)
    sel(A("tri"), A("M1W"), [[1, 136]], OP_.is_gt, -8, -1)
    lin(A("m5"), A("PM", 24, 160), 512.0)
    tt(A("M2W"), A("m5"), A("tri"), add_)
    iota(A("sc"), [[1024, 4], [8, 128]], 0, 0)
    lin(newcol("cn"), col("c16"), col("nk"))
    lin(A("NN"), A("sc"), col("nk"), col("cn"))
    lin(A("NMh"), A("NN"), -1.0, col("shift"))
    sel(A("E", 0, V), A("E0"), [[0, V]], OP_.is_ge, 0, 0)
    iota(A("X", 0, 1024), [[0, 1024]], 128, 0)
    for k in range(1, 4):
        dma("sp", A("X", 1024 * k, 1024 * k + 1024), A("X", 0, 1024), 262144)
    dma("pool", A("X"), A("X0"), 2097152, True)

    def lanes(Z, rhs):
        return [(A(Z, 15 - x, 143 - x), A(rhs[1], rhs[2] + x, rhs[3], 16)) for x in range(16)]

    XWIN = A("X")
    nscan, nsend = [0], [0]
    for t in range(RO):
        blk, last = 1024 * (t % 4), t == RO - 1
        XR = "XR%d" % t
        EW, XC, up = (A("E", 0, V), XWIN, 128.0) if t else (A("E0"), A("X0"), 0.0)
        parts = [(t, blk - 1024, blk) if t % 4 else (t, 3072 if t else 0, XW)]
        if not last:
            parts += [(t + 1, a, b) for a, b in ((0, blk), (blk + 1024, XW)) if a < b]
        for k, (to, a, b) in enumerate(parts):
            par = (to, nsend[0])
            nsend[0] += 1
            add("pool", "send2" if k else "send", None, [A("X" if to else "X0", a, b)], par, 3000 + 1.5 * (b - a), 1500)
            add(None, "arrive", A("XR%d" % to, a, b), [], par, 0)
        dma("sp", A("W", 0, 1024), A("X", blk, blk + 1024), 262144)
        if t == 1:
            iota(A("X0", 1024, XW), [[0, 3072]], -128, 0)
        if last:
            dma("pool", A("X0", 1024, XW), A("X", 1024, XW), 1572864, True)
            dma("sp", HB("yx", 1024, XW), A("X0", 1024, XW), 786432)
        for hf in range(2):
            o0, o1, pb = 512 * hf, 512 * hf + 512, bank("eq")
            mm(A(pb), A("vr"), A("NWIDE", o0, o1), True, False)
            for g4 in range(4):
                g_ = 4 * hf + g4
                mm(A(pb, 128 * g4, 128 * g4 + 128), A("WIDE", 128 * g_, 128 * g_ + 128), A("vr"), False, g4 == 3)
            ts(A("EQ", o0, o1), A(pb), 0.0, eq, 2048.0, mul)
            sel(A("EQm", o0, o1), A("EQ", o0, o1), [[0, 4], [1, 128]], OP_.is_gt, 0, -1)
        ts(A("N1h"), IND(EW, A("VL")), col("shift"), add_)
        pb = bank("lp")
        mms(A(pb, 64, 128), [(PK[1][h], A("N1h", h, 128, 2)) for h in range(2)])
        mms(A(pb, 0, 64), [(A("I2K"), A("ONES", 0, 64))] + [(PK[0][h], A("N1h", h, 128, 2)) for h in range(2)])
        moved("LP", A("LP"), A(pb, 0, 128))
        for hf in range(2):
            o0, o1 = 512 * hf, 512 * hf + 512
            ts(A("N2h", o0, o1), IND(EW, A("LP", 64 + 32 * hf, 96 + 32 * hf)), col("shift"), add_)
            act(A("XP", o0, o1), IND(XC, A("LP", 32 * hf, 32 * hf + 32)), AF.Copy)
            add("dve", "tr", A("Th", o0, o1), [A("N2h", o0, o1)], None, vcost(A("Th", o0, o1), [A("N2h", o0, o1)]))
            if hf == 0:
                pb = bank("op")
                for yy in range(2):
                    mms(A(pb, yy, 32, 2), [(R[e][yy], A("Th", 16 * e, 512, 32)) for e in range(2)])
                moved("OPa", A("OP", 0, 32), A(pb, 0, 32), 2048.0)
        for c in range(2):
            pb = bank("op")
            for jj in range(4):
                lo = 32 if c == 0 and jj == 0 else 0
                for yy in range(2):
                    mms(A(pb, 64 * jj + lo + yy, 64 * jj + 64, 2),
                        [(R[e][yy], A("Th", 16 * lo + 16 * e + 4 * c + jj, 1024, 32)) for e in range(2)])
            lo = 0 if c else 32
            moved("OP%d" % c, A("OP", 256 * c + lo, 256 * c + 256), A(pb, lo, 256), 2048.0)
            pb = bank("al")
            for i in range(1, 8):
                mms(A(pb, 32 * (i - 1), 32 * i), [(Q[c][l2], A("N2h", 8 * l2 + i, 1024, 32)) for l2 in range(4)])
                if i in (3, 5, 6):
                    cut()
            moved("AL%d" % c, A("AL", 224 * c, 224 * c + 224), A(pb, 0, 224))
        df = bank("df")
        for pos in range(8):
            pairs = [(A("N2h", 7 - pos, 1024, 8), A("SelS"))]
            if pos < 7:
                pairs.append((A("N2h", 6 - pos, 1024, 8), A("NSel")))
            mms(A(df, pos, 512, 8), pairs)

        def subs(c):
            k = 224 * c
            for width in OPT["a_cut"][c]:
                named("a%d" % (k // 32 + c + 1))
                act(A("a", 16 * k, 16 * (k + width)), IND(XC, A("AL", k, k + width)), AF.Copy)
                k += width

        def cross(y0, y1):
            n_ = y1 - y0
            lb = A(bank("bl"), 0, 16 * n_)
            for y in range(y0, y1):
                pb = bank("cr")
                for j in (2 * y, 2 * y + 1):
                    for l0, l1 in ([(0, 32), (32, 64)] if j in OPT["halves"] else [(0, 64)]):
                        named("m%d%s" % (j, "b" if l0 else ""))
                        tt(A("m", 1024 * j + 16 * l0, 1024 * j + 16 * l1), IND(XC, A("OP", 64 * j + l0, 64 * j + l1)),
                           A("XP", 16 * l0, 16 * l1), mn)
                    named("cr%d" % j, j > 2 * y)
                    for i in range(8):
                        mm(A(pb, 8 * (j & 1) + 7 - i, 128, 16), A("m", 1024 * j + i, 1024 * j + 1024, 8), OBb)
                w0, w1 = 128 * y, 128 * y + 128
                named("al%d" % y)
                under(A("al", w0, w1), A(pb, 0, 128), 16 * up + 79.5)
                named("sc%d" % y)
                scan(A("sc", w0, w1), A("al", w0, w1), A(df, w0, w1), mul, add_)
                named("Zs%d" % y)
                ts(ND("Zs", y, slice(7, 64, 8)), A("sc", w0 + 7, w1, 8), 0.0, mx, V - 1.0, mn)
                named("bl%d" % y)
                for x in range(8 // n_):
                    mm(lb, ND("Zs", y, slice(7 - n_ * x - y + y0, 71 - n_ * x - y + y0)),
                       A("IWh", 32 + x, 160, 8 // n_), y == y0 and x == 0, False)
            moved("BL%d" % y0, A("BL", 16 * y0, 16 * y1), lb)
            named("b%d" % y0)
            act(A("b", 256 * y0, 256 * y1), IND(XC, A("BL", 16 * y0, 16 * y1)), AF.Copy)

        def penalties(y, zb, o):
            w0, w1, tb = 128 * y, 128 * y + 128, bank("pt")
            act(A("P", w0, w1), A(zb, o, o + 128), AF.Sigmoid, -256 * 24.5)
            mms(A(tb, 0, 128), [(A("al", w0, w1), ID), (A("P", w0, w1), A("IDa"))])
            lin(A("penT", w0, w1), A(tb, 0, 128), 1.0, 128.0)

        def misfits(y):
            zb, o = bank("z"), 1792 * y
            named("z%d" % y)
            mm(A(zb, 0, 128), A("I8M"), A("al", 128 * y, 128 * y + 128), True, False)
            for i0, i1 in OPT["runs"]:
                for j0 in range(2):
                    pb, n_, nm = bank("ab"), 128 * (i1 - i0), "%d%d" % (2 * y + j0, i0)
                    named("da" + nm)
                    mm(A(pb, 0, n_), ID, A("a", 2 * y + j0 + 512 * (i0 - 1), 512 * (i1 - 1), 4), True, False)
                    named("db" + nm)
                    for k in range(i1 - i0):
                        mm(A(pb, 128 * k, 128 * k + 128), NID, A("b", 256 * y + j0, 256 * y + 256, 2), False, False)
                    named("ad" + nm)
                    act(A("ad", o, o + n_), A(pb, 0, n_), AF.Abs)
                    named("z" + nm, True)
                    for k in range(i1 - i0):
                        mm(A(zb, 8 * j0 + 7 - i0 - k, 128, 16), A("ad", o + 128 * k, o + 128 * k + 128), A("OB256"),
                           False, False)
                    o += n_
            penalties(y, zb, 0)

        def misfits4():
            zb, B = bank("z"), A("b", 512, 1024)
            named("z4")
            mm(A(zb, 0, 256), A("I8M"), A("al", 256, 512), True, False)
            for i in range(1, 8):
                o, nm, terms = 3584 + 512 * (i - 1), "q%d" % i, [("ad", "OB256")]
                if i in OPT["fused"]:
                    named("a" + nm)
                    tt(A("a", o, o + 512), IND(XC, A("AL", 192 + 32 * i, 224 + 32 * i)), B, sub_)
                    named("ad" + nm)
                    ts(A("ad", o, o + 512), A("a", o, o + 512), 0.0, mx)
                    terms = [("a", "OBn"), ("ad", "OB512")]
                else:
                    pb = bank("ab")
                    named("da" + nm)
                    mm(A(pb), ID, A("a", o, o + 512), True, False)
                    named("db" + nm)
                    mm(A(pb), NID, B, False, True)
                    named("ad" + nm)
                    act(A("ad", o, o + 512), A(pb), AF.Abs)
                for name, rhs in terms:
                    named("z" + name + nm, True)
                    for jj in range(4):
                        oo = 128 * (jj >> 1)
                        mm(A(zb, oo + 8 * (jj & 1) + 7 - i, oo + 128, 16), A(name, o + jj, o + 512, 4),
                           A(rhs), False, False)
            for yy in range(2):
                penalties(2 + yy, zb, 128 * yy)

        def greatest(y):
            for j0 in range(2):
                for hf in range(2):
                    pb = bank("mx")
                    pT = A("penT", 128 * y + 64 * hf, 128 * y + 64 * hf + 64)
                    for i in range(8):
                        x = 8 * j0 + 7 - i
                        mm(A(pb, i, 512, 8), A("BD", 128 * x, 128 * x + 128) if i else A("N64"), pT, once=i == 0)
                    o = 2048 * y + 1024 * j0 + 512 * hf
                    src = A(pb)
                    if (o // 512) in OPT["via_act"]:
                        src = A("z", 512 * (nscan[0] % 3), 512 * (nscan[0] % 3) + 512)
                        nscan[0] += 1
                        named("z%d" % (o // 512 + 1))
                        act(src, A(pb), AF.Copy)
                    scan(A("s", o, o + 512), src, A("m", o, o + 512), add_, mx)

        def pi(c):
            pb = bank("pi")
            for j in range(4 * c, 4 * c + 4):
                y, x = j >> 1, 7 + 8 * (j & 1)
                named(None, j & 3 > 0)
                mms(A(pb, j & 3, 512, 4), [(A("BD", 128 * x, 128 * x + 128), A("penT", 128 * y, 128 * y + 128)),
                                           (ID, A("s", 1024 * j + 7, 1024 * j + 1024, 8))])
            lin(A("W", 1024 + 512 * c, 1536 + 512 * c), A(pb), 1.0, -up)

        def hashes(c):
            q0, q1, hb, pairs = 32 * c, 32 * c + 32, A(bank("ha"), 0, 32), []
            for y in (2 * c, 2 * c + 1):
                pairs += [(A("WP", 14 - 4 * l2 - 2 * (y & 1), 142 - 4 * l2 - 2 * (y & 1)),
                           A("penT", 128 * y + l2, 128 * y + 128, 4)) for l2 in range(4)]
                for j in (2 * y, 2 * y + 1):
                    pairs += [(A("WW", 15 - 4 * l2 - (j & 3), 143 - 4 * l2 - (j & 3)),
                               A("s", 1024 * j + 8 * l2 + 7, 1024 * j + 1024, 32)) for l2 in range(4)]
            for k, (lhsT, rhs) in enumerate(pairs):
                if k in (8, 12, 20):
                    named(None, True)
                mm(hb, lhsT, rhs, k == 0, False)
            moved("ui%d" % c, A("ui", q0, q1), hb, A("wsf", 1, 2) if t else A("wsf", 4, 5))
            ts(A("u", q0, q1), A("ui", q0, q1), 4095, band)
            ts(A("u32", q0, q1), A("u", q0, q1), 32.0, add_)
            tt(A("uw", q0, q1), A("u", q0, q1), A("u32", q0, q1), mul)
            ts(A("h", q0, q1), A("uw", q0, q1), 5, shr, 4095, band)
            cp(A("HL", q0, q1), A("h", q0, q1))
            moved("hq%d" % c, A("hq", q0, q1), A("h", q0, q1), -2048.0)

        def known(c):
            q0, q1, o0, o1 = 32 * c, 32 * c + 32, 512 * c, 512 * c + 512
            PI = A("W", 1024 + o0, 1024 + o1)
            if c == 0:
                named("d20")
                tt(A("d2", 0, 512), IND(XWIN, A("HL", 0, 32)), PI, sub_)
                named("ad20")
                act(A("ad2"), A("d2", 0, 512), AF.Abs)
            else:
                for hf in range(2):
                    o, src = 512 + 256 * hf, IND(XWIN, A("HL", 32 + 16 * hf, 48 + 16 * hf))
                    named("d21" + "b" * hf)
                    tt(A("d2", o, o + 256), src, A("W", 1024 + o, 1280 + o), mn)
                    named("xh1" + "b" * hf)
                    act(A("xh", o, o + 256), src, AF.Copy)
            lin(A("rec", o0, o1), IND(A(XR), A("HL", q0, q1)), 1.0, 0.0 if t else 128.0)
            pb = A(bank("me"))
            named("mp%d" % c)
            mm(pb, ID, PI, True, False)
            named("mr%d" % c)
            mm(pb, ID, A("rec", o0, o1), False, True)
            lin(A("W", 2048 + o0, 2048 + o1), pb, 0.5, -0.25)

        subs(0)
        cross(0, 1)
        cross(1, 2)
        misfits(0)
        misfits(1)
        subs(1)
        cross(2, 4)
        greatest(0)
        greatest(1)
        misfits4()
        pi(0)
        hashes(0)
        known(0)
        greatest(2)
        greatest(3)
        pens = [(A("penT", 128 * y, 128 * y + 128), A("BLK", 0, 128, 2)) for y in range(4)]
        pb = A(bank("yn"), 0, 64)
        mms(pb, pens)
        lin(A("yn"), pb, 1.0 / 64, 64.4375)
        pb = A(bank("st"), 0, 64)
        mms(pb, pens + [(A("N64"), A("yn"))])
        act(ND("st", slice(None), slice(0, 8)), pb, AF.Sigmoid, A("thr"), 256.0, acc=None if last else A("acc"))
        pb = bank("ld")
        mm(A(pb, 0, 8), A("vr"), OBb, True, False)
        mm(A(pb, 0, 8), A("N2K"), ND("st", slice(None), 0), False, False)
        for g_ in range(8):
            mm(A(pb, g_, g_ + 1), A("EQm", 128 * g_, 128 * g_ + 128), ND("st", g_, slice(0, 1)), False, g_ == 7)
        act(A("Zl", 15, 143, 16), A(pb, 0, 8), AF.Relu, col("d2k"), -1.0)
        pb = A(bank("sf"), 0, 128)
        mms(pb, [(A("FW", 6 - 2 * y, 134 - 2 * y), A("penT", 128 * y, 128 * y + 128)) for y in range(4)]
            + [(ND("st", slice(None)), A("I2K"))])
        act(A("sf"), pb, AF.Sigmoid, col("sfb"), 256.0)
        pb = A(bank("sl"), 0, 8)
        mms(pb, [(ID, A("DL"))] + lanes("Zl", NID))
        moved("SL", A("SL"), pb)
        if not last:
            pb = A(bank("ac"), 0, 1)
            mm(pb, A("ONE", 0, 128), A("acc"))
            lin(A("yq"), pb, -1.0 / 64, 128 + 1100 - 0.4375)
            lin(A("af"), pb, -32.0, 256 * (4096.0 + 14.5 + 1024 + 8800))
            lin(A("thr"), A("yq"), -2048.0, A("af"))
        pi(1)
        hashes(1)
        known(1)
        pb = bank("ky")
        mm(A(pb, 0, 72), ID32, A("JK"), True, False)
        mm(A(pb, 0, 72), A("I8M"), ND("st", slice(None), slice(0, 9)), False, False)
        mm(A(pb, 8, 72, 9), A("N1h"), A("IWh", 40 + t, 160, 16), False, False)
        for j in range(8):
            o = 1024 + 512 * (j >> 2)
            if j == 4:
                cut()
            mm(A(pb, j, 72, 9), A("W", o + (j & 3), o + 512, 4), A("OBk"), False, False)
            mm(A(pb, j, 72, 9), ID, ND("Zs", j >> 1, slice(7, 64, 8), j & 1), False, j == 7)
        scan(A("k4"), A("RS"), A(pb, 0, 72), mul, mx)
        ts(A("kr"), A("k4", 8, 72, 9), BIG, add_, BIG, sub_)
        tt(A("Zv", 15, 143, 16), A("k4", 8, 72, 9), A("kr"), sub_)
        pb = A(bank("vl"), 0, 8)
        mms(pb, lanes("Zv", ID))
        moved("VL", A("yvf" if last else "VL"), pb)
        if not last:
            pb = A(bank("vr"), 0, 128)
            mm(pb, A("Zv", 15, 143), ID)
            moved("vr", A("vr"), pb)
        pb = bank("nm")
        mm(A(pb, 0, 128), NID, A("N1h"), True, False)
        for y in range(4):
            mm(A(pb, 0, 128), ND("Zs", y, slice(3 - y, 67 - y)), ID, False, False)
        for c in range(2):
            for l2 in range(4):
                mm(A(pb, l2, 128, 4), SH[c][l2], A("hq", 32 * c, 32 * c + 32), False, c == 1 and l2 == 3)
            cut()
        tt(A("e2"), A(pb, 0, 128), A("sf"), mul)
        q = t % 4
        nb = A(bank("n2"), 0, 128)
        mms(nb, [(ID, A("N1h")), (NID, A("NMh", 128 * q, 128 * q + 128)), (ID32, A("e2"))])
        pb = bank("ak")
        mm(A(pb, 0, 128), A("I2K"), A("sf"), True, False)
        terms = [("ad2", 0, 0, "OBW", 0, 128), ("W", 1, 1536, "OBW", 0, 128)]
        terms += [(name, 1, 512, win, 64 * hf, 64 * hf + 64) for name, win in (("xh", "OBW"), ("d2", "OBW2"))
                  for hf in range(2)]
        for name, c, at, win, l0, l1 in terms:
            named("k%s%d%s" % (name, c, "b" if l0 else ""), True)
            for jj in range(4):
                mm(A(pb, l0, l1), A(win, 15 - 4 * c - jj, 143 - 4 * c - jj), A(name, at + 4 * l0 + jj, at + 4 * l1, 4),
                   False, False)
        under(A("nask"), A(pb, 0, 128), 2048.0 + 24.5)
        tt(A("t2"), nb, A("nask"), mul)
        tt(IND(A("E"), A("SL")), A("t2"), A("NN", 128 * q, 128 * q + 128), sub_)
        scan(A("incl", 1, 129), A("ONES"), A("nask"), mul, add_)
        pb = A(bank("u1"), 0, 64)
        mms(pb, [(M3[l0], A("nask", l0, 128, 2)) for l0 in range(2)])
        tt(A("u1"), pb, A("C1n"), mul)
        pb = A(bank("tq"), 0, 64)
        mm(pb, ID, A("nL"), True, False)
        for name, win in (("nask", "M2W"), ("incl", "M1W")):
            for l0 in range(2):
                mm(pb, A(win, 8 - 8 * l0, 136 - 8 * l0), A(name, l0, 128, 2), False, False)
            cut()
        under(A("tq"), pb, 255.5)
        pb = A(bank("cl"), 0, 64)
        mm(pb, ID, A("PL"), True, False)
        mm(pb, ID, A("u1"), False, False)
        cut()
        mm(pb, A("I1K"), A("tq"), False, True)
        moved("CL", A("CL"), pb)
        if not last:
            lin(A("X", blk, blk + 1024), IND(A("W"), A("CL")), 1.0)
        else:
            lin(A("X0", 0, 512), IND(A("W"), A("CL", 0, 32)), 1.0, -128.0)
            ts(A("X0", 512, 1024), IND(A("W"), A("CL", 32, 64)), -128.0, add_)
    dma("sp", HB("ye", 0, 960), A("E", 0, 960), 1000000)
    dma("sp", HB("ye", 960, V), A("E", 960, V), 1000000)
    dma("sp", HB("yv"), A("yvf"), 4096)
    dma("sp", HB("yx", 0, 1024), A("X0", 0, 1024), 262144)
    return ops


ASYNC = ("dma", "send", "send2", "arrive")


def dependencies(flat):
    ops, seen, user = [], {}, {}
    for o in flat:
        if ops and ops[-1]["piece"] == o["piece"]:
            p = ops[-1]
            p["calls"].append(o)
            p["ns"] += o["ns"]
            p["hold"] += o["hold"]
        else:
            p = dict(o, calls=[o], hard=set(), soft=set(), opens=None, closes=None)
            ops.append(p)
        k = len(ops) - 1
        reads = [s for x in o["ins"] for s in _spans(x)]
        writes = _spans(o["acc"])
        whole = True
        if o["out"] is not None:
            if o["out"][0] == "ind":
                writes, reads = writes + _spans(o["out"][1]), reads + _spans(o["out"][2])
            else:
                writes = writes + _spans(o["out"])
                whole = o["out"][0] == "ap" and o["out"][4] == 1
        for isw, group in ((False, reads), (True, writes)):
            for name, lo, hi in group:
                psum = SPEC[name][0] == "psum"
                if psum:
                    if name not in user:
                        p["opens"] = name
                    user[name] = k
                keep = []
                for rec in seen.get(name, []):
                    k2, w2, lo2, hi2 = rec
                    if k2 == k:
                        keep.append(rec)
                        continue
                    same = ops[k2]["eng"] == o["eng"] and o["kind"] not in ASYNC and ops[k2]["kind"] not in ASYNC
                    if psum:
                        if not (p["any"] and ops[k2]["any"]):
                            p["soft" if same else "hard"].add(k2)
                        if p["any"]:
                            keep.append(rec)
                        continue
                    if lo < hi2 and lo2 < hi and (isw or w2):
                        p["hard"].add(k2)
                        if isw and lo <= lo2 and hi2 <= hi and (whole or not same):
                            continue
                    keep.append(rec)
                if (k, isw, lo, hi) not in keep:
                    keep.append((k, isw, lo, hi))
                seen[name] = keep
    for name, k in user.items():
        ops[k]["closes"] = name
    send = {o["par"]: k for k, o in enumerate(ops) if o["kind"] in ("send", "send2")}
    count = {}
    for o in ops:
        o["soft"] -= o["hard"]
        o["time"] = set([send[o["par"]]]) if o["kind"] == "arrive" else set()
        out = o["out"]
        key = o["eng"][0] + (out[1].split(".")[0] if out[0] != "ind" else out[1][1] + "!") if out and o["eng"] else "-"
        key = "g" + key[1:] if o["eng"] == "pool" else "aX" if key == "aX0" else key
        if o["kind"] == "send":
            count.clear()
            first = send[o["par"]]
        if o["kind"] == "send2":
            o["soft"].add(first)
        if o["tag"]:
            o["key"] = key[0] + o["tag"]
            continue
        count[key] = count.get(key, 0) + 1
        o["key"] = "%s#%d" % (key, count[key])
    return ops


ROUND = """
dN1h#1 pvr#1' ptq#1' ptq#2' pmp1' atq#1' pmr1' pu1#1' plp#1 du1#1' avr' dLP dN2h#1 dN2h#2 dTh#1 aW#4' pcl#1' pcl#2'
aCL' aX#1' pac#1' peq#1 dTh#2 aXP#1 aXP#2 pal#1 pop#1 dEQ#1 pal#2 pal#3 pal#4 aAL0 aa5 dOPa pop#2 dm0 aa7 pop#3 dOP0
dm0b dm1 dm2b pdf#1 pal#5 pal#6 pal#7 pal#8 aAL1 pcr0 pcr1 dal0 pda15 dm2 pcr2 aa1 dsc0 pda05 pz0 dOP1 aa3 dZs0 ayq#1'
pbl0 aBL0 aaf#1' dm3 pda01 dm4 pcr3 dal1 ab0 aa11 pdb01 pdb15 aad01 pdb05 aad05 pda11 pda31 dsc1 dZs1 pbl1 aBL1 dm4b
dm5 dm6 pda35 pdb11 pda25 pz01 pz05 aad15 ab1 pcr4 dm7 aad11 pda21 pdb35 aad35 pdb21 pdb25 pz15 pdaq3 aad25 pz11 aP#1
pdb31 pz1 aad21 pdaq4 ppt#1 apenT#1 pz25 aad31 pcr5 dal2 pz21 pmx#1 ds#1 pcr6 pcr7 dal3 dsc2 pz35 pmx#2 dsc3 dZs2 aa9
pz31 dZs3 pmx#4 pmx#3 pbl2 pbl3 aP#2 ppt#2 ds#2 pdaq1 aBL2 apenT#2 pha#1 ds#3 ds#4 pdaq2 pmx#5 ab2 pmx#7 pdbq3 pdbq4
pdbq1 aa13 ds#5 aadq3 pmx#8 aadq4 peq#2 aadq1 daq6 dadq6 pdaq5 pdbq5 aadq5 pdbq2 aadq2 pz4 pzadq6 pzadq1 daq7 ds#7
pzadq3 pmx#6 dadq7 pzaq7 pzaq6 pzadq4 pzadq5 pzadq7 pzadq2 aP#3 ppi#1 ds#6 pha#2 ds#8 athr#1' dEQ#2 aP#4 pha#3 ppt#3
ppi#2 pha#4 ppi#3 apenT#3 dui0 du#1 du32#1 ppt#4 pmx#10 duw#1 apenT#4 pmx#9 az10 pmx#12 pyn#1 ayn#1 pmx#11 ds#9 dh#1
pmx#16 pst#1 ds#10 az12 pmx#14 pmx#13 ast#1 pmx#15 ds#11 az16 pld#1 psf#1 ppi#4 ds#12 ppi#5 ds#13 dHL#1 pha#5 az14
pha#6 aZl#1 ppi#6 psl#1 ds#16 asf#1 ds#14 pha#7 aW#1 ds#15 pha#8 ppi#7 dd20 ppi#8 arec#1 aui1 pmp0 du#2 du32#2 duw#2
dh#2 dHL#2 dhq1 pky#1 pmr0 pak#1 ahq0 aW#3 pkW1 pnm#1 pnm#2 pky#2 aad20 dd21 axh1b axh1 pkad20 pkxh1b pkd21 dd21b
de2#1 dk4#1 dkr#1 dSL dZv#1 pkd21b arec#2 pkxh1 pn2#1 dnask#1 dt2#1 dincl#1 aW#2 pvl#1 dE!#1 dVL
"""
LAST = ("pn2#1 pmp1 dnask#1 dt2#1 dincl#1 pu1#1 ptq#1 aW#2 pmr1 ptq#2 dE!#1 du1#1 atq#1 pcl#1 aW#4 pcl#2 aCL aX#1 "
        "pvl#1 dX0#1 dVL").split()
FIRST = "IC IW r rg rgw ONES PM PM#2 sc PM#3 PM#4 SelS rj".split()
LOOK = 120.0


def serial(ops, text):
    n = len(ops)
    edge = [k for k, o in enumerate(ops) if o["kind"] == "send"] + [n]
    names = text.split()
    place = {w.rstrip("'"): i + len(names) * w.count("'") for i, w in enumerate(names)}
    key, listed = [0.0] * n, set()
    for k, o in enumerate(ops):
        t = sum(1 for e in edge if e <= k) - 1
        if t == RO - 1 and o["key"] in LAST:
            listed.add(k)
            key[k] = len(names) * t + place[LAST[0]] + LAST.index(o["key"]) / 100
        elif t >= 0 and o["key"] in place:
            listed.add(k)
            key[k] = len(names) * t + place[o["key"]]
        else:
            key[k] = -1.0
        for d in o["hard"] | o["soft"] | o["time"]:
            key[k] = max(key[k], key[d] + 1e-4)
    return sorted(range(n), key=lambda k: (key[k], k)), listed


def allot(ops, seq):
    free, held, lastuse, final = list(BANKS), {}, {}, {}
    for k in seq:
        if ops[k]["eng"] == "pe":
            final[ops[k]["out"][1]] = ops[k]["calls"][-1]
    for c in final.values():
        c["par"] = (c["par"][0], True)
    for k in seq:
        o = ops[k]
        if o["opens"]:
            b = free.pop(0)
            held[o["opens"]] = b
            SPEC[o["opens"]] = SPEC[o["opens"]][:3] + (b, 0)
            if b in lastuse:
                d, name = lastuse[b]
                o["soft" if ops[d]["eng"] == o["eng"] else "hard"].add(d)
                if name.split(".")[0] == o["opens"].split(".")[0]:
                    o["calls"] = [c for c in o["calls"] if not c["once"]]
        if o["closes"]:
            free.append(held[o["closes"]])
            lastuse[held[o["closes"]]] = (k, o["closes"])


def arrange(ops, seq, listed):
    n = len(ops)
    after = [[] for _ in ops]
    left = [0] * n
    for k, o in enumerate(ops):
        for d in o["hard"] | o["soft"] | o["time"]:
            p = ops[d]
            lag = 0.0 if p["eng"] is None else LAG[1] if p["eng"] == o["eng"] else LAG[0]
            after[d].append((k, p["hold"] if d in o["soft"] else p["ns"] + lag))
            left[k] += 1
    fixed = {e: [k for k in seq if k in listed and ops[k]["eng"] == e] for e in ENG}
    due, free = [0.0] * n, {e: 0.0 for e in ENG}
    for k in seq:
        if k in listed:
            due[k] = max(due[k], free[ops[k]["eng"]])
            free[ops[k]["eng"]] = due[k] + ops[k]["hold"]
        for x, w in after[k]:
            due[x] = max(due[x], due[k] + w)
    end = max(due) + 5000.0
    for k in reversed(seq):
        if k not in listed:
            due[k] = min([due[x] - w for x, w in after[k]] + [end])
    turn = [due[k] + ops[k]["ns"] * (-1 if ops[k]["eng"] == "sp" and k > 6 else 1) for k in range(n)]
    for k in range(n):
        if ops[k]["eng"] == "pool":
            name = ops[k]["key"][1:].replace("#1", "")
            turn[k] = FIRST.index(name) - 99.0 if name in FIRST else due[k] / 100 if ops[k]["kind"] == "send" else due[k]
    ready, start = [max(0.0, due[k] - 60000.0) if ops[k]["kind"] == "iota" else 0.0 for k in range(n)], [0.0] * n
    free, head = {e: 0.0 for e in ENG}, {e: 0 for e in ENG}
    pool, order = {e: [] for e in ENG}, {e: [] for e in ENG}

    def release(k):
        for x, w in after[k]:
            ready[x] = max(ready[x], start[k] + w)
            left[x] -= 1
            if left[x] == 0 and ops[x]["eng"] is None:
                start[x] = ready[x]
                release(x)
            elif left[x] == 0 and x not in listed:
                pool[ops[x]["eng"]].append(x)
    for k in range(n):
        if left[k] == 0 and k not in listed:
            pool[ops[k]["eng"]].append(k)
    while True:
        best = None
        for e in ENG:
            h = fixed[e][head[e]] if head[e] < len(fixed[e]) else None
            pick = h if h is not None and left[h] == 0 else None
            if pool[e]:
                soon = max(free[e], min(ready[x] for x in pool[e])) + LOOK
                d = min((x for x in pool[e] if ready[x] <= soon), key=lambda x: (turn[x], x))
                fits = pick is not None and max(free[e], ready[d]) + ops[d]["hold"] <= max(free[e], ready[h]) + 60
                if pick is None or due[d] < due[h] or fits:
                    pick = d
            if pick is not None and (best is None or max(free[e], ready[pick]) < best[0]):
                best = (max(free[e], ready[pick]), e, pick)
        if best is None:
            break
        time, e, k = best
        if k in listed:
            head[e] += 1
        else:
            pool[e].remove(k)
        start[k], free[e] = time, time + ops[k]["hold"]
        order[e].append(k)
        release(k)
    assert sum(len(x) for x in order.values()) == sum(1 for o in ops if o["eng"])
    return order, start


def plan(text=None):
    ops = dependencies(program())
    seq, listed = serial(ops, text or ROUND)
    allot(ops, seq)
    order, start = arrange(ops, seq, listed)
    pos = {}
    for e in ENG:
        for i, k in enumerate(order[e]):
            pos[k] = i
    seq = sorted((k for e in ENG for k in order[e]), key=lambda k: (start[k], pos[k]))
    know = {e: {} for e in ENG}
    done = {}
    for k in seq:
        o = ops[k]
        kn = know[o["eng"]]
        waits = []
        for d in sorted(o["hard"], key=lambda d: -start[d]):
            od = ops[d]
            if od["kind"] in ASYNC:
                if ("x", d) not in kn:
                    waits.append(d)
                    kn[("x", d)] = 1
                    for key, val in done.get(d, {}).items():
                        kn[key] = max(kn.get(key, -1), val)
            elif kn.get(od["eng"], -1) < pos[d]:
                waits.append(d)
                kn[od["eng"]] = pos[d]
                for key, val in done[d].items():
                    kn[key] = max(kn.get(key, -1), val)
        o["waits"] = waits
        done[k] = dict(kn)
    needed = set(d for o in ops if o["eng"] is not None for d in o["waits"])
    count = {}
    for e in ENG:
        c = 0
        for k in order[e]:
            if k in needed and ops[k]["kind"] not in ASYNC:
                c += 1
                count[k] = c
    return ops, order, count, needed, start


_PLAN = []


def rank_program(g, core, T, topo):
    rank = T.rank_of(core)
    if rank is None:
        return
    if not _PLAN:
        _PLAN.append(plan())
    ops, order, count, needed, _ = _PLAN[0]
    queue = {"pe": g.tensor, "dve": g.vector, "act": g.scalar, "pool": g, "sp": g.sync}
    n = len(T.cores)

    def ap(x):
        if not isinstance(x, tuple):
            return x
        if x[0] == "ind":
            return ap(x[1]).indirect(ap(x[2]))
        if x[0] == "hbm":
            return T[x[1]][:] if x[2] is None else T[x[1]][:, x[2]:x[3]]
        if x[0] == "nd":
            return T[x[1]][(slice(None),) + x[2]]
        buf, at = SPEC[x[1]][3:]
        if x[4] == 1:
            return T[buf][:, at + x[2]:at + x[3]]
        return T[buf][:, at + x[2]:at + x[3]:x[4]]

    def sem_of(d):
        o = ops[d]
        if o["kind"] == "dma":
            return T.sem[o["par"][0]], 16
        if o["kind"] in ("send", "send2"):
            dst = T.cores[(rank - 1 - o["par"][0] % (n - 1)) % n]
            return T.sem["snt%d" % o["par"][1]], len(topo.engines(core, dst))
        if o["kind"] == "arrive":
            src = T.cores[(rank + 1 + o["par"][0] % (n - 1)) % n]
            return T.sem["arr%d" % o["par"][1]], len(topo.engines(src, core))
        return T.sem["c_" + o["eng"]], count[d]

    def call(q, o):
        kind, par = o["kind"], o["par"]
        out = ap(o["out"]) if o["out"] is not None else None
        ins = [ap(x) for x in o["ins"]]
        if kind in ("send", "send2"):
            dst = T.cores[(rank - 1 - par[0] % (n - 1)) % n]
            rid, pid, _ = topo.addr(dst)
            return g.remote_dma(T["XR%d" % par[0]][:, o["ins"][0][2]:o["ins"][0][3]], ins[0], T.sem["arr%d" % par[1]],
                                T.sem["snt%d" % par[1]], pid, rid, topo.mask(core, dst))
        if kind == "dma":
            if par[1]:
                return q.dma_start(out, ins[0], accum_op=OP_.add, max_dma_last_dim=4096).then_inc(T.sem[par[0]], 16)
            return q.dma_start(out, ins[0]).then_inc(T.sem[par[0]], 16)
        if kind == "mm":
            return q.matmul(out, ins[0], ins[1], par[0], par[1])
        if kind == "copy":
            return q.tensor_copy(out, ins[0])
        if kind == "ts":
            if par[1] is None:
                return q.tensor_scalar(out, ins[0], ins[1], None, par[0])
            return q.tensor_scalar(out, ins[0], ins[1], ins[2], par[0], par[1])
        if kind == "tt":
            return q.tensor_tensor(out, ins[0], ins[1], par)
        if kind == "scan":
            return q.tensor_tensor_scan(out, ins[0], ins[1], 0.0, par[0], par[1])
        if kind == "memset":
            return q.memset(out, par)
        if kind == "tr":
            return q.transpose(out, ins[0])
        if kind == "act":
            if o["acc"] is not None:
                return q.activation(out, ins[0], par, ins[1], ins[2], accum_out=ap(o["acc"]))
            return q.activation(out, ins[0], par, ins[1], ins[2])
        if kind == "iota":
            if SPEC[o["out"][1]][2] == "int32":
                return g.iota(out, par[0], par[1], par[2])
            return g.iota(out, par[0], par[1], par[2], allow_small_or_imprecise_dtypes=True)
        return g.affine_select(out, ins[0], par[0], par[1], 0.0, par[2], par[3])

    for e in ENG:
        q = queue[e]
        for k in order[e]:
            for d in ops[k]["waits"]:
                s, val = sem_of(d)
                q.wait_ge(s, val)
            for o in ops[k]["calls"]:
                r = call(q, o)
            if k in count:
                r.then_inc(T.sem["c_" + e], 1)
    for k, o in enumerate(ops):
        if o["kind"] in ASYNC and k not in needed:
            s, val = sem_of(k)
            g.sync.wait_ge(s, val)
